import numpy as np, ml_dtypes
CORES = [9,25,41,57]
N = 4
BF = ml_dtypes.bfloat16
S, V, KW, L, ST = 4096, 1024, 1024, 256, 6
def parts(rng):
    lev = rng.integers(0, 256, (N, 8, 1, S)); x = np.clip(lev + rng.integers(-48, 49, (N, 8, 16, S)), 0, 255)
    order = np.argsort(lev[:, :, 0], axis=-1); w = S // 8
    pos = rng.integers(0, S - w + 1, (N, 8, 1, 2 * V)) + rng.integers(0, w, (N, 8, 16, 2 * V))
    near = np.take_along_axis(order, pos.reshape(N, 8, -1), 2).reshape(pos.shape)
    b = np.where(rng.random((N, 8, 1, 2 * V)) < 0.6, near, rng.integers(0, S, (N, 8, 16, 2 * V)))
    k = rng.integers(0, S, (N, 8, 16, KW))
    return x, b, k, rng.integers(0, S, (N, 8, L)), rng.integers(0, V, (N, 8, L)), rng.integers(0, 2, (N, 8, L))
def pack(x, b, k, c, v, d):
    return {"x": np.ascontiguousarray(x.reshape(N, 128, S)).astype(np.float32).astype(BF), "bnd": np.ascontiguousarray(b.reshape(N, 128, 2 * V)).astype(np.int32),
            "kt": np.ascontiguousarray(k.reshape(N, 128, KW)).astype(np.int32), "lc": c.astype(np.int32), "lv": v.astype(np.int32), "ld": d.astype(np.int32)}
def setup_inputs(rng):
    return pack(*parts(rng))
def setup_inputs_spread(rng):
    x, b, k, c, v, d = parts(rng)
    x = np.minimum((np.exp2(8.2 * rng.random((N, 8, 1, S))) * rng.random((N, 8, 16, S))).astype(np.int64), 255)
    def low(n, shape): return np.minimum((n * rng.random(shape) ** 3).astype(np.int64), n - 1)
    b = np.where(rng.random(b.shape) < 0.5, low(S, b.shape), b); k = np.where(rng.random(k.shape) < 0.5, low(S, k.shape), k)
    return pack(x, b, k, low(S, c.shape), low(V, v.shape), (rng.random(d.shape) < rng.random((N, 8, 1))).astype(np.int64))
def setup_inputs_ends(rng):
    def ends(hi, shape):
        u = rng.random(shape)
        return np.where(u < 0.37, 0, np.where(u < 0.75, hi, rng.integers(0, hi + 1, shape)))
    kind = rng.integers(0, 3, (N, 8, 1, S)); kind[..., 1:S - 1:2] = 2
    kind[..., S - 1] = 1; kind[:, 1, :, S - 1] = 0; kind[..., S - 2] = 0; kind[..., 0] = 0; kind[:, 3, :, 0] = 1; kind[:, 7, :, 0] = 1
    x = np.where(kind == 2, 255 * rng.integers(0, 2, (N, 8, 16, S)), 255 * kind)
    b = ends(S - 1, (N, 8, 16, 2 * V)); k = ends(S - 1, (N, 8, 16, KW)); c = ends(S - 1, (N, 8, L)); v = ends(V - 1, (N, 8, L)); d = rng.integers(0, 2, (N, 8, L))
    b[..., 0] = 0; b[..., 1] = 0; b[..., 2 * V - 2] = S - 2
    b[:, :, :15, 2 * V - 1] = 1 + 2 * rng.integers(0, S // 2 - 1, (N, 8, 15)); b[:, :, 15, 2 * V - 1] = S - 1
    for i, w, s in ((0, 0, 1), (1, 0, 0), (L - 2, V - 1, 1), (L - 1, V - 1, 0)):
        c[..., i] = S - 1; v[..., i] = w; d[..., i] = s
    b[..., 10] = S - 1; b[:, :, 15, 10] = S - 2; c[..., 2] = S - 2; v[..., 2] = 5; d[..., 2] = 1
    return pack(x, b, k, c, v, d)
def setup_inputs_corners(rng):
    base = rng.choice(np.array([1, 4, 100, 128, 254]), (N, 8, 1, 1)); sh = np.arange(S); h = S // 4
    m = 8 + (sh // 2) % 3; sgn = np.where(sh % 2 == 0, 1, -1)
    rk = np.argsort(rng.random((N, 8, 16, S)), axis=2)
    x = base + np.where(sh < h, 0, sgn * np.where(rk < m, rng.integers(0, 2, rk.shape), -1))
    kind = rng.integers(0, 5, (N, 8, 1, 2 * V)); at = rng.choice(np.array([0, 7, 15]), kind.shape); hit = np.arange(16)[:, None] == at
    mm = np.where(kind == 4, rng.integers(8, 11, (N, 8, 16, 2 * V)), np.where(kind == 1, 9, np.where((kind == 2) & hit, 10, np.where((kind == 3) & hit, 9, 8))))
    b = 6 * rng.integers((h + 5) // 6, (S - 6) // 6 + 1, mm.shape) + 2 * (mm - 8) + (1 - np.arange(2 * V) % 2)
    few = np.array([0, h - 1, h // 2, S - 1])
    k = np.where(rng.random((N, 8, 16, KW)) < 0.7, rng.integers(0, h, (N, 8, 16, KW)), rng.choice(few, (N, 8, 16, KW)))
    c = np.where(rng.random((N, 8, L)) < 0.7, rng.integers(0, h, (N, 8, L)), rng.choice(few, (N, 8, L)))
    v = np.where(rng.random((N, 8, L)) < 0.7, rng.integers(0, V, (N, 8, L)), rng.choice(np.array([0, V - 1]), (N, 8, L))); d = rng.integers(0, 2, (N, 8, L))
    for i in range(8):
        v[..., i] = V - 1 - i; d[..., i] = i % 2; w = 2 * (V - 1 - i) + 1 - i % 2
        if i < 4: b[:, :, :, w] = c[:, :, i][:, :, None]
        else: b[:, :, 15, w] = c[:, :, i]
    return pack(x, b, k, c, v, d)
def setup_inputs_crowd(rng):
    x, b, k, c, v, d = parts(rng)
    for q in range(N):
        for g in range(8):
            kind = (g + q) % 8; o = rng.permutation(S); s = int(rng.integers(0, 2)); w = int(rng.choice(np.array([0, V - 1, V // 2, 5])))
            one = int(rng.choice(np.array([0, L // 2, L - 1])))
            if kind < 4:
                top = 255 if s == 0 else 0
                a, z, e = o[:48], o[48:96], o[96:112]
                x[q, g][:, a] = top; x[q, g][:, z] = 255 - top; x[q, g][:, e] = np.clip(x[q, g][:, e], 1, 254)
                b[q, g, :, 2 * w + 1 - s] = e; v[q, g] = w; d[q, g] = s
                u, y = (a, z) if kind < 2 else (z, a)
                c[q, g] = u[0] if (kind + q) % 2 == 0 and q % 4 < 2 else rng.choice(u, L)
                if kind % 2 == 1: c[q, g, one] = y[3]
            elif kind == 4: v[q, g] = rng.choice(np.array([0, V - 1, 7, w]), L); c[q, g] = rng.choice(np.array([0, S - 1, int(o[0]), int(o[1])]), L)
            elif kind == 5: k[q, g] = k[q, g, :, :1]
            elif kind == 6: k[q, g] = rng.choice(np.array([0, S - 1]), (16, KW))
            else: c[q, g] = o[0]; v[q, g] = w; d[q, g] = s
    return pack(x, b, k, c, v, d)
def setup_inputs_limits(rng):
    x, b, k, c, v, d = parts(rng); w = S // 8
    for q in range(N):
        for g in range(8):
            o = rng.permutation(S - w); z = o[:14]; at = np.arange(S); at[z] = o[14:28]
            if g % 2 == 1:
                at[S - w:] = o[28:28 + w]; x[q, g][:, S - w:] = 255 * rng.integers(0, 2, (16, 1)); x[q, g, 15, S - w:] = 255
            b[q, g] = at[b[q, g]]; k[q, g] = at[k[q, g]]; c[q, g] = at[c[q, g]]
            x[q, g][:, z] = np.array([255, 255, 255, 255, 0, 0, 0, 0, 200, 200, 200, 200, 40, 160])
            f = int(rng.integers(0, 16)); x[q, g, f, z[1]] = 254; x[q, g, f, z[5]] = 1; x[q, g, f, z[6]] = 3
            x[q, g, rng.permutation(16)[:8], z[3]] = 254
            r = rng.permutation(V - 1); u = [int(a) for a in r[:9]] + [V - 1]; v[q, g] = r[9 + rng.integers(0, V - 10, L)]
            for n, (i, own, s, rest, row, one) in enumerate(((0, 0, 0, 1, 15, 2), (L - 1, 0, 1, 1, 15, 2), (1, 3, 1, 2, 15, 4), (L - 2, 3, 1, 2, 0, 6), (2, 0, 0, 4, 15, 5), (L - 3, 7, 1, 2, 15, 1))):
                c[q, g, i] = z[own]; v[q, g, i] = u[n]; d[q, g, i] = s
                b[q, g, :, 2 * u[n] + 1 - s] = z[rest]; b[q, g, row, 2 * u[n] + 1 - s] = z[one]
            for n, j in enumerate((16, 32, 64, 128)):
                c[q, g, j - 1] = z[12]; c[q, g, j] = z[13]; v[q, g, j - 1:j + 1] = u[6 + n]; d[q, g, j - 1:j + 1] = 0
                b[q, g, :, 2 * u[6 + n] + 1] = z[8 + n]
    return pack(x, b, k, c, v, d)
def check_inputs(d):
    bad = []
    for k, hi in (("x", 255), ("bnd", S - 1), ("kt", S - 1), ("lc", S - 1), ("lv", V - 1), ("ld", 1)):
        a = np.asarray(d[k]).astype(np.float32)
        if not (np.min(a) >= 0 and np.max(a) <= hi): bad.append("range of " + k)
        elif k == "x" and np.any(np.floor(a) != a): bad.append("whole numbers in x")
    return bad
def first(w):
    return ~np.any((w[..., :, None] == w[..., None, :]) & np.tril(np.ones((L, L), bool), -1), axis=-1)
def append(b, col, val, t):
    n, g, i = np.nonzero(first(col)); b[n, g, (5 * t + i) & 15, col[n, g, i]] = val[n, g, i]
def reference(x, bnd, kt, lc, lv, ld):
    X = x.astype(np.float32).astype(np.int32).reshape(N, 8, 16, S).copy(); B = bnd.astype(np.int32).reshape(N, 8, 16, 2 * V).copy(); K = kt.astype(np.int32).reshape(N, 8, 16, KW)
    c, v, d = lc.astype(np.int64), lv.astype(np.int64), ld.astype(np.int64); A = np.zeros((N, 8), np.int64); miss = []
    for t in range(ST):
        q = np.take_along_axis(X, c[:, :, None, :], 3)
        E = np.take_along_axis(B, (2 * v + 1 - d)[:, :, None, :], 3).astype(np.int64)
        xe = np.take_along_axis(X, E.reshape(N, 8, 1, 16 * L), 3).reshape(N, 8, 16, 16, L)
        qq = q[:, :, :, None, :]
        fits = np.where((d == 0)[:, :, None, None, :], qq <= xe, xe <= qq)
        good = np.add.reduce(fits.astype(np.int32), axis=2) >= (9 + (A & 1))[:, :, None, None]
        M = np.add.reduce(np.minimum(xe, qq), axis=2); D = np.add.reduce(np.abs(xe - qq), axis=2)
        hit = np.any(good, axis=2)
        ks = np.where(hit, np.argmax(np.where(good, M, -1), axis=2), np.argmin(D, axis=2))[:, :, None, :]
        e = np.take_along_axis(E, ks, 2)[:, :, 0]; p = (np.take_along_axis(D, ks, 2)[:, :, 0] & 15).astype(np.int64)
        y = np.take_along_axis(X, e[:, :, None, :], 3)
        place = np.where(hit, e, c); value = np.where(hit[:, :, None, :], np.abs(y - (q >> 2)), (q + y) >> 1)
        n, g, i = np.nonzero(first(place)); X[n, g, :, place[n, g, i]] = value[n, g, :, i]
        append(B, 2 * v + d, c, t)
        kc = np.take_along_axis(K, (c & (KW - 1))[:, :, None, :], 3).astype(np.int64); ke = np.take_along_axis(K, (e & (KW - 1))[:, :, None, :], 3).astype(np.int64)
        pair = []
        for z in (p, p ^ 1):
            pair.append((np.take_along_axis(kc, z[:, :, None, :], 2)[:, :, 0], np.take_along_axis(ke, z[:, :, None, :], 2)[:, :, 0] & (V - 1), d ^ (z & 1)))
        c2, v2, d2 = [np.roll(a, 1 + t % (N - 1), axis=0) for a in pair[1]]
        append(B, 2 * v2 + d2, c2, t)
        c, v, d = pair[0]; A = np.add.reduce((~hit).astype(np.int64), axis=2); miss.append(A)
    ys = np.add.reduce(X.reshape(N, 8, 16, 8, S // 8), axis=4)
    return {"yb": B.reshape(N, 128, 2 * V).astype(np.float32), "yc": c.astype(np.float32), "yv": v.astype(np.float32), "yd": d.astype(np.float32),
            "ys": ys.reshape(N, 128, 8).astype(np.float32), "ym": np.stack(miss, axis=2).astype(np.float32)}

@@ -1,0 +1,581 @@
+from concourse.mybir import AluOpType as ALU, ActivationFunctionType as ACT
+
+ST = 6
+F32, BF, F16, I32, U16 = "float32", "bfloat16", "float16", "int32", "uint16"
+XO = 4160
+BIG = 16384.0
+SEG = (0, 256, 448, 576, 640)
+S_CHUNKS = (0,)
+
+
+def _sb(n, dt):
+    return ("sbuf", [128, n], dt)
+
+
+SCRATCH = {
+    "XT": _sb(2 * XO, BF), "B": _sb(2112, F32), "BI": _sb(2048, I32),
+    "KI": _sb(1024, I32), "KA": _sb(1024, I32), "KF": _sb(1024, F32), "KV": _sb(1024, F32), "LN": _sb(768, I32),
+    "JF": _sb(256, F32), "SI": _sb(256, F32), "SR": _sb(272, F32), "CG": _sb(128, F32), "DI": _sb(128, F32), "TI": _sb(16, F32),
+    "PI": _sb(8, I32), "COL": _sb(24, F32), "LIN": _sb(256, U16), "LAST": _sb(8, U16), "ENDS": _sb(2, U16), "REV": _sb(16, U16),
+    "MS": _sb(256, F32), "ND": _sb(256, BF), "BM": _sb(272, F32), "BNB": _sb(272, BF),
+    "MK": _sb(640, BF), "RSB": _sb(256, F32), "RS0": _sb(128, F32), "TRB": _sb(16, F32), "TRX": _sb(16, F32),
+    "BO": _sb(384, F16), "S8F": _sb(8, F32), "S8H": _sb(8, F16), "W3": _sb(40, BF),
+    "WD": _sb(256, BF), "CQ": _sb(640, BF), "ON": _sb(128, BF), "IV": _sb(512, BF), "IF": _sb(128, F32), "ZH": _sb(144, F16),
+    "EU": _sb(256, U16), "EF": _sb(256, F32), "QC": _sb(256, BF), "QQ": _sb(4096, BF),
+    "SD": _sb(4096, BF), "HD": _sb(4096, BF), "GD": _sb(2048, BF),
+    "P8": _sb(256, F32), "NC": _sb(256, F32), "TA": _sb(256, F32), "KEY": _sb(256, F32), "SC1": _sb(256, F32),
+    "EQ": _sb(256, F32), "RP": _sb(256, F32), "SC2": _sb(256, F32),
+    "YI": _sb(16, I32), "PP": _sb(16, I32), "SM": _sb(32, F32), "SE": _sb(16, I32), "HL": _sb(16, BF), "CL": _sb(16, F32), "T5": _sb(32, F32),
+    "PM": _sb(256, BF), "PM2": _sb(256, BF), "DG": _sb(512, F16), "EI": _sb(32, I32), "EW": _sb(16, U16), "E10": _sb(16, U16),
+    "MM": _sb(1280, F16), "KC": _sb(256, F32), "KE": _sb(256, F32), "DX": _sb(256, BF), "DL": _sb(128, BF), "PA": _sb(16, I32), "PF": _sb(8, F32),
+    "WS": _sb(64, F32), "SW": _sb(256, F32), "C2": _sb(16, F32), "CR": _sb(16, F32), "CO": _sb(32, F32), "CRU": _sb(16, U16), "WX": _sb(32, F32),
+    "CI": _sb(32, I32), "CU": _sb(16, U16), "C10": _sb(16, U16), "CPF": _sb(16, F32), "CPU": _sb(16, U16),
+    "ABX": _sb(640, BF), "AB2": _sb(640, BF), "ABO": _sb(640, BF), "SCX": _sb(640, BF), "SC3": _sb(640, BF), "SCO": _sb(640, BF),
+    "UX": _sb(32, F32), "U2": _sb(16, F32), "UO": _sb(32, F32),
+    "OC": _sb(16, U16), "RC": _sb(16, U16), "OX": _sb(16, U16),
+    "VO": _sb(256, F32), "OLD": _sb(256, F32), "OL2": _sb(256, F32),
+    "HM": _sb(256, BF), "PE_": _sb(256, F32),
+    "QT": _sb(256, BF), "QH": _sb(512, BF), "YT": _sb(256, BF), "AA": _sb(256, BF), "RR": _sb(256, F32), "R2": _sb(256, BF),
+    "VA": _sb(256, BF), "VC": _sb(256, BF), "SND": _sb(16 * ST, F32), "LND": _sb(16 * ST, F32), "SV": _sb(256 * ST, F32), "LV": _sb(256 * ST, F32),
+    "YS": _sb(8, F32), "YM": _sb(8, F32), "YO": _sb(768, F32), "YR": _sb(768, F32),
+}
+for _b in range(8):
+    SCRATCH["P%d" % _b] = ("psum", [128, 512], F32)
+NDMA = 24
+SEMAPHORES = ["qV", "qS", "qT", "qG", "sent"] + ["arr%d" % t for t in range(ST)] + ["arv%d" % t for t in range(ST)] + ["d%d" % i for i in range(NDMA)]
+
+
+SHIFT = {'G.SR.':3,'G.sndy.sndb':-22,'S..YR0!':20,'S..YR1!':25,'S..YR2!':35,'S..YS7!':60,'S.AA.P6:a':10,'S.AB211.SW!':-35,'S.AB24.SW':-20,'S.B.Bt':20,'S.C2n.SW':7,'S.C2n.SW!':-33,'S.DL.LIN':-12,'S.EF.CRU':-5,'S.GD0.C14':65,'S.KI.':5,'S.QQ1_0.QC':43,'S.QQ1_1.QC':35,'S.QQ1_11.QC':20,'S.QQ1_15.QC':15,'S.QQ1_3.QC':27,'S.QQ1_5.QC':30,'S.QQ1_9.QC':21,'S.R2.RR':8,'S.Xc0.Xt0':-37,'S.YM.P3:p':-8,'S.YR1.YO1!':20,'S.YS1.X!':-12,'S.YS3.X!':5,'S.YS5.X!':12,'S.YS7.X!':30,'T.P0:q.IF!':-12,'T.P0:q.W30':-3,'T.P0:q.W34!':-35,'T.P1:q.MD!':1,'T.P1:q.WD1':-20,'T.P5:v.IV0':-45,'T.P5:v.M2':-21,'T.P6:a.IV2':67,'T.P6:a.IV3':60,'T.P6:a.IV3!':20,'V.B.VO!':28,'V.BM.C0':-35,'V.BNB.C0':-8,'V.BO5.C0':-27,'V.C0.PI2':12,'V.C15.PI4':-4,'V.C2_.PI2':12,'V.CO0.WS1':12,'V.CPF.WS2':-2,'V.CR.WS0':-3,'V.CU.CI0':25,'V.DL.':-60,'V.E10.EI1!':-1,'V.EQ0.KEY0':-22,'V.EW.EI0!':8,'V.GD1.':-3,'V.M1.KC!':35,'V.MS.C0':-35,'V.NC0.P80':-60,'V.ND.C0':-70,'V.OC.UO':44,'V.OLD.OC!':10,'V.OX.UX':12,'V.P2:y0.P80':-6,'V.P81.P1:q':-5,'V.PA0.P7:n':-54,'V.PA1.PA0':-20,'V.RP0.P2:y0':-9,'V.SD1.QQ0_15!':-12,'V.SD3.QQ1_15':-8,'V.SM1.CL':20,'V.T50.CL':5,'V.T50.CL!':13,'V.T51.HL':60,'V.T51.HL!':30,'V.TRa.C0':-60,'V.UO.CO1!':60,'V.W31.S8F':60,'V.W34.S8F':-35,'V.Xc.OX':3,'V.Xt.':-20,'V.snda.C2n!':8,'Y.X0.':-20}
+
+
+def _graph(ops):
+    writer, readers, deps = {}, {}, []
+    for i, o in enumerate(ops):
+        d = set(writer[k] for k in o[2] if k in writer)
+        for k in o[3]:
+            d.update(([writer[k]] if k in writer else []) + readers.get(k, []))
+        for k in o[2]:
+            readers.setdefault(k, []).append(i)
+        for k in o[3]:
+            writer[k] = i
+            readers[k] = []
+        d.discard(i)
+        deps.append(sorted(d))
+    return deps
+
+
+def _kinds(ops):
+    short = lambda ks: "".join(k[:3] + k[4:] if k[1:3] == "nd" else k for k in ks)
+    kinds = [o[0] + "." + short(o[3][:1]) + "." + short(o[2][-1:]) for o in ops]
+    final = max(i for i, k in enumerate(kinds) if k == "V.EU.CRU")
+    return [k + "!" if i >= final else k for i, k in enumerate(kinds)]
+
+
+def _order(ops, shift):
+    deps, kinds = _graph(ops), _kinds(ops)
+    key = [i + shift.get(k, shift.get(k.rstrip("!"), 0)) for i, k in enumerate(kinds)]
+    placed, order = [False] * len(ops), []
+
+    def place(i):
+        placed[i] = True
+        for j in deps[i]:
+            if not placed[j]:
+                place(j)
+        order.append(i)
+    for i in sorted(range(len(ops)), key=lambda i: (key[i], i)):
+        if not placed[i]:
+            place(i)
+    return order
+
+
+def _emit(g, T, ops):
+    q = {"V": g.vector, "S": g.scalar, "T": g.tensor, "G": g, "Y": g.sync}
+    writer, readers, bank = {}, {}, {}
+    deps = []
+    for i, (e, fn, r, w, kind) in enumerate(ops):
+        d = set()
+        for k in r:
+            if k in writer:
+                d.add(writer[k])
+        for k in w:
+            d.update(([writer[k]] if k in writer else []) + readers.get(k, []))
+        for k in set(x[:2] for x in list(r) + list(w) if x[2:3] == ":"):
+            if k in bank and bank[k][0] != e:
+                d.add(bank[k][1])
+            bank[k] = (e, i)
+        if e == "T":
+            d = set(j for j in d if ops[j][0] != "T")
+        for k in r:
+            readers.setdefault(k, []).append(i)
+        for k in w:
+            writer[k] = i
+            readers[k] = []
+        deps.append(d)
+
+    def stream(j):
+        return ops[j][0] if ops[j][4] == "c" else ("op", j)
+
+    known, clock, waits, need = {}, {}, [], set()
+    for i, (e, fn, r, w, kind) in enumerate(ops):
+        kn = known.setdefault(e, {})
+        mine = []
+        if kind[0] != "arrive":
+            for j in sorted(deps[i], reverse=True):
+                if kn.get(stream(j), -1) < j and ops[j][4][0] != "send":
+                    mine.append(j)
+                    need.add(j)
+                    kn[stream(j)] = j
+                    for s, v in clock[j].items():
+                        if kn.get(s, -1) < v:
+                            kn[s] = v
+        waits.append(mine)
+        clock[i] = dict(kn) if kind[0] != "arrive" else {}
+    mark, cnt, nd, total = {}, {}, [0], {}
+    for i, (e, fn, r, w, kind) in enumerate(ops):
+        for j in waits[i]:
+            q[e].wait_ge(T.sem[mark[j][0]], mark[j][1])
+        if kind == "c":
+            ins = fn(q[e])
+            if i in need:
+                cnt[e] = cnt.get(e, 0) + 1
+                ins.then_inc(T.sem["q" + e], 1)
+                mark[i] = ("q" + e, cnt[e])
+                total["q" + e] = cnt[e]
+        elif kind == "d":
+            s = "d%d" % nd[0]
+            nd[0] += 1
+            fn(q[e]).then_inc(T.sem[s], 16)
+            mark[i] = (s, 16)
+            total[s] = 16
+        elif kind[0] == "send":
+            fn(q[e])
+            total["sent"] = total.get("sent", 0) + kind[1]
+        else:
+            mark[i] = (kind[1], kind[2])
+            total[kind[1]] = kind[2]
+    for s in sorted(total):
+        g.wait_ge(T.sem[s], total[s])
+
+
+def rank_program(g, core, T, topo):
+    rank = T.rank_of(core)
+    if rank is None:
+        return
+    n = len(T.cores)
+    ops = []
+
+    def op(e, fn, r, w, kind="c"):
+        ops.append((e, fn, r.split(), w.split(), kind))
+
+    def tt(out, a, b, o, r, w):
+        op("V", lambda q: q.tensor_tensor(out, a, b, o), r, w)
+
+    def ts(out, a, s1, o0, r, w, s2=None, o1=None):
+        if o1 is None:
+            op("V", lambda q: q.tensor_scalar(out, a, s1, None, o0), r, w)
+        else:
+            op("V", lambda q: q.tensor_scalar(out, a, s1, s2, o0, o1), r, w)
+
+    def cp(out, a, r, w):
+        op("V", lambda q: q.tensor_copy(out, a), r, w)
+
+    def scan(out, d0, d1, o0, o1, r, w):
+        op("V", lambda q: q.tensor_tensor_scan(out, d0, d1, 0.0, o0, o1), r, w)
+
+    def ms(ap, c, w):
+        op("V", lambda q: q.memset(ap, c), "", w)
+
+    def act(out, a, r, w, f=ACT.Identity, bias=0.0, scale=1.0, acc=None):
+        op("S", lambda q: q.activation(out, a, f, bias=bias, scale=scale, accum_out=acc), r, w)
+
+    def mm(out, l, rh, st, sp, r, w):
+        op("T", lambda q: q.matmul(out, l, rh, st, sp), r, w + " bank" + w[1])
+
+    def dma(e, out, a, r, w):
+        op(e, lambda q: q.dma_start(out, a), r, w, "d")
+
+    def iota(out, pat, base, cm, w, fl=True):
+        if fl:
+            op("G", lambda q: q.iota(out, pat, base, cm, allow_small_or_imprecise_dtypes=True), "", w)
+        else:
+            op("G", lambda q: q.iota(out, pat, base, cm), "", w)
+
+    def weave(*chains):
+        chains = [list(c) for c in chains]
+        while any(chains):
+            for c in chains:
+                if c:
+                    c.pop(0)()
+
+    A = ALU
+    col = lambda i: T.COL[:, i:i + 1]
+    PR, PG, ZC, RVC, MI, EN, SG, PAR, R0, R0N, R1A, R1B, E1, E2, HALF = [col(i) for i in range(15)]
+    XW, BW = T.XT[:], T.B[:]
+    XK = "X Xc Xt"
+    BK = "B B1 B2 B3 Bt"
+    c16 = T.LIN[:, 0:16]
+    I1, IH, IB, INB = [T.IV[:, 128 * i:128 * i + 128] for i in range(4)]
+    M1, M3, MD, M2, M4 = [T.MM[:, 256 * i:256 * i + 256] for i in range(5)]
+    BO1, BOX, BON = T.BO[:, 0:128], T.BO[:, 128:256], T.BO[:, 256:384]
+    PQ = [T.P0, T.P1]
+
+    ms(T.LN[:], 0, "LNz")
+    dma("S", T.KI[:], T.kt[:], "", "KI")
+    dma("Y", T.LN[0::16, 0:256], T.lc[:], "LNz", "LN")
+    dma("Y", T.LN[0::16, 256:512], T.lv[:], "LNz", "LN1")
+    dma("Y", T.LN[0::16, 512:768], T.ld[:], "LNz", "LN2")
+    dma("Y", T.XT[:, 0:2048], T.x[:, 0:2048], "", "X0")
+    dma("Y", T.XT[:, 2048:4096], T.x[:, 2048:4096], "", "X")
+    dma("Y", T.BI[:, 0:1024], T.bnd[:, 0:1024], "", "BI0")
+    dma("Y", T.BI[:, 1024:2048], T.bnd[:, 1024:2048], "", "BI1")
+
+    iota(T.PI[:, 0:1], [[0, 1]], 0, 1, "PI0", False)
+    iota(T.JF[:], [[1, 256]], 0, 0, "JF")
+    iota(T.CG[:], [[1, 8], [0, 16]], 0, 0, "CG")
+    iota(T.DI[:], [[1, 128]], 0, -1, "DI")
+    iota(T.SI[:], [[0, 16], [1, 16]], 0, 0, "SI")
+    iota(T.SR[:], [[0, 17], [-1, 16]], 15, 0, "SR")
+    iota(T.TI[:], [[0, 4], [16, 4]], 0, 0, "TI")
+    for mi in range(4):
+        iota(T.SD[:, SEG[mi]:SEG[mi + 1]], [[0, 4], [1, 64 - 16 * mi]], 0, 0, "SJ%d" % mi)
+    ts(T.PI[:, 1:2], T.PI[:, 0:1], 15, A.bitwise_and, "PI0", "PI1")
+    ts(T.PI[:, 2:3], T.PI[:, 0:1], 4, A.arith_shift_right, "PI0", "PI2")
+    ts(T.PI[:, 3:4], T.PI[:, 0:1], 1, A.bitwise_and, "PI0", "PI3")
+    ts(T.PI[:, 4:5], T.PI[:, 0:1], 3, A.bitwise_and, "PI0", "PI4")
+    ts(T.PI[:, 5:6], T.PI[:, 0:1], 2, A.arith_shift_right, "PI0", "PI5", 3, A.bitwise_and)
+    cp(T.COL[:, 0:2], T.PI[:, 1:3], "PI1 PI2", "C0")
+    ts(ZC, T.PI[:, 2:3], 16.0, A.mult, "PI2", "C2_", 15.0, A.add)
+    ts(RVC, T.PI[:, 1:2], -1.0, A.mult, "PI1", "C3", 255.0, A.add)
+    ts(R0, T.PI[:, 1:2], 0.0, A.is_equal, "PI1", "C8")
+    ts(R0N, T.PI[:, 1:2], 0.0, A.is_equal, "PI1", "C9", -2048.0, A.mult)
+    ts(SG, T.PI[:, 3:4], -2.0, A.mult, "PI3", "C6", 1.0, A.add)
+    cp(PAR, T.PI[:, 3:4], "PI3", "C7")
+    ts(R1A, T.PI[:, 1:2], 1.0, A.is_equal, "PI1", "C10_", -2.0 ** 27, A.mult)
+    ts(R1B, T.PI[:, 1:2], 1.0, A.is_equal, "PI1", "C11", -float(XO), A.mult)
+    cp(MI, T.PI[:, 4:5], "PI4", "C4")
+    ts(E1, T.PI[:, 4:5], -32.0, A.mult, "PI4", "C12", 288.0, A.add)
+    ts(E2, T.PI[:, 4:5], -16.0, A.mult, "PI4", "C15", 64.0, A.add)
+    ts(EN, T.PI[:, 5:6], 1.0, A.add, "PI5 C15", "C16", E2, A.mult)
+    ts(E2, EN, -1.0, A.add, "C16", "C13 C15")
+    ts(T.REV[:], T.JF[:, 0:16], -16.0, A.mult, "JF C3", "REV", RVC, A.add)
+    ts(T.ZH[:], T.JF[:, 0:144], ZC, A.is_equal, "JF C2_", "ZH")
+    ts(T.ENDS[:, 0:1], E1, MI, A.mult, "C12 C4 C13", "ENDS", E2, A.add)
+    ts(T.S8H[:], T.JF[:, 0:8], PG, A.is_equal, "JF C0", "S8H")
+    ts(T.S8F[:], T.JF[:, 0:8], PG, A.is_equal, "JF C0", "S8F")
+    cp(T.LIN[:], T.JF[:], "JF", "LIN")
+    ts(T.LAST[:], T.JF[:, 0:8], 16.0, A.mult, "JF", "LAST", 15.0, A.add)
+    ts(BO1, T.CG[:], PG, A.is_equal, "CG C0", "BO")
+    ts(BOX, T.CG[:], PG, A.is_equal, "CG C0", "BO4", float(XO), A.mult)
+    ts(T.WD[:, 0:128], T.CG[:], PG, A.is_equal, "CG C0 C10_", "WD0", R1A, A.mult)
+    ts(T.WD[:, 128:256], T.CG[:], PG, A.is_equal, "CG C0 C11", "WD1", R1B, A.mult)
+    for i, s in enumerate((1.0, 0.5, 1024.0, -1024.0)):
+        ts(T.IV[:, 128 * i:128 * i + 128], T.DI[:], 0.0, A.is_equal, "DI", "IV%d" % i, s, A.mult)
+    ts(T.IF[:], T.DI[:], 0.0, A.is_equal, "DI", "IF")
+    ts(M1, T.LN[:, 0:256].indirect(T.REV[:]), R0N, A.add, "LN LN1 LN2 C9 REV", "M1")
+    ts(M3, T.LN[:, 256:512].indirect(T.REV[:]), 2.0, A.mult, "LN LN1 LN2 REV", "M3")
+    ts(MD, T.LN[:, 512:768].indirect(T.REV[:]), -1.0, A.mult, "LN LN1 LN2 C8 REV", "MD", R0, A.add)
+    ts(T.BNB[:], T.SR[:], PR, A.not_equal, "SR C0", "BNB", -BIG, A.mult)
+    ms(T.XT[:, 4096:XO], 0.0, "Xt0")
+    ms(T.XT[:, XO + 4096:2 * XO], 0.0, "Xt")
+    act(T.XT[:, XO:XO + 2048], T.XT[:, 0:2048], "X0 Xt0", "Xc0", bias=255.0, scale=-1.0)
+
+    def wbatch():
+        for r in range(16):
+            mm(T.P4[:, 0:48], T.ZH[:, 15 - r:143 - r], T.MM[:, r:768:16], r == 0, r == 15, "ZH M1 M3 MD", "P4:w")
+
+    def wbatch_s():
+        act(T.WS[:, 32:48], T.P4[:, 32:48], "P4:w", "WS2", bias=2048.0 + XO, scale=-float(XO))
+        act(T.WS[:, 0:16], T.P4[:, 32:48], "P4:w", "WS0")
+        act(T.WS[:, 16:32], T.P4[:, 32:48], "P4:w", "WS1", bias=1.0, scale=-1.0)
+
+    def lanes_w():
+        return [
+            lambda: tt(T.CPF[:], T.P4[:, 0:16], T.WS[:, 32:48], A.add, "P4:w WS2", "CPF"),
+            lambda: ts(T.CI[:, 0:16], T.P4[:, 0:16], 2048.0, A.add, "P4:w", "CI0"),
+            lambda: tt(T.CR[:], T.P4[:, 16:32], T.WS[:, 0:16], A.add, "P4:w WS0", "CR"),
+            lambda: tt(T.CO[:, 0:16], T.P4[:, 16:32], T.WS[:, 16:32], A.add, "P4:w WS1", "CO0"),
+            lambda: cp(T.CPU[:], T.CPF[:], "CPF", "CPU"),
+            lambda: ts(T.CI[:, 16:32], T.CI[:, 0:16], 1023, A.bitwise_and, "CI0", "CI1"),
+            lambda: cp(T.CU[:], T.CI[:, 0:16], "CI0", "CU"),
+            lambda: cp(T.CRU[:], T.CR[:], "CR", "CRU"),
+            lambda: cp(T.C10[:], T.CI[:, 16:32], "CI1", "C10")]
+
+    def distances(ab, rows, w, rk, wk):
+        for m in range(16):
+            b, mi = m // 4, m % 4
+            st = SEG[mi] + b * (64 - 16 * mi)
+            act(ab[:, st:st + 64 - 16 * mi], rows[:, 16 * m:64 * b + 64], rk, "%s%d" % (wk, m), f=ACT.Abs, bias=w(m), scale=-1.0)
+
+    def rivals(sc, ab, u, tr, neg, out, k, rk, wk):
+        return [lambda: scan(sc[:], ab[:], T.MK[:], A.min, A.max, "MK " + " ".join("%s%d" % (k, m) for m in range(16)), k + "s"),
+                lambda: tt(u, sc[:].indirect(T.ENDS[:, 0:1]), tr[:], A.subtract, "ENDS TR " + k + "s", k + "u"),
+                lambda: tt(out, u, neg, A.min, k + "u " + rk, wk)]
+
+    def lanes_pe(t):
+        o = (-5 * t) % 16
+        mm(T.P3[:, 256:512], BO1, MD, True, True, "BO MD", "P3:d")
+        for h in range(2):
+            mm(T.P3[:, 8 * h:8 * h + 8], T.MM[:, 128 * h:128 * h + 128], T.S8H[:], True, True, "M1 S8H", "P3:p")
+        mm(T.P5[:, 256:512], BO1, M3, True, False, "BO M3", "P5:o")
+        mm(T.P5[:, 256:512], BO1, MD, False, True, "BO MD", "P5:o")
+        mm(T.P5[:, 0:256], I1, T.BNB[:, o:o + 256], True, False, "IV0 BNB", "P5:v")
+        if t < ST - 1:
+            mm(T.P5[:, 0:256], BOX, MD, False, False, "BO4 MD", "P5:v")
+        mm(T.P5[:, 0:256], BO1, M1, False, True, "BO M1", "P5:v")
+
+    def lanes_s0():
+        act(T.DX[:], T.P3[:, 256:512], "P3:d C6 C7", "DX", bias=PAR, scale=SG)
+        act(T.CL[:], T.P3[:, 0:16], "P3:p", "CL")
+
+    def lanes_s():
+        act(T.VO[:], T.P5[:, 0:256], "P5:v", "VO", bias=2048.0)
+        act(T.CO[:, 16:32], T.CO[:, 0:16], "CO0", "CO1", scale=-1.0 / BIG)
+        distances(T.ABO, T.P5[:, 256:512], lambda m: T.CR[:, m:m + 1], "P5:o CR", "ABO")
+
+    def own_rivals():
+        return rivals(T.SCO, T.ABO, T.UO[:, 0:16], T.TRB, T.CO[:, 16:32], T.UO[:, 16:32], "ABO", "CO1", "UO") + [
+            lambda: ts(T.OC[:], T.UO[:, 16:32], -BIG, A.mult, "UO", "OC")]
+
+    def shapes_of_lanes():
+        act(T.QC[:], XW.indirect(T.CPU[:]), XK + " CPU", "QC")
+        for h in range(2):
+            for k in range(16):
+                act(T.QQ[:, 2048 * h + k:2048 * h + 2048:16], T.QC[:, 128 * h:128 * h + 128], "QC", "QQ%d_%d" % (h, k))
+
+    def remote(out, in_, sem, dst, src, r, w, landed):
+        rid, pid, _ = topo.addr(dst)
+        op("G", lambda q: q.remote_dma(out, in_, T.sem[sem], T.sem.sent, pid, rid, topo.mask(core, dst)), r, w,
+           ("send", len(topo.engines(core, dst))))
+        op("G", None, w, landed, ("arrive", sem, len(topo.engines(src, core))))
+
+    def append(t, oc, old, val, ok, rk, vk):
+        o = (-5 * t) % 16
+        return [lambda: tt(old[:], BW.indirect(oc[:]), T.BM[:, o:o + 256], A.subtract, BK + " BM " + rk, ok)] + [
+            (lambda b=b: tt(BW.indirect(oc[:, 4 * b:4 * b + 4]), old[:, 64 * b:64 * b + 64], val[:, 64 * b:64 * b + 64], A.max,
+                            ok + " " + rk + " " + vk, "B")) for b in range(4)]
+
+    wbatch()
+    wbatch_s()
+    lanes_pe(0)
+    ms(T.ON[:], 1.0 / 128, "ON")
+    ms(T.CQ[:, 128:256], 2.0 ** 26, "CQ1")
+    ms(T.CQ[:, 256:384], 2.0 ** 25, "CQ2")
+    ms(T.CQ[:, 512:640], -64.0, "CQ4")
+    ms(T.DL[:], 60.0, "DL")
+    ms(T.B[:, 2048:2112], 0.0, "Bt")
+    ms(HALF, 0.5, "C14")
+    for c in range(2):
+        if c not in S_CHUNKS and S_CHUNKS:
+            ms(T.GD[:, 1024 * c:1024 * c + 1024], 1.0, "GD%d" % c)
+    weave(lanes_w())
+    lanes_s0()
+    for i, s in enumerate((8192.0, -4096.0, -8192.0, -4096.0, 4.0)):
+        ts(T.W3[:, 8 * i:8 * i + 8], T.S8F[:], s, A.mult, "S8F", "W3%d" % i)
+    ts(T.CQ[:, 0:128], T.SI[:, 0:128], 256.0, A.mult, "SI", "CQ0")
+    ts(T.CQ[:, 384:512], T.SI[:, 0:128], -256.0, A.mult, "SI", "CQ3")
+    ts(T.MS[:], T.SI[:], PR, A.is_equal, "SI C0", "MS")
+    ts(T.ND[:], T.SI[:], PR, A.not_equal, "SI C0", "ND", BIG, A.mult)
+    ts(T.BM[:], T.SR[:], PR, A.is_equal, "SR C0", "BM", BIG, A.mult)
+    ts(BON, T.CG[:], PG, A.is_equal, "CG C0", "BO5", -float(XO), A.mult)
+    ts(T.RSB[:], T.SI[:], 0.0, A.is_equal, "SI", "RSB", 2.0 ** 28, A.mult)
+    ts(T.RS0[:], T.SI[:, 0:128], 1.0, A.min, "SI", "RS0")
+    ts(T.MK[:], T.SD[:, 0:640], PR, A.is_le, "SJ0 SJ1 SJ2 SJ3 C0", "MK SD0", BIG, A.mult)
+    ts(T.TRX[:], T.TI[:], PR, A.add, "TI C0", "TRa", 1.0 / BIG, A.mult)
+    cp(T.KF[:], T.KI[:], "KI", "KF")
+    ts(T.TRB[:], T.TRX[:], 2048.0 / BIG, A.add, "TRa", "TR")
+    ts(T.KA[:], T.KI[:], 1023, A.bitwise_and, "KI", "KA")
+    ts(T.TRX[:], T.TRX[:], 4096.0 / BIG, A.add, "TRa", "TRa TR")
+    ts(T.KV[:], T.KA[:], 2.0, A.mult, "KA", "KV")
+    act(T.XT[:, XO + 2048:XO + 4096], T.XT[:, 2048:4096], "X Xc0", "Xc", bias=255.0, scale=-1.0)
+    shapes_of_lanes()
+    ts(T.B[:, 0:1024:2], T.BI[:, 0:1024:2], float(XO), A.add, "BI0", "B2")
+    cp(T.B[:, 1:1024:2], T.BI[:, 1:1024:2], "BI0", "B1")
+    ts(T.B[:, 1024:2048:2], T.BI[:, 1024:2048:2], float(XO), A.add, "BI1", "B")
+    cp(T.B[:, 1025:2048:2], T.BI[:, 1025:2048:2], "BI1", "B3")
+
+    for t in range(ST):
+        last = t == ST - 1
+        o = (-5 * t) % 16
+        sa = slice(16 * t, 16 * t + 16)
+        sk, lk = "snd%d" % t, "lnd%d" % t
+        cp(T.EU[:], BW.indirect(T.CRU[:]), BK + " CRU", "EU")
+        act(T.EF[:], BW.indirect(T.CRU[:]), BK + " CRU", "EF")
+        for h in range(2):
+            k = "P%d:q" % h
+            mm(PQ[h][:], T.ON[:], T.CQ[:, 0:512], True, False, "ON CQ0 CQ1 CQ2 CQ3", k)
+            mm(PQ[h][:, 256:512], T.DX[:, 128 * h:128 * h + 128], T.WD[:], False, False, "DX WD0 WD1", k)
+        if S_CHUNKS:
+            mm(PQ[0][:, 0:128], T.ON[:], T.CQ[:, 512:640], False, False, "ON CQ4", "P0:q")
+        for h in range(2):
+            mm(PQ[h][:, 384:512], T.EF[:, 128 * h:128 * h + 128], T.IF[:], False, False, "EF IF", "P%d:q" % h)
+        if t:
+            act(T.DL[:], T.PF[:].indirect(T.LIN[:, 0:8]), "PF LIN", "DL", bias=60.0, scale=-8.0)
+        for h in range(2):
+            mm(PQ[h][:, 0:128], T.ON[:], T.DL[:], False, False, "ON DL", "P%d:q" % h)
+        if last:
+            act(T.B[:, 0:2048:2], T.B[:, 0:2048:2], BK, "B", bias=-float(XO))
+        for c in range(4):
+            sl = slice(1024 * c, 1024 * c + 1024)
+            tt(T.SD[:, sl], XW.indirect(T.EU[:, 64 * c:64 * c + 64]), T.QQ[:, sl], A.subtract,
+               XK + " EU " + " ".join("QQ%d_%d" % (c // 2, k) for k in range(16)), "SD%d" % c)
+            if c in S_CHUNKS:
+                act(T.HD[:, sl], T.SD[:, sl], "SD%d" % c, "HD%d" % c, f=ACT.Relu)
+                act(T.GD[:, sl], T.SD[:, sl], "SD%d C14" % c, "GD%d" % c, f=ACT.Sign, bias=HALF)
+            for j in ([c - 1] if c > 0 and c - 1 not in S_CHUNKS else []) + ([c] if c == 3 else []):
+                ts(T.HD[:, 1024 * j:1024 * j + 1024], T.SD[:, 1024 * j:1024 * j + 1024], -2.0 ** -10, A.max, "SD%d" % j, "HD%d" % j)
+            if c % 2:
+                h = c // 2
+                for k in range(16):
+                    mm(PQ[h][:, 128 + k:512:16], T.SD[:, 2048 * h + k:2048 * h + 2048:16], T.W3[:, 8:32], False, False,
+                       "SD%d SD%d W31 W32 W33" % (c - 1, c), "P%d:q" % h)
+            if c >= 2:
+                h = c - 2
+                sg = h == 0 and bool(S_CHUNKS)
+                for k in range(16):
+                    mm(PQ[h][:, k:128:16], T.HD[:, 2048 * h + k:2048 * h + 2048:16], T.W3[:, 0:8], False, k == 15 and not sg,
+                       "HD%d HD%d W30" % (2 * h, 2 * h + 1), "P%d:q" % h)
+                for k in range(16 if sg else 0):
+                    mm(PQ[0][:, k:128:16], T.GD[:, k:2048:16], T.W3[:, 32:40], False, k == 15, "GD0 GD1 W34", "P0:q")
+        lanes_s()
+        act(T.QT[:], XW.indirect(T.CU[:]), XK + " CU", "QT")
+        act(T.KC[:], T.KF[:].indirect(T.C10[:]), "KF C10", "KC", bias=-2048.0)
+        act(T.QH[:, 0:256], T.QT[:], "QT", "QH0", bias=-159.625, scale=-0.25)
+        act(T.QH[:, 256:512], T.QT[:], "QT", "QH1", scale=0.5)
+        mm(T.P6[:], I1, T.QH[:], True, False, "IV0 QH0 QH1", "P6:a")
+        mm(T.P7[:, 0:256], I1, T.ND[:], True, False, "IV0 ND", "P7:r")
+
+        def choice(h):
+            sl = slice(128 * h, 128 * h + 128)
+            s2 = slice(256 + 128 * h, 384 + 128 * h)
+            k, H = "P%d:q" % h, str(h)
+            return [
+                lambda: ts(T.P8[:, sl], PQ[h][:, 0:128], 1.5 * 2.0 ** 31, A.add, k, "P8" + H, -1.5 * 2.0 ** 31, A.add),
+                lambda: tt(T.NC[:, sl], T.P8[:, sl], PQ[h][:, 0:128], A.is_gt, k + " P8" + H, "NC" + H),
+                lambda: tt(T.P2[:, s2], T.P8[:, sl], PQ[h][:, 384:512], A.add, k + " P8" + H, "P2:y" + H),
+                lambda: tt(T.TA[:, sl], T.NC[:, sl], PQ[h][:, 128:256], A.mult, k + " NC" + H, "TA" + H),
+                lambda: tt(T.P2[:, sl], T.TA[:, sl], PQ[h][:, 256:384], A.max, k + " TA" + H, "P2:t" + H),
+                lambda: tt(T.KEY[:, sl], T.P8[:, sl], T.P2[:, sl], A.add, "P8%s P2:t%s" % (H, H), "KEY" + H),
+                lambda: scan(T.SC1[:, sl], T.RSB[:, 0:128], T.KEY[:, sl], A.max, A.min, "RSB KEY" + H, "SC1" + H),
+                lambda: tt(T.EQ[:, sl], T.SC1[:, sl].indirect(T.LAST[:]), T.KEY[:, sl], A.is_equal, "LAST SC1%s KEY%s" % (H, H), "EQ" + H),
+                lambda: tt(T.RP[:, sl], T.EQ[:, sl], T.P2[:, s2], A.mult, "EQ%s P2:y%s" % (H, H), "RP" + H),
+                lambda: scan(T.SC2[:, sl], T.RS0[:], T.RP[:, sl], A.mult, A.max, "RS0 RP" + H, "SC2" + H)]
+        c0, c1 = choice(0), choice(1)
+        ow = own_rivals()
+        weave(c0[:6], ow[:1])
+        weave(c1, c0[6:] + ow[1:])
+        own = append(t, T.OC, T.OLD, T.VO, "OLD", "OC", "VO")
+        cp(T.YI[:], T.SC2[:, 15::16], "SC20 SC21", "YI")
+        ts(T.HL[:], T.SC1[:, 15::16], 2.0 ** 26, A.is_lt, "SC10 SC11", "HL")
+        ts(T.SE[:], T.YI[:], 4095, A.bitwise_and, "YI", "SE")
+        ts(T.PP[:], T.YI[:], 12, A.arith_shift_right, "YI", "PP", 15, A.bitwise_and)
+        ts(T.SM[:, 0:16], T.SE[:], -2048.0, A.add, "SE", "SM0")
+        act(T.HM[:], T.HL[:].indirect(c16), "HL LIN", "HM")
+        tt(T.PM[:], T.PP[:].indirect(c16), T.SI[:], A.is_equal, "PP LIN SI", "PM")
+        tt(T.DG[:, 0:256], T.SM[:, 0:16].indirect(c16), T.MS[:], A.mult, "SM0 LIN MS", "DG0")
+        act(T.PM2[:, 0::2], T.PM[:, 1::2], "PM", "PM2a")
+        act(T.PM2[:, 1::2], T.PM[:, 0::2], "PM", "PM2b")
+        for h in range(2):
+            mm(T.P3[:, 128 * h:128 * h + 128], T.PM[:, 128 * h:128 * h + 128], I1, True, True, "PM IV0", "P3:p")
+        for j in range(2):
+            mm(T.P4[:, 128 + 8 * j:136 + 8 * j], T.DG[:, 128 * j:128 * j + 128], T.S8H[:], True, True, "DG0 S8H", "P4:e")
+        for h in range(2):
+            mm(T.P2[:, 128 * h:128 + 128 * h], T.PM2[:, 128 * h:128 * h + 128], I1, True, True, "PM2a PM2b IV0", "P2:t0 P2:t1")
+        tt(T.T5[:, 0:16], T.SM[:, 0:16], T.CL[:], A.subtract, "SM0 CL", "T50")
+        tt(MD, T.P3[:, 0:256], T.DX[:], A.mult, "P3:p DX", "MD")
+        tt(T.T5[:, 16:32], T.T5[:, 0:16], T.HL[:], A.mult, "T50 HL", "T51")
+        ts(T.EI[:, 0:16], T.P4[:, 128:144], 2048.0, A.add, "P4:e", "EI0")
+        tt(T.SM[:, 16:32], T.T5[:, 16:32], T.CL[:], A.add, "T51 CL", "SM1")
+        ts(T.EI[:, 16:32], T.EI[:, 0:16], 1023, A.bitwise_and, "EI0", "EI1")
+        cp(T.EW[:], T.EI[:, 0:16], "EI0", "EW")
+        cp(T.E10[:], T.EI[:, 16:32], "EI1", "E10")
+        mm(T.P7[:, 0:256], BO1, MD, False, False, "BO MD", "P7:r")
+        mm(T.P1[:, 0:256], BO1, MD, True, False, "BO MD", "P1:q")
+        act(T.KE[:], T.KV[:].indirect(T.E10[:]), "KV E10", "KE")
+        act(T.PE_[:], T.SM[:, 16:32].indirect(c16), "SM1 LIN", "PE")
+        act(T.YT[:], XW.indirect(T.EW[:]), XK + " EW", "YT")
+        tt(M2, T.P2[:, 0:256], T.KC[:], A.mult, "P2:t0 P2:t1 KC", "M2")
+        tt(M1, T.P3[:, 0:256], T.KC[:], A.mult, "P3:p KC", "M1")
+        tt(M4, T.P2[:, 0:256], T.KE[:], A.mult, "P2:t0 P2:t1 KE", "M4")
+        tt(T.DG[:, 256:512], T.SM[:, 16:32].indirect(c16), T.MS[:], A.mult, "SM1 LIN MS", "DG1")
+        for h in range(2):
+            sl, s2 = slice(128 * h, 128 * h + 128), slice(256 + 128 * h, 384 + 128 * h)
+            mm(T.P6[:, sl], T.HM[:, sl], INB, False, False, "HM IV3", "P6:a")
+            mm(T.P6[:, s2], T.HM[:, sl], IB, False, False, "HM IV2", "P6:a")
+        mm(T.P7[:, 0:256], BO1, M4, False, True, "BO M4", "P7:r")
+        mm(T.P1[:, 0:256], BO1, M4, False, True, "BO M4", "P1:q")
+        for j in range(2):
+            mm(T.P4[:, 144 + 8 * j:152 + 8 * j], T.DG[:, 256 + 128 * j:384 + 128 * j], T.S8H[:], True, True, "DG1 S8H", "P4:x")
+        for h in range(2):
+            sl = slice(128 * h, 128 * h + 128)
+            mm(T.P0[:, sl], T.PE_[:, sl], T.IF[:], True, True, "PE IF", "P0:q")
+        mm(T.P6[:, 0:256], I1, T.YT[:], False, False, "IV0 YT", "P6:a")
+        mm(T.P6[:, 256:512], IH, T.YT[:], False, True, "IV1 YT", "P6:a")
+        dst = T.cores[(rank + 1 + t % (n - 1)) % n]
+        src = T.cores[(rank - 1 - t % (n - 1)) % n]
+        sv = slice(256 * t, 256 * t + 256)
+        mm(T.P5[:, 0:256], I1, T.BNB[:, o:o + 256], True, False, "BNB IV0", "P5:v")
+        if not last:
+            mm(T.P5[:, 0:256], BON, MD, False, False, "MD BO5", "P5:v")
+        mm(T.P5[:, 0:256], BO1, M2, False, True, "BO M2", "P5:v")
+        act(T.SV[:, sv], T.P5[:, 0:256], "P5:v", sk + "b", bias=2048.0 if last else 2048.0 + XO)
+        remote(T.LV[:, sv], T.SV[:, sv], "arv%d" % t, dst, src, sk + "b", sk + "y", lk + "v")
+        scan(T.SW[:], T.RSB[:], T.P7[:, 0:256], A.max, A.min, "RSB P7:r", "SW")
+        tt(M3, T.P3[:, 0:256], T.KE[:], A.mult, "P3:p KE", "M3")
+        distances(T.AB2, T.P1[:, 0:256], lambda m: T.SW[:, 16 * m + 15:16 * m + 16], "P1:q SW", "AB2")
+        act(T.C2[:], T.SW[:, 15::16], "SW", "C2n", scale=-1.0 / BIG)
+        act(T.WX[:, 0:16], T.P4[:, 144:160], "P4:x", "WX0")
+        act(T.WX[:, 16:32], T.P4[:, 144:160], "P4:x", "WX1", scale=-1.0 / BIG, bias=-2048.0 / BIG)
+        if not last:
+            wbatch()
+        distances(T.ABX, T.P0[:, 0:256], lambda m: T.WX[:, m:m + 1], "P0:q WX0", "ABX")
+        act(T.AA[:], T.P6[:, 0:256], "P6:a", "AA", f=ACT.Abs, bias=1184.0)
+        act(T.RR[:], T.P6[:, 256:512], "P6:a", "RR", bias=1.5 * 2.0 ** 23, scale=0.9995)
+        act(T.R2[:], T.RR[:], "RR", "R2", bias=-1.5 * 2.0 ** 23)
+        s2 = rivals(T.SC3, T.AB2, T.U2[:], T.TRB, T.C2[:], T.SND[:, sa], "AB2", "C2n", sk + "a")
+        xr = rivals(T.SCX, T.ABX, T.UX[:, 0:16], T.TRX, T.WX[:, 16:32], T.UX[:, 16:32], "ABX", "WX1", "UX") + [
+            lambda: ts(T.OX[:], T.UX[:, 16:32], -BIG, A.mult, "UX", "OX")]
+        weave(own[:2])
+        weave(s2, own[2:])
+        remote(T.LND[:, sa], T.SND[:, sa], "arr%d" % t, dst, src, sk + "a " + sk + "y", sk + "x", lk)
+        weave(xr)
+        tt(T.VA[:], T.AA[:], T.R2[:], A.min, "AA R2", "VA")
+        for h in range(2):
+            mm(T.P3[0:8, 16:17], T.HL[:, 8 * h:8 * h + 8], T.ON[:, 0:1], h == 0, h == 1, "HL ON", "P3:p")
+        if not last:
+            act(T.VC[:], T.VA[:], "VA", "VC", bias=255.0, scale=-1.0)
+            for h in range(2):
+                mm(T.P7[:, 256:264], T.ON[:], T.HL[:, 8 * h:8 * h + 8], h == 0, h == 1, "HL ON", "P7:n")
+        act(T.YM[0:8, t:t + 1], T.P3[0:8, 16:17], "P3:p", "YM", bias=256.0, scale=-128.0)
+        xa = [(lambda b=b: cp(T.XT[:, 0:XO].indirect(T.OX[:, 4 * b:4 * b + 4]), T.VA[:, 64 * b:64 * b + 64], "VA OX", "X")) for b in range(4)]
+        xc = [(lambda b=b: cp(T.XT[:, XO:2 * XO].indirect(T.OX[:, 4 * b:4 * b + 4]), T.VC[:, 64 * b:64 * b + 64], "VC OX", "Xc")) for b in range(4)]
+        if not last:
+            wbatch_s()
+            lanes_pe(t + 1)
+            lanes_s0()
+            lw = lanes_w()
+            weave(xa, xc[:3])
+            weave(xc[3:] + [lw[4]], [lw[0]])
+            shapes_of_lanes()
+            fill = lw[1:4] + lw[5:] + [lambda: ts(T.PA[:, 0:8], T.P7[:, 256:264], 128.0, A.mult, "P7:n", "PA0"),
+                                       lambda: ts(T.PA[:, 8:16], T.PA[:, 0:8], 1, A.bitwise_and, "PA0", "PA1"),
+                                       lambda: cp(T.PF[:], T.PA[:, 8:16], "PA1", "PF")]
+        else:
+            fill = []
+            weave(xa)
+            for b in range(8):
+                act(T.SD[:, 512 * b:512 * b + 512], T.XT[:, 512 * b:512 * b + 512], "X", "YS%d SD%d" % (b, b // 2), acc=T.YS[:, b:b + 1])
+            dma("S", T.ys[:], T.YS[:], " ".join("YS%d" % b for b in range(8)), "")
+            dma("S", T.ym[:], T.YM[0:8, 0:ST], "YM", "")
+            for j, (a, b) in enumerate(((1.0, 2048.0), (0.5, 0.0), (-1.0, 1.0))):
+                bank = (T.P5, T.P5, T.P7)[j]
+                cs = slice(256 * (j % 2), 256 * (j % 2) + 256)
+                k = ("P5:v", "P5:o", "P7:r")[j]
+                mm(bank[:, cs], BO1, (M1, M3, MD)[j], True, True, "BO M1 M3 MD", k)
+                act(T.YO[:, 256 * j:256 * j + 256], bank[:, cs], k, "YO%d" % j, bias=b, scale=a)
+                act(T.YR[:, 256 * j:256 * j + 256], T.YO[:, 256 * j:256 * j + 256].indirect(T.REV[:]), "REV YO%d" % j, "YR%d" % j)
+                dma("S", (T.yc, T.yv, T.yd)[j][:], T.YR[0::16, 256 * j:256 * j + 256], "YR%d" % j, "")
+        ts(T.RC[:], T.LND[:, sa], -BIG, A.mult, lk, "RC")
+        rec = append(t, T.RC, T.OL2, T.LV[:, sv], "OL2", "RC", lk + "v")
+        weave(rec, fill[0::2], fill[1::2])
+    dma("Y", T.yb[:], T.B[:, 0:2048], "B", "")
+    _emit(g, T, [ops[i] for i in _order(ops, SHIFT)])

@@ -2,136 +2,144 @@ from concourse.mybir import AluOpType as ALU, ActivationFunctionType as ACT
 
 ST = 6
 F32, BF, F16, I32, U16 = "float32", "bfloat16", "float16", "int32", "uint16"
-XO = 4160
 BIG = 16384.0
 SEG = (0, 256, 448, 576, 640)
-S_CHUNKS = (0,)
+QD, QA, QKE, QKC, QE, QM, QP, QA2, Q1 = 0, 1, 2, 3, 4, 5, 6, 7, 15
+CHUNKS = ((0, 1024, "S"), (1024, 2048, "S"), (2048, 3072, "S"), (3072, 3584, "S"), (3584, 4096, "S"))
 
-
-def _sb(n, dt):
-    return ("sbuf", [128, n], dt)
-
-
-SCRATCH = {
-    "XT": _sb(2 * XO, BF), "B": _sb(2112, F32), "BI": _sb(2048, I32),
-    "KI": _sb(1024, I32), "KA": _sb(1024, I32), "KF": _sb(1024, F32), "KV": _sb(1024, F32), "LN": _sb(768, I32),
-    "JF": _sb(256, F32), "SI": _sb(256, F32), "SR": _sb(272, F32), "CG": _sb(128, F32), "DI": _sb(128, F32), "TI": _sb(16, F32),
-    "PI": _sb(8, I32), "COL": _sb(24, F32), "LIN": _sb(256, U16), "LAST": _sb(8, U16), "ENDS": _sb(2, U16), "REV": _sb(16, U16),
-    "MS": _sb(256, F32), "ND": _sb(256, BF), "BM": _sb(272, F32), "BNB": _sb(272, BF),
-    "MK": _sb(640, BF), "RSB": _sb(256, F32), "RS0": _sb(128, F32), "TRB": _sb(16, F32), "TRX": _sb(16, F32),
-    "BO": _sb(384, F16), "S8F": _sb(8, F32), "S8H": _sb(8, F16), "W3": _sb(40, BF),
-    "WD": _sb(256, BF), "CQ": _sb(640, BF), "ON": _sb(128, BF), "IV": _sb(512, BF), "IF": _sb(128, F32), "ZH": _sb(144, F16),
-    "EU": _sb(256, U16), "EF": _sb(256, F32), "QC": _sb(256, BF), "QQ": _sb(4096, BF),
-    "SD": _sb(4096, BF), "HD": _sb(4096, BF), "GD": _sb(2048, BF),
-    "P8": _sb(256, F32), "NC": _sb(256, F32), "TA": _sb(256, F32), "KEY": _sb(256, F32), "SC1": _sb(256, F32),
-    "EQ": _sb(256, F32), "RP": _sb(256, F32), "SC2": _sb(256, F32),
-    "YI": _sb(16, I32), "PP": _sb(16, I32), "SM": _sb(32, F32), "SE": _sb(16, I32), "HL": _sb(16, BF), "CL": _sb(16, F32), "T5": _sb(32, F32),
-    "PM": _sb(256, BF), "PM2": _sb(256, BF), "DG": _sb(512, F16), "EI": _sb(32, I32), "EW": _sb(16, U16), "E10": _sb(16, U16),
-    "MM": _sb(1280, F16), "KC": _sb(256, F32), "KE": _sb(256, F32), "DX": _sb(256, BF), "DL": _sb(128, BF), "PA": _sb(16, I32), "PF": _sb(8, F32),
-    "WS": _sb(64, F32), "SW": _sb(256, F32), "C2": _sb(16, F32), "CR": _sb(16, F32), "CO": _sb(32, F32), "CRU": _sb(16, U16), "WX": _sb(32, F32),
-    "CI": _sb(32, I32), "CU": _sb(16, U16), "C10": _sb(16, U16), "CPF": _sb(16, F32), "CPU": _sb(16, U16),
-    "ABX": _sb(640, BF), "AB2": _sb(640, BF), "ABO": _sb(640, BF), "SCX": _sb(640, BF), "SC3": _sb(640, BF), "SCO": _sb(640, BF),
-    "UX": _sb(32, F32), "U2": _sb(16, F32), "UO": _sb(32, F32),
-    "OC": _sb(16, U16), "RC": _sb(16, U16), "OX": _sb(16, U16),
-    "VO": _sb(256, F32), "OLD": _sb(256, F32), "OL2": _sb(256, F32),
-    "HM": _sb(256, BF), "PE_": _sb(256, F32),
-    "QT": _sb(256, BF), "QH": _sb(512, BF), "YT": _sb(256, BF), "AA": _sb(256, BF), "RR": _sb(256, F32), "R2": _sb(256, BF),
-    "VA": _sb(256, BF), "VC": _sb(256, BF), "SND": _sb(16 * ST, F32), "LND": _sb(16 * ST, F32), "SV": _sb(256 * ST, F32), "LV": _sb(256 * ST, F32),
-    "YS": _sb(8, F32), "YM": _sb(8, F32), "YO": _sb(768, F32), "YR": _sb(768, F32),
+SB = {
+    "XT": (4160, BF), "B": (2112, F32), "BI": (2048, I32), "KI": (2048, I32), "KA": (2048, I32), "LN": (768, I32),
+    "PI": (8, I32), "COL": (24, F32), "JF": (256, F32), "CG": (128, F32), "SI": (128, F32), "SR": (272, F32), "EQ": (16, F32),
+    "REP": (1024, BF), "IDUP": (256, BF), "CI0": (512, F32), "CIN": (512, F16), "SJ": (640, BF), "SM": (640, BF), "MK": (640, BF),
+    "REPT": (640, BF), "RH": (128, BF), "BO": (128 * 15, BF), "IV": (128 * 5, BF), "IF": (128, F32), "ZH": (144 * 4, BF), "W3": (32, BF),
+    "S8": (8, BF), "BM": (272, F32), "BNB": (272, BF), "RSB": (128, F32), "CZ": (512, BF), "ON": (128, BF), "ZE": (128, BF),
+    "REV": (16, U16), "ENDS": (2, U16), "SELQ": (8, U16),
+    "EU": (256, U16), "EF": (256, F16), "QC": (256, BF), "QCT": (256, F16), "XG": (4096, BF), "H": (4096, F16),
+    "R0": (256, I32), "N": (256, F32), "NC": (256, F32), "SC1": (256, F32), "NE": (256, F32), "HY": (256, F32), "SC2": (256, F32),
+    "YI": (16, I32), "BT": (64, I32), "T5": (32, F32), "LT": (256, F16), "CL": (32, I32), "C10": (16, I32),
+    "G": (256, F16), "WT": (512, F32), "UW": (64, U16), "MSK": (256, BF), "MM": (512, F16), "WA": (128, BF), "PA": (8, I32), "PF": (8, F32),
+    "CU": (16, U16), "CRU": (16, U16), "OC": (16, U16), "OX": (16, U16),
+    "TW": (384, F16), "AB": (640 * 3, BF), "SC": (640 * 3, BF), "DW": (48, F32), "NG": (48, F32), "WN": (48, F32),
+    "VO": (256, F32), "OLD": (256, F32), "OL2": (256, F32), "YT": (256, BF), "ZR": (512, I32), "VA": (256, BF),
+    "SND": (16 * ST, U16), "LND": (16 * ST, U16), "SV": (256 * ST, F32), "LV": (256 * ST, F32),
+    "YS": (8, F32), "YM": (8, F32), "YO": (768, F32), "YR": (768, F32),
 }
-for _b in range(8):
-    SCRATCH["P%d" % _b] = ("psum", [128, 512], F32)
+SCRATCH = {k: ("sbuf", [128, n], dt) for k, (n, dt) in SB.items()}
+for _b in range(4):
+    SCRATCH["P%d" % _b] = ("psum", [128, 1024], F32)
 NDMA = 24
 SEMAPHORES = ["qV", "qS", "qT", "qG", "sent"] + ["arr%d" % t for t in range(ST)] + ["arv%d" % t for t in range(ST)] + ["d%d" % i for i in range(NDMA)]
 
 
-SHIFT = {'G.SR.':3,'G.sndy.sndb':-22,'S..YR0!':20,'S..YR1!':25,'S..YR2!':35,'S..YS7!':60,'S.AA.P6:a':10,'S.AB211.SW!':-35,'S.AB24.SW':-20,'S.B.Bt':20,'S.C2n.SW':7,'S.C2n.SW!':-33,'S.DL.LIN':-12,'S.EF.CRU':-5,'S.GD0.C14':65,'S.KI.':5,'S.QQ1_0.QC':43,'S.QQ1_1.QC':35,'S.QQ1_11.QC':20,'S.QQ1_15.QC':15,'S.QQ1_3.QC':27,'S.QQ1_5.QC':30,'S.QQ1_9.QC':21,'S.R2.RR':8,'S.Xc0.Xt0':-37,'S.YM.P3:p':-8,'S.YR1.YO1!':20,'S.YS1.X!':-12,'S.YS3.X!':5,'S.YS5.X!':12,'S.YS7.X!':30,'T.P0:q.IF!':-12,'T.P0:q.W30':-3,'T.P0:q.W34!':-35,'T.P1:q.MD!':1,'T.P1:q.WD1':-20,'T.P5:v.IV0':-45,'T.P5:v.M2':-21,'T.P6:a.IV2':67,'T.P6:a.IV3':60,'T.P6:a.IV3!':20,'V.B.VO!':28,'V.BM.C0':-35,'V.BNB.C0':-8,'V.BO5.C0':-27,'V.C0.PI2':12,'V.C15.PI4':-4,'V.C2_.PI2':12,'V.CO0.WS1':12,'V.CPF.WS2':-2,'V.CR.WS0':-3,'V.CU.CI0':25,'V.DL.':-60,'V.E10.EI1!':-1,'V.EQ0.KEY0':-22,'V.EW.EI0!':8,'V.GD1.':-3,'V.M1.KC!':35,'V.MS.C0':-35,'V.NC0.P80':-60,'V.ND.C0':-70,'V.OC.UO':44,'V.OLD.OC!':10,'V.OX.UX':12,'V.P2:y0.P80':-6,'V.P81.P1:q':-5,'V.PA0.P7:n':-54,'V.PA1.PA0':-20,'V.RP0.P2:y0':-9,'V.SD1.QQ0_15!':-12,'V.SD3.QQ1_15':-8,'V.SM1.CL':20,'V.T50.CL':5,'V.T50.CL!':13,'V.T51.HL':60,'V.T51.HL!':30,'V.TRa.C0':-60,'V.UO.CO1!':60,'V.W31.S8F':60,'V.W34.S8F':-35,'V.Xc.OX':3,'V.Xt.':-20,'V.snda.C2n!':8,'Y.X0.':-20}
+def r(name, a=0, b=None, s=1, p=(0, 128, 1)):
+    return (name, a, SB[name][0] if b is None else b, s, p)
+
+
+def bank(k, a=0, b=512, s=1, p=(0, 128, 1)):
+    return ("P%d" % (k // 2), 512 * (k % 2) + a, 512 * (k % 2) + b, s, p)
+
+
+def sub(x, a, b, s=1):
+    return (x[0], x[1] + a * x[3], x[1] + (b - 1) * x[3] + 1, x[3] * s, x[4])
+
+
+def size(x):
+    return 16 * size(x[2]) if x[0] == "*" else len(range(x[1], x[2], x[3]))
+
+
+def _meet(x, y):
+    if x[2] <= y[1] or y[2] <= x[1] or x[4][1] <= y[4][0] or y[4][1] <= x[4][0]:
+        return False
+    return not (x[3] == y[3] > 1 and (x[1] - y[1]) % x[3])
+
+
+def _banks(x):
+    return [(x[0], k) for k in range(x[1] // 512, (x[2] - 1) // 512 + 1)] if x[0] not in SB and x[0][0] == "P" else []
 
 
 def _graph(ops):
-    writer, readers, deps = {}, {}, []
-    for i, o in enumerate(ops):
-        d = set(writer[k] for k in o[2] if k in writer)
-        for k in o[3]:
-            d.update(([writer[k]] if k in writer else []) + readers.get(k, []))
-        for k in o[2]:
-            readers.setdefault(k, []).append(i)
-        for k in o[3]:
-            writer[k] = i
-            readers[k] = []
+    seen, last, deps = {}, {}, []
+    for i, (e, fn, rd, wr, kind, cost) in enumerate(ops):
+        d = set()
+        for x, w in [(x, False) for x in rd] + [(x, True) for x in wr]:
+            d.update(j for j, y, v in seen.get(x[0], []) if (w or v) and _meet(x, y))
+        for k in set(b for x in rd + wr for b in _banks(x)):
+            old = last.get(k, (e, [], []))
+            if old[0] != e:
+                old = (e, [], old[1])
+            d.update(old[2] + (old[1][-1:] if e == "T" else []))
+            last[k] = (e, old[1] + [i], old[2])
+        for x in wr:
+            seen[x[0]] = [z for z in seen.get(x[0], []) if not (x[3] == 1 and x[4] == (0, 128, 1) and x[1] <= z[1][1] and z[1][2] <= x[2]) and z[1] != x]
+        for x, w in [(x, False) for x in rd] + [(x, True) for x in wr]:
+            seen.setdefault(x[0], []).append((i, x, w))
         d.discard(i)
         deps.append(sorted(d))
     return deps
 
 
-def _kinds(ops):
-    short = lambda ks: "".join(k[:3] + k[4:] if k[1:3] == "nd" else k for k in ks)
-    kinds = [o[0] + "." + short(o[3][:1]) + "." + short(o[2][-1:]) for o in ops]
-    final = max(i for i, k in enumerate(kinds) if k == "V.EU.CRU")
-    return [k + "!" if i >= final else k for i, k in enumerate(kinds)]
-
-
-def _order(ops, shift):
-    deps, kinds = _graph(ops), _kinds(ops)
-    key = [i + shift.get(k, shift.get(k.rstrip("!"), 0)) for i, k in enumerate(kinds)]
-    placed, order = [False] * len(ops), []
-
-    def place(i):
-        placed[i] = True
+def _order(ops, deps, after):
+    n = len(ops)
+    users = [[] for _ in ops]
+    for i in range(n):
         for j in deps[i]:
-            if not placed[j]:
-                place(j)
+            users[j].append(i)
+    hop = lambda j, i: 0 if ops[j][0] == ops[i][0] == "T" else HOP
+    tail = [0.0] * n
+    for i in reversed(range(n)):
+        tail[i] = ops[i][5] + max([tail[u] + hop(i, u) for u in users[i]] + [0])
+    left = [len(d) for d in deps]
+    then = {}
+    for i, j in after:
+        left[i] += 1
+        then.setdefault(j, []).append(i)
+    ready = {i: 0.0 for i in range(n) if not left[i]}
+    free, order, done = {}, [], {}
+    while ready:
+        start = {i: max(t, free.get(ops[i][0], 0.0)) for i, t in ready.items()}
+        i = min(start, key=lambda j: (start[j], -tail[j]))
+        near = [j for j in start if ops[j][0] == ops[i][0] and start[j] <= start[i] + NEAR * ops[i][5]]
+        i = max(near, key=lambda j: (tail[j], -j))
+        end = start[i] + ops[i][5]
+        free[ops[i][0]] = end if ops[i][4] == "c" else start[i] + (ops[i][5] if ops[i][4][0] == "send" else 60)
         order.append(i)
-    for i in sorted(range(len(ops)), key=lambda i: (key[i], i)):
-        if not placed[i]:
-            place(i)
+        del ready[i]
+        for u, at in [(u, end + hop(i, u)) for u in users[i]] + [(u, start[i]) for u in then.get(i, [])]:
+            left[u] -= 1
+            done[u] = max(done.get(u, 0.0), at)
+            if not left[u]:
+                ready[u] = done[u]
     return order
 
 
-def _emit(g, T, ops):
+HOP, NEAR = 80.0, 0.5
+
+
+def _emit(g, T, ops, deps, order):
     q = {"V": g.vector, "S": g.scalar, "T": g.tensor, "G": g, "Y": g.sync}
-    writer, readers, bank = {}, {}, {}
-    deps = []
-    for i, (e, fn, r, w, kind) in enumerate(ops):
-        d = set()
-        for k in r:
-            if k in writer:
-                d.add(writer[k])
-        for k in w:
-            d.update(([writer[k]] if k in writer else []) + readers.get(k, []))
-        for k in set(x[:2] for x in list(r) + list(w) if x[2:3] == ":"):
-            if k in bank and bank[k][0] != e:
-                d.add(bank[k][1])
-            bank[k] = (e, i)
-        if e == "T":
-            d = set(j for j in d if ops[j][0] != "T")
-        for k in r:
-            readers.setdefault(k, []).append(i)
-        for k in w:
-            writer[k] = i
-            readers[k] = []
-        deps.append(d)
+    pos = {j: i for i, j in enumerate(order)}
 
     def stream(j):
         return ops[j][0] if ops[j][4] == "c" else ("op", j)
 
-    known, clock, waits, need = {}, {}, [], set()
-    for i, (e, fn, r, w, kind) in enumerate(ops):
+    known, clock, waits, need = {}, {}, {}, set()
+    for i in order:
+        e, kind = ops[i][0], ops[i][4]
         kn = known.setdefault(e, {})
-        mine = []
+        waits[i] = []
         if kind[0] != "arrive":
-            for j in sorted(deps[i], reverse=True):
-                if kn.get(stream(j), -1) < j and ops[j][4][0] != "send":
-                    mine.append(j)
+            for j in sorted(deps[i], key=lambda j: -pos[j]):
+                if kn.get(stream(j), -1) < pos[j] and ops[j][4][0] != "send" and not (e == "T" == ops[j][0]):
+                    waits[i].append(j)
                     need.add(j)
-                    kn[stream(j)] = j
+                    kn[stream(j)] = pos[j]
                     for s, v in clock[j].items():
                         if kn.get(s, -1) < v:
                             kn[s] = v
-        waits.append(mine)
         clock[i] = dict(kn) if kind[0] != "arrive" else {}
     mark, cnt, nd, total = {}, {}, [0], {}
-    for i, (e, fn, r, w, kind) in enumerate(ops):
+    for i in order:
+        e, fn, kind = ops[i][0], ops[i][1], ops[i][4]
         for j in waits[i]:
             q[e].wait_ge(T.sem[mark[j][0]], mark[j][1])
         if kind == "c":
@@ -162,420 +170,381 @@ def rank_program(g, core, T, topo):
     if rank is None:
         return
     n = len(T.cores)
-    ops = []
-
-    def op(e, fn, r, w, kind="c"):
-        ops.append((e, fn, r.split(), w.split(), kind))
-
-    def tt(out, a, b, o, r, w):
-        op("V", lambda q: q.tensor_tensor(out, a, b, o), r, w)
-
-    def ts(out, a, s1, o0, r, w, s2=None, o1=None):
-        if o1 is None:
-            op("V", lambda q: q.tensor_scalar(out, a, s1, None, o0), r, w)
-        else:
-            op("V", lambda q: q.tensor_scalar(out, a, s1, s2, o0, o1), r, w)
-
-    def cp(out, a, r, w):
-        op("V", lambda q: q.tensor_copy(out, a), r, w)
-
-    def scan(out, d0, d1, o0, o1, r, w):
-        op("V", lambda q: q.tensor_tensor_scan(out, d0, d1, 0.0, o0, o1), r, w)
-
-    def ms(ap, c, w):
-        op("V", lambda q: q.memset(ap, c), "", w)
-
-    def act(out, a, r, w, f=ACT.Identity, bias=0.0, scale=1.0, acc=None):
-        op("S", lambda q: q.activation(out, a, f, bias=bias, scale=scale, accum_out=acc), r, w)
-
-    def mm(out, l, rh, st, sp, r, w):
-        op("T", lambda q: q.matmul(out, l, rh, st, sp), r, w + " bank" + w[1])
-
-    def dma(e, out, a, r, w):
-        op(e, lambda q: q.dma_start(out, a), r, w, "d")
-
-    def iota(out, pat, base, cm, w, fl=True):
-        if fl:
-            op("G", lambda q: q.iota(out, pat, base, cm, allow_small_or_imprecise_dtypes=True), "", w)
-        else:
-            op("G", lambda q: q.iota(out, pat, base, cm), "", w)
-
-    def weave(*chains):
-        chains = [list(c) for c in chains]
-        while any(chains):
-            for c in chains:
-                if c:
-                    c.pop(0)()
-
+    ops, after = [], []
     A = ALU
-    col = lambda i: T.COL[:, i:i + 1]
-    PR, PG, ZC, RVC, MI, EN, SG, PAR, R0, R0N, R1A, R1B, E1, E2, HALF = [col(i) for i in range(15)]
-    XW, BW = T.XT[:], T.B[:]
-    XK = "X Xc Xt"
-    BK = "B B1 B2 B3 Bt"
-    c16 = T.LIN[:, 0:16]
-    I1, IH, IB, INB = [T.IV[:, 128 * i:128 * i + 128] for i in range(4)]
-    M1, M3, MD, M2, M4 = [T.MM[:, 256 * i:256 * i + 256] for i in range(5)]
-    BO1, BOX, BON = T.BO[:, 0:128], T.BO[:, 128:256], T.BO[:, 256:384]
-    PQ = [T.P0, T.P1]
 
-    ms(T.LN[:], 0, "LNz")
-    dma("S", T.KI[:], T.kt[:], "", "KI")
-    dma("Y", T.LN[0::16, 0:256], T.lc[:], "LNz", "LN")
-    dma("Y", T.LN[0::16, 256:512], T.lv[:], "LNz", "LN1")
-    dma("Y", T.LN[0::16, 512:768], T.ld[:], "LNz", "LN2")
-    dma("Y", T.XT[:, 0:2048], T.x[:, 0:2048], "", "X0")
-    dma("Y", T.XT[:, 2048:4096], T.x[:, 2048:4096], "", "X")
-    dma("Y", T.BI[:, 0:1024], T.bnd[:, 0:1024], "", "BI0")
-    dma("Y", T.BI[:, 1024:2048], T.bnd[:, 1024:2048], "", "BI1")
+    def ap(x):
+        if not isinstance(x, tuple):
+            return x
+        if x[0] == "*":
+            return ap(x[1]).indirect(ap(x[2]))
+        return T[x[0]][x[4][0]:x[4][1]:x[4][2], x[1]:x[2]:x[3]]
 
-    iota(T.PI[:, 0:1], [[0, 1]], 0, 1, "PI0", False)
-    iota(T.JF[:], [[1, 256]], 0, 0, "JF")
-    iota(T.CG[:], [[1, 8], [0, 16]], 0, 0, "CG")
-    iota(T.DI[:], [[1, 128]], 0, -1, "DI")
-    iota(T.SI[:], [[0, 16], [1, 16]], 0, 0, "SI")
-    iota(T.SR[:], [[0, 17], [-1, 16]], 15, 0, "SR")
-    iota(T.TI[:], [[0, 4], [16, 4]], 0, 0, "TI")
+    def ind(win, off):
+        return ("*", win, off)
+
+    def op(e, fn, out, ins, per, kind="c"):
+        ins = [x for x in ins if isinstance(x, tuple)]
+        rd = [y for x in ins for y in (x[1:] if x[0] == "*" else [x])] + [x[2] for x in out if x[0] == "*"]
+        wr = [x[1] if x[0] == "*" else x for x in out]
+        if kind == "c" and e in "VS":
+            per = 3.8 if out[0][0] == "*" else 1.56 if any(x[0] == "*" for x in ins) else per
+            per = 50 + 0.83 * max(size(out[0]) * per, 64 if e == "V" else 0)
+        ops.append((e, fn, rd, wr, kind, per))
+
+    def half(*xs):
+        return 0.5 if all(x[0] in SB and SB[x[0]][1] in (BF, F16, U16) for x in xs) else 1
+
+    def tt(out, a, b, o):
+        op("V", lambda q: q.tensor_tensor(ap(out), ap(a), ap(b), o), [out], [a, b], 1 if _banks(a) + _banks(b) else 2)
+
+    def ts(out, a, s1, o0, s2=None, o1=None):
+        if o1 is None:
+            op("V", lambda q: q.tensor_scalar(ap(out), ap(a), ap(s1), None, o0), [out], [a, s1], half(out, a))
+        else:
+            op("V", lambda q: q.tensor_scalar(ap(out), ap(a), ap(s1), ap(s2), o0, o1), [out], [a, s1, s2], half(out, a))
+
+    def cp(out, a):
+        op("V", lambda q: q.tensor_copy(ap(out), ap(a)), [out], [a], half(out, a))
+
+    def scan(out, d0, d1, o0, o1):
+        op("V", lambda q: q.tensor_tensor_scan(ap(out), ap(d0), ap(d1), 0.0, o0, o1), [out], [d0, d1], half(out, d0, d1))
+
+    def ms(out, c):
+        op("V", lambda q: q.memset(ap(out), c), [out], [], half(out))
+
+    def act(out, a, f=ACT.Identity, bias=0.0, scale=1.0, acc=None):
+        op("S", lambda q: q.activation(ap(out), ap(a), f, bias=ap(bias), scale=ap(scale), accum_out=ap(acc)), [out] + ([acc] if acc else []), [a, bias, scale], 1)
+
+    def mm(out, l, rh, st, sp):
+        c = max(min(64, size(l)), size(rh)) * (4 if SB[l[0]][1] == F32 else 1)
+        op("T", lambda q: q.matmul(ap(out), ap(l), ap(rh), st, sp), [out], [l, rh], 0.5 * c)
+
+    def dma(e, out, a, wr, rd, nbytes):
+        op(e, lambda q: q.dma_start(ap(out), ap(a)), wr, rd, 2000 + nbytes / 190.0, "d")
+
+    def iota(out, pat, base=0, cm=0):
+        if SB[out[0]][1] == I32:
+            op("G", lambda q: q.iota(ap(out), pat, base, cm), [out], [], 130 + 1.66 * size(out))
+        else:
+            op("G", lambda q: q.iota(ap(out), pat, base, cm, allow_small_or_imprecise_dtypes=True), [out], [], 130 + 1.66 * size(out))
+
+    col = lambda i: r("COL", i, i + 1)
+    PR, PG, PP, P63, ZC, RVC, EVN, ODD, RHO, XB, BB, BB1, BBH, SQ, CA, CK, E1, E2, EN, MI, PX, XBH = [col(i) for i in range(22)]
+    eq = lambda i: r("EQ", i, i + 1)
+    bo = lambda i, k=1: r("BO", 128 * i, 128 * (i + k))
+    BO1, BOH, BOU, BOE, BOO, BOD, BODN, BOP, BO8, WM, WB1, WB2, WAC, WGA, WG2 = [bo(i) for i in range(15)]
+    s8 = lambda x: sub(x, 0, 128, 16)
+    I1, IQ, IH, PRV = [r("IV", 128 * i, 128 * i + 128) for i in range(4)]
+    ZH = lambda i, k: r("ZH", 144 * i + 15 - k, 144 * i + 143 - k)
+    lt = lambda q: r("LT", q, 256, 16)
+    XW, BW, G, MC, ME = r("XT"), r("B"), r("G"), r("MM", 0, 256), r("MM", 256, 512)
+    hf = lambda x, h: sub(x, 128 * h, 128 * h + 128)
+    row0 = (0, 128, 16)
+    MB = 1 << 20
+
+    ms(r("LN"), 0)
+    loads = [(r("LN", 256 * i, 256 * i + 256, 1, row0), x[:], r("LN", 256 * i, 256 * i + 256), 0) for i, x in ((1, T.lv), (2, T.ld), (0, T.lc))]
+    loads += [(r("BI"), T.bnd[:], r("BI"), MB), (r("XT", 0, 4096), T.x[:], r("XT", 0, 4096), 2 * MB), (r("KI", 0, 1024), T.kt[:], r("KI", 0, 1024), 2.5 * MB)]
+    loads += [(r("KI", 1024, 2048, 1, (u, 128, 2)), T.kt[1 - u::2, :], r("KI", 1024 + 512 * u, 1536 + 512 * u), 3 * MB) for u in range(2)]
+    for i, (out, a, wr, nbytes) in enumerate(loads):
+        dma("Y", out, a, [wr], [], nbytes)
+        if i:
+            after.append((len(ops) - 1, len(ops) - 2))
+
+    iota(r("PI", 0, 1), [[0, 1]], 0, 1)
+    iota(r("JF"), [[1, 256]])
+    iota(r("CG"), [[1, 8], [0, 16]])
+    iota(r("REP"), [[1, 64], [0, 16]])
+    iota(r("SI"), [[0, 8], [1, 16]])
+    iota(r("SR"), [[0, 17], [-1, 16]], 15)
     for mi in range(4):
-        iota(T.SD[:, SEG[mi]:SEG[mi + 1]], [[0, 4], [1, 64 - 16 * mi]], 0, 0, "SJ%d" % mi)
-    ts(T.PI[:, 1:2], T.PI[:, 0:1], 15, A.bitwise_and, "PI0", "PI1")
-    ts(T.PI[:, 2:3], T.PI[:, 0:1], 4, A.arith_shift_right, "PI0", "PI2")
-    ts(T.PI[:, 3:4], T.PI[:, 0:1], 1, A.bitwise_and, "PI0", "PI3")
-    ts(T.PI[:, 4:5], T.PI[:, 0:1], 3, A.bitwise_and, "PI0", "PI4")
-    ts(T.PI[:, 5:6], T.PI[:, 0:1], 2, A.arith_shift_right, "PI0", "PI5", 3, A.bitwise_and)
-    cp(T.COL[:, 0:2], T.PI[:, 1:3], "PI1 PI2", "C0")
-    ts(ZC, T.PI[:, 2:3], 16.0, A.mult, "PI2", "C2_", 15.0, A.add)
-    ts(RVC, T.PI[:, 1:2], -1.0, A.mult, "PI1", "C3", 255.0, A.add)
-    ts(R0, T.PI[:, 1:2], 0.0, A.is_equal, "PI1", "C8")
-    ts(R0N, T.PI[:, 1:2], 0.0, A.is_equal, "PI1", "C9", -2048.0, A.mult)
-    ts(SG, T.PI[:, 3:4], -2.0, A.mult, "PI3", "C6", 1.0, A.add)
-    cp(PAR, T.PI[:, 3:4], "PI3", "C7")
-    ts(R1A, T.PI[:, 1:2], 1.0, A.is_equal, "PI1", "C10_", -2.0 ** 27, A.mult)
-    ts(R1B, T.PI[:, 1:2], 1.0, A.is_equal, "PI1", "C11", -float(XO), A.mult)
-    cp(MI, T.PI[:, 4:5], "PI4", "C4")
-    ts(E1, T.PI[:, 4:5], -32.0, A.mult, "PI4", "C12", 288.0, A.add)
-    ts(E2, T.PI[:, 4:5], -16.0, A.mult, "PI4", "C15", 64.0, A.add)
-    ts(EN, T.PI[:, 5:6], 1.0, A.add, "PI5 C15", "C16", E2, A.mult)
-    ts(E2, EN, -1.0, A.add, "C16", "C13 C15")
-    ts(T.REV[:], T.JF[:, 0:16], -16.0, A.mult, "JF C3", "REV", RVC, A.add)
-    ts(T.ZH[:], T.JF[:, 0:144], ZC, A.is_equal, "JF C2_", "ZH")
-    ts(T.ENDS[:, 0:1], E1, MI, A.mult, "C12 C4 C13", "ENDS", E2, A.add)
-    ts(T.S8H[:], T.JF[:, 0:8], PG, A.is_equal, "JF C0", "S8H")
-    ts(T.S8F[:], T.JF[:, 0:8], PG, A.is_equal, "JF C0", "S8F")
-    cp(T.LIN[:], T.JF[:], "JF", "LIN")
-    ts(T.LAST[:], T.JF[:, 0:8], 16.0, A.mult, "JF", "LAST", 15.0, A.add)
-    ts(BO1, T.CG[:], PG, A.is_equal, "CG C0", "BO")
-    ts(BOX, T.CG[:], PG, A.is_equal, "CG C0", "BO4", float(XO), A.mult)
-    ts(T.WD[:, 0:128], T.CG[:], PG, A.is_equal, "CG C0 C10_", "WD0", R1A, A.mult)
-    ts(T.WD[:, 128:256], T.CG[:], PG, A.is_equal, "CG C0 C11", "WD1", R1B, A.mult)
-    for i, s in enumerate((1.0, 0.5, 1024.0, -1024.0)):
-        ts(T.IV[:, 128 * i:128 * i + 128], T.DI[:], 0.0, A.is_equal, "DI", "IV%d" % i, s, A.mult)
-    ts(T.IF[:], T.DI[:], 0.0, A.is_equal, "DI", "IF")
-    ts(M1, T.LN[:, 0:256].indirect(T.REV[:]), R0N, A.add, "LN LN1 LN2 C9 REV", "M1")
-    ts(M3, T.LN[:, 256:512].indirect(T.REV[:]), 2.0, A.mult, "LN LN1 LN2 REV", "M3")
-    ts(MD, T.LN[:, 512:768].indirect(T.REV[:]), -1.0, A.mult, "LN LN1 LN2 C8 REV", "MD", R0, A.add)
-    ts(T.BNB[:], T.SR[:], PR, A.not_equal, "SR C0", "BNB", -BIG, A.mult)
-    ms(T.XT[:, 4096:XO], 0.0, "Xt0")
-    ms(T.XT[:, XO + 4096:2 * XO], 0.0, "Xt")
-    act(T.XT[:, XO:XO + 2048], T.XT[:, 0:2048], "X0 Xt0", "Xc0", bias=255.0, scale=-1.0)
+        iota(r("SJ", SEG[mi], SEG[mi + 1]), [[0, 4], [1, 64 - 16 * mi]])
+        iota(r("SM", SEG[mi], SEG[mi + 1]), [[4, 4], [0, 64 - 16 * mi]], mi)
+    iota(r("IDUP"), [[16, 8], [0, 2], [1, 16]])
+    iota(r("RH"), [[0, 8], [-2, 8], [0, 2]])
+    iota(r("CI0"), [[32, 16], [0, 2], [2, 16]])
+    pi = lambda i: r("PI", i, i + 1)
+    ts(pi(1), pi(0), 15, A.bitwise_and)
+    ts(pi(2), pi(0), 4, A.arith_shift_right)
+    ts(pi(3), pi(0), 63, A.bitwise_and)
+    ts(pi(4), pi(0), 1, A.bitwise_and)
+    ts(pi(5), pi(0), 3, A.bitwise_and)
+    ts(pi(6), pi(0), 2, A.arith_shift_right, 3, A.bitwise_and)
+    ts(pi(7), pi(0), 16, A.bitwise_and)
+    act(r("COL", 0, 2), r("PI", 1, 3))
+    act(PP, pi(0))
+    act(P63, pi(3))
+    act(ZC, PG, bias=15.0, scale=16.0)
+    act(RVC, PR, bias=255.0, scale=-1.0)
+    act(ODD, pi(4))
+    act(EVN, ODD, bias=1.0, scale=-1.0)
+    act(XB, PR, bias=4096.0 + 48)
+    act(XBH, PR, bias=2048.0 + 24, scale=0.5)
+    act(BB, PR, bias=2048.0 + 48)
+    act(BBH, PR, bias=1024.0 + 24, scale=0.5)
+    act(BB1, PR, bias=1024.0 + 23.5, scale=0.5)
+    ts(r("EQ"), r("JF", 0, 16), PR, A.is_equal)
+    ts(r("REV"), r("JF", 0, 16), -16.0, A.mult, RVC, A.add)
+    ts(r("ZH", 432, 576), r("JF", 0, 144), ZC, A.is_equal)
+    ts(r("ZH", 0, 144), r("ZH", 432, 576), EVN, A.mult)
+    ts(r("ZH", 144, 288), r("ZH", 432, 576), ODD, A.mult)
+    ts(r("ZH", 288, 432), r("ZH", 432, 576), eq(QD), A.mult, -0.5, A.mult)
+    ts(BO1, r("CG"), PG, A.is_equal)
+    ts(I1, r("JF", 0, 128), PP, A.is_equal)
+    ts(CK, eq(0), -2048.0, A.mult)
+    ts(MC, ind(r("LN", 0, 256), r("REV")), CK, A.add)
+    cp(ME, ind(r("LN", 256, 512), r("REV")))
+    ts(G, ind(r("LN", 512, 768), r("REV")), eq(Q1), A.add)
+    for x, c, w in ((BOH, -0.5, None), (BOU, -2.0 ** -13, None), (BOE, EVN, None), (BOO, ODD, None), (BOD, eq(QD), 0.5), (BODN, eq(QD), -0.5),
+                    (BOP, eq(QP), None), (BO8, eq(QD), 0.125), (WB1, eq(Q1), 8192.0), (WB2, eq(Q1), 2.0 ** -14), (WAC, eq(QM), -1.0 / 16)):
+        ts(x, BO1, c, A.mult, w, w and A.mult)
+    ts(CA, eq(Q1), -17.0 / 32, A.mult, eq(QD), A.add)
+    ts(WGA, BO1, CA, A.mult)
+    ts(WG2, BO1, CA, A.mult)
+    ts(r("S8"), s8(BOD), 2048.0, A.mult)
+    for i, w in enumerate((-1.0, -1.0, 0.5, 2.0 ** -13)):
+        act(r("W3", 8 * i, 8 * i + 8), s8(BO1), scale=w)
+    act(IQ, I1, scale=-0.25)
+    act(IH, I1, scale=0.5)
+    act(r("IF"), I1, scale=2.0 ** -12)
+    ts(PX, pi(1), -2.0, A.mult, PP, A.add)
+    act(PX, PX, bias=15.0)
+    ts(PRV, r("JF", 0, 128), PX, A.is_equal, 2.0 ** -25, A.mult)
+    ts(r("REP"), r("REP"), P63, A.is_equal)
+    ms(r("XT", 4096, 4160), 0.0)
+    ms(r("B", 2048, 2112), 0.0)
+    ms(r("ON"), 1.0)
+    ms(r("ZE"), 0.0)
+    ms(r("WA"), 0.0)
+    act(r("LT"), r("JF"), scale=0.0)
+    act(lt(Q1), r("ON", 0, 16))
+    ms(r("CZ", 0, 512, 2), -31.5 / 128)
+    ms(r("CZ", 1, 512, 2), 63.5 / 128)
+    ts(r("RSB"), r("SI"), 0.0, A.is_equal, 2.0 ** 20, A.mult)
+    ts(r("BNB"), r("SR"), PR, A.not_equal, -BIG, A.mult)
+    ts(r("BM"), r("SR"), PR, A.is_equal, BIG, A.mult)
+    ts(r("MK"), r("SJ"), PR, A.is_le, 2.0 ** 30, A.mult)
+    for mi in range(3):
+        ms(r("MK", SEG[mi] + 63 - 16 * mi, SEG[mi + 1], 64 - 16 * mi), 8.0 * (3 - mi))
+    ts(r("REPT"), r("SM"), PP, A.is_equal, -1.0, A.mult)
+    act(MI, pi(5))
+    act(E1, MI, bias=288.0, scale=-32.0)
+    act(E2, MI, bias=64.0, scale=-16.0)
+    ts(EN, pi(6), 1.0, A.add, E2, A.mult)
+    act(EN, EN, bias=-1.0)
+    ts(r("ENDS", 0, 1), E1, MI, A.mult, EN, A.add)
+    ts(SQ, pi(1), 32.0, A.mult)
+    tt(SQ, SQ, pi(7), A.add)
+    ts(r("SELQ"), r("JF", 0, 8), SQ, A.add)
+    ts(r("IDUP"), r("IDUP"), PP, A.is_equal)
+    ts(r("RH"), r("RH"), eq(QA), A.mult, eq(QA2), A.add)
+    tt(WM, r("RH"), BO1, A.mult)
+    tt(RHO, PR, ODD, A.subtract)
+    act(RHO, RHO, ACT.Square, scale=0.5)
+    act(RHO, RHO, bias=1.0, scale=-1.0)
+    ts(E2, eq(QE), eq(QP), A.add, 2048.0, A.mult)
+    ts(r("CIN"), r("CI0"), eq(QM), A.mult, E2, A.add)
+    ts(r("KA"), r("KI"), 1023, A.bitwise_and)
+    act(r("KI"), r("KI"), bias=-2048.0)
+    act(r("B", 0, 2048), r("BI"))
 
-    def wbatch():
-        for r in range(16):
-            mm(T.P4[:, 0:48], T.ZH[:, 15 - r:143 - r], T.MM[:, r:768:16], r == 0, r == 15, "ZH M1 M3 MD", "P4:w")
+    def rivals(k, pk, tw, terms, neg, base, out):
+        p16 = (0, 16, 1)
+        mm(sub(tw, 0, 128), r("ZE", 0, 16), r("ZE"), True, False)
+        for j, (src, w) in enumerate(terms):
+            for i in range(16):
+                mm(sub(tw, i, 128, 16), sub(src, i, 256, 16), s8(w), False, j == len(terms) - 1 and i == 15)
+        own = r("TW", 128 * k, 128 * k + 128, 1, p16)
+        act(own, tw)
+        for bk in range(2):
+            lo, hi = 512 * bk, min(640, 512 * bk + 512)
+            parts = [(0, 0, 256)] + [(SEG[mi] + b * (64 - 16 * mi), 64 * b + 16 * mi, 64 - 16 * mi) for mi in (1, 2, 3) for b in range(4)]
+            parts = [x for x in parts if lo <= x[0] < hi]
+            for j, (src, w) in enumerate(terms):
+                if j == 0:
+                    mm(bank(pk, lo, hi), r("ZE"), r("CZ", 0, hi - lo), True, False)
+                for a, c, ln in parts:
+                    mm(bank(pk, a, a + ln), w, sub(src, c, c + ln), False, False)
+            mm(bank(pk, lo, hi), own, r("REPT", lo, hi, 1, p16), False, True)
+        ab, sc, wn = r("AB", 640 * k, 640 * k + 640), r("SC", 640 * k, 640 * k + 640), r("WN", 16 * k, 16 * k + 16)
+        act(ab, bank(pk, 0, 640), ACT.Abs, scale=BIG)
+        scan(sc, ab, r("MK"), A.min, A.max)
+        tt(wn, ind(sc, r("ENDS", 0, 1)), neg, A.min)
+        ts(out, wn, -2.0, A.mult, base, A.add)
 
-    def wbatch_s():
-        act(T.WS[:, 32:48], T.P4[:, 32:48], "P4:w", "WS2", bias=2048.0 + XO, scale=-float(XO))
-        act(T.WS[:, 0:16], T.P4[:, 32:48], "P4:w", "WS0")
-        act(T.WS[:, 16:32], T.P4[:, 32:48], "P4:w", "WS1", bias=1.0, scale=-1.0)
-
-    def lanes_w():
-        return [
-            lambda: tt(T.CPF[:], T.P4[:, 0:16], T.WS[:, 32:48], A.add, "P4:w WS2", "CPF"),
-            lambda: ts(T.CI[:, 0:16], T.P4[:, 0:16], 2048.0, A.add, "P4:w", "CI0"),
-            lambda: tt(T.CR[:], T.P4[:, 16:32], T.WS[:, 0:16], A.add, "P4:w WS0", "CR"),
-            lambda: tt(T.CO[:, 0:16], T.P4[:, 16:32], T.WS[:, 16:32], A.add, "P4:w WS1", "CO0"),
-            lambda: cp(T.CPU[:], T.CPF[:], "CPF", "CPU"),
-            lambda: ts(T.CI[:, 16:32], T.CI[:, 0:16], 1023, A.bitwise_and, "CI0", "CI1"),
-            lambda: cp(T.CU[:], T.CI[:, 0:16], "CI0", "CU"),
-            lambda: cp(T.CRU[:], T.CR[:], "CR", "CRU"),
-            lambda: cp(T.C10[:], T.CI[:, 16:32], "CI1", "C10")]
-
-    def distances(ab, rows, w, rk, wk):
-        for m in range(16):
-            b, mi = m // 4, m % 4
-            st = SEG[mi] + b * (64 - 16 * mi)
-            act(ab[:, st:st + 64 - 16 * mi], rows[:, 16 * m:64 * b + 64], rk, "%s%d" % (wk, m), f=ACT.Abs, bias=w(m), scale=-1.0)
-
-    def rivals(sc, ab, u, tr, neg, out, k, rk, wk):
-        return [lambda: scan(sc[:], ab[:], T.MK[:], A.min, A.max, "MK " + " ".join("%s%d" % (k, m) for m in range(16)), k + "s"),
-                lambda: tt(u, sc[:].indirect(T.ENDS[:, 0:1]), tr[:], A.subtract, "ENDS TR " + k + "s", k + "u"),
-                lambda: tt(out, u, neg, A.min, k + "u " + rk, wk)]
-
-    def lanes_pe(t):
+    def append(t, oc, old, val):
         o = (-5 * t) % 16
-        mm(T.P3[:, 256:512], BO1, MD, True, True, "BO MD", "P3:d")
+        tt(old, ind(BW, oc), r("BM", o, o + 256), A.subtract)
+        for b in range(4):
+            tt(ind(BW, sub(oc, 4 * b, 4 * b + 4)), sub(old, 64 * b, 64 * b + 64), sub(val, 64 * b, 64 * b + 64), A.max)
+
+    def masked(t, ps, w, out):
+        o = (-5 * t) % 16
+        mm(ps, I1, r("BNB", o, o + 256), True, False)
+        mm(ps, w, MC, False, True)
+        act(out, ps, bias=2048.0)
+
+    def lanes(t, dw):
+        for i in range(16):
+            mm(bank(6, 256, 288), ZH(0, i), r("MM", i, 512, 16), i == 0, False)
+        for i in range(16):
+            mm(bank(6, 272, 288), ZH(2, i), sub(G, i, 256, 16), False, i == 15)
         for h in range(2):
-            mm(T.P3[:, 8 * h:8 * h + 8], T.MM[:, 128 * h:128 * h + 128], T.S8H[:], True, True, "M1 S8H", "P3:p")
-        mm(T.P5[:, 256:512], BO1, M3, True, False, "BO M3", "P5:o")
-        mm(T.P5[:, 256:512], BO1, MD, False, True, "BO MD", "P5:o")
-        mm(T.P5[:, 0:256], I1, T.BNB[:, o:o + 256], True, False, "IV0 BNB", "P5:v")
-        if t < ST - 1:
-            mm(T.P5[:, 0:256], BOX, MD, False, False, "BO4 MD", "P5:v")
-        mm(T.P5[:, 0:256], BO1, M1, False, True, "BO M1", "P5:v")
-
-    def lanes_s0():
-        act(T.DX[:], T.P3[:, 256:512], "P3:d C6 C7", "DX", bias=PAR, scale=SG)
-        act(T.CL[:], T.P3[:, 0:16], "P3:p", "CL")
-
-    def lanes_s():
-        act(T.VO[:], T.P5[:, 0:256], "P5:v", "VO", bias=2048.0)
-        act(T.CO[:, 16:32], T.CO[:, 0:16], "CO0", "CO1", scale=-1.0 / BIG)
-        distances(T.ABO, T.P5[:, 256:512], lambda m: T.CR[:, m:m + 1], "P5:o CR", "ABO")
-
-    def own_rivals():
-        return rivals(T.SCO, T.ABO, T.UO[:, 0:16], T.TRB, T.CO[:, 16:32], T.UO[:, 16:32], "ABO", "CO1", "UO") + [
-            lambda: ts(T.OC[:], T.UO[:, 16:32], -BIG, A.mult, "UO", "OC")]
-
-    def shapes_of_lanes():
-        act(T.QC[:], XW.indirect(T.CPU[:]), XK + " CPU", "QC")
+            mm(bank(6, 288 + 8 * h, 296 + 8 * h), hf(MC, h), s8(BOE), True, True)
+            mm(bank(6, 304 + 8 * h, 312 + 8 * h), hf(G, h), r("S8"), True, True)
+        act(r("CU"), bank(6, 256, 272), bias=2048.0)
+        act(r("CRU"), bank(6, 272, 288), bias=1.0, scale=2.0)
+        act(r("CL", 0, 16), bank(6, 288, 304), bias=2048.0)
+        act(r("CL", 16, 32), bank(6, 304, 320))
+        tt(r("NG", 0, 16), dw, bank(6, 272, 288), A.subtract)
+        ts(r("C10"), r("CL", 0, 16), 1023, A.bitwise_and)
+        act(r("QC"), ind(XW, r("CU")), bias=-127.5)
         for h in range(2):
-            for k in range(16):
-                act(T.QQ[:, 2048 * h + k:2048 * h + 2048:16], T.QC[:, 128 * h:128 * h + 128], "QC", "QQ%d_%d" % (h, k))
+            mm(bank(4, 128 * h, 128 * h + 128), hf(r("QC"), h), I1, True, False)
+            mm(bank(4, 128 * h, 128 * h + 128), hf(G, h), BO8, False, True)
+        act(r("QCT"), bank(4, 0, 256), bias=-1.0 / 16)
+        masked(t, bank(5, 0, 256), BOE, r("VO"))
+        rivals(0, 0, bank(6, 384, 512, 1, (0, 16, 1)), [(G, BOD), (ME, BOE)], r("NG", 0, 16), BB, r("OC"))
 
-    def remote(out, in_, sem, dst, src, r, w, landed):
+    def remote(out, in_, sem, dst, src):
         rid, pid, _ = topo.addr(dst)
-        op("G", lambda q: q.remote_dma(out, in_, T.sem[sem], T.sem.sent, pid, rid, topo.mask(core, dst)), r, w,
+        tok = ("tok" + sem, 0, 1, 1, (0, 1, 1))
+        op("G", lambda q: q.remote_dma(ap(out), ap(in_), T.sem[sem], T.sem.sent, pid, rid, topo.mask(core, dst)), [tok, ("sends", 0, 1, 1, (0, 1, 1))], [in_], 300,
            ("send", len(topo.engines(core, dst))))
-        op("G", None, w, landed, ("arrive", sem, len(topo.engines(src, core))))
+        op("A", None, [out], [tok], 1800 + size(out) * 8, ("arrive", sem, len(topo.engines(src, core))))
 
-    def append(t, oc, old, val, ok, rk, vk):
-        o = (-5 * t) % 16
-        return [lambda: tt(old[:], BW.indirect(oc[:]), T.BM[:, o:o + 256], A.subtract, BK + " BM " + rk, ok)] + [
-            (lambda b=b: tt(BW.indirect(oc[:, 4 * b:4 * b + 4]), old[:, 64 * b:64 * b + 64], val[:, 64 * b:64 * b + 64], A.max,
-                            ok + " " + rk + " " + vk, "B")) for b in range(4)]
-
-    wbatch()
-    wbatch_s()
-    lanes_pe(0)
-    ms(T.ON[:], 1.0 / 128, "ON")
-    ms(T.CQ[:, 128:256], 2.0 ** 26, "CQ1")
-    ms(T.CQ[:, 256:384], 2.0 ** 25, "CQ2")
-    ms(T.CQ[:, 512:640], -64.0, "CQ4")
-    ms(T.DL[:], 60.0, "DL")
-    ms(T.B[:, 2048:2112], 0.0, "Bt")
-    ms(HALF, 0.5, "C14")
-    for c in range(2):
-        if c not in S_CHUNKS and S_CHUNKS:
-            ms(T.GD[:, 1024 * c:1024 * c + 1024], 1.0, "GD%d" % c)
-    weave(lanes_w())
-    lanes_s0()
-    for i, s in enumerate((8192.0, -4096.0, -8192.0, -4096.0, 4.0)):
-        ts(T.W3[:, 8 * i:8 * i + 8], T.S8F[:], s, A.mult, "S8F", "W3%d" % i)
-    ts(T.CQ[:, 0:128], T.SI[:, 0:128], 256.0, A.mult, "SI", "CQ0")
-    ts(T.CQ[:, 384:512], T.SI[:, 0:128], -256.0, A.mult, "SI", "CQ3")
-    ts(T.MS[:], T.SI[:], PR, A.is_equal, "SI C0", "MS")
-    ts(T.ND[:], T.SI[:], PR, A.not_equal, "SI C0", "ND", BIG, A.mult)
-    ts(T.BM[:], T.SR[:], PR, A.is_equal, "SR C0", "BM", BIG, A.mult)
-    ts(BON, T.CG[:], PG, A.is_equal, "CG C0", "BO5", -float(XO), A.mult)
-    ts(T.RSB[:], T.SI[:], 0.0, A.is_equal, "SI", "RSB", 2.0 ** 28, A.mult)
-    ts(T.RS0[:], T.SI[:, 0:128], 1.0, A.min, "SI", "RS0")
-    ts(T.MK[:], T.SD[:, 0:640], PR, A.is_le, "SJ0 SJ1 SJ2 SJ3 C0", "MK SD0", BIG, A.mult)
-    ts(T.TRX[:], T.TI[:], PR, A.add, "TI C0", "TRa", 1.0 / BIG, A.mult)
-    cp(T.KF[:], T.KI[:], "KI", "KF")
-    ts(T.TRB[:], T.TRX[:], 2048.0 / BIG, A.add, "TRa", "TR")
-    ts(T.KA[:], T.KI[:], 1023, A.bitwise_and, "KI", "KA")
-    ts(T.TRX[:], T.TRX[:], 4096.0 / BIG, A.add, "TRa", "TRa TR")
-    ts(T.KV[:], T.KA[:], 2.0, A.mult, "KA", "KV")
-    act(T.XT[:, XO + 2048:XO + 4096], T.XT[:, 2048:4096], "X Xc0", "Xc", bias=255.0, scale=-1.0)
-    shapes_of_lanes()
-    ts(T.B[:, 0:1024:2], T.BI[:, 0:1024:2], float(XO), A.add, "BI0", "B2")
-    cp(T.B[:, 1:1024:2], T.BI[:, 1:1024:2], "BI0", "B1")
-    ts(T.B[:, 1024:2048:2], T.BI[:, 1024:2048:2], float(XO), A.add, "BI1", "B")
-    cp(T.B[:, 1025:2048:2], T.BI[:, 1025:2048:2], "BI1", "B3")
+    for i in range(16):
+        mm(bank(7, 0, 16), ZH(2, i), sub(G, i, 256, 16), i == 0, i == 15)
+    act(r("DW", 0, 16), bank(7, 0, 16), bias=BBH, scale=2.0)
+    lanes(0, r("DW", 0, 16))
 
     for t in range(ST):
         last = t == ST - 1
-        o = (-5 * t) % 16
-        sa = slice(16 * t, 16 * t + 16)
-        sk, lk = "snd%d" % t, "lnd%d" % t
-        cp(T.EU[:], BW.indirect(T.CRU[:]), BK + " CRU", "EU")
-        act(T.EF[:], BW.indirect(T.CRU[:]), BK + " CRU", "EF")
+        bw = r("BI") if t == 0 else BW
+        cp(r("EU"), ind(bw, r("CRU")))
+        act(r("EF"), ind(bw, r("CRU")), bias=-2048.0)
         for h in range(2):
-            k = "P%d:q" % h
-            mm(PQ[h][:], T.ON[:], T.CQ[:, 0:512], True, False, "ON CQ0 CQ1 CQ2 CQ3", k)
-            mm(PQ[h][:, 256:512], T.DX[:, 128 * h:128 * h + 128], T.WD[:], False, False, "DX WD0 WD1", k)
-        if S_CHUNKS:
-            mm(PQ[0][:, 0:128], T.ON[:], T.CQ[:, 512:640], False, False, "ON CQ4", "P0:q")
-        for h in range(2):
-            mm(PQ[h][:, 384:512], T.EF[:, 128 * h:128 * h + 128], T.IF[:], False, False, "EF IF", "P%d:q" % h)
-        if t:
-            act(T.DL[:], T.PF[:].indirect(T.LIN[:, 0:8]), "PF LIN", "DL", bias=60.0, scale=-8.0)
-        for h in range(2):
-            mm(PQ[h][:, 0:128], T.ON[:], T.DL[:], False, False, "ON DL", "P%d:q" % h)
-        if last:
-            act(T.B[:, 0:2048:2], T.B[:, 0:2048:2], BK, "B", bias=-float(XO))
-        for c in range(4):
-            sl = slice(1024 * c, 1024 * c + 1024)
-            tt(T.SD[:, sl], XW.indirect(T.EU[:, 64 * c:64 * c + 64]), T.QQ[:, sl], A.subtract,
-               XK + " EU " + " ".join("QQ%d_%d" % (c // 2, k) for k in range(16)), "SD%d" % c)
-            if c in S_CHUNKS:
-                act(T.HD[:, sl], T.SD[:, sl], "SD%d" % c, "HD%d" % c, f=ACT.Relu)
-                act(T.GD[:, sl], T.SD[:, sl], "SD%d C14" % c, "GD%d" % c, f=ACT.Sign, bias=HALF)
-            for j in ([c - 1] if c > 0 and c - 1 not in S_CHUNKS else []) + ([c] if c == 3 else []):
-                ts(T.HD[:, 1024 * j:1024 * j + 1024], T.SD[:, 1024 * j:1024 * j + 1024], -2.0 ** -10, A.max, "SD%d" % j, "HD%d" % j)
-            if c % 2:
-                h = c // 2
+            mm(bank(2 * h, 0, 256), hf(G, h), bo(13, 2), True, False)
+            for s in range(2):
+                mm(bank(2 * h, 128 * s, 128 * s + 128), hf(r("QC"), h), BO1, False, False)
+            mm(bank(2 * h, 128, 256), r("ON"), r("WA"), False, False)
+            mm(bank(2 * h + 1, 0, 256), hf(r("QC"), h), bo(0, 2), True, False)
+            mm(bank(2 * h + 1, 128, 256), hf(G, h), WB1, False, False)
+        qy = lambda h: bank(7 - 2 * h, 0, 128)
+        for c, (a, b, e) in enumerate(CHUNKS):
+            ring = 4 + 2 * (c % 2)
+            for i in range(a // 512, b // 512):
+                pp = (64 * (i % 4 // 2), 64 * (i % 4 // 2) + 64, 1)
+                mm(bank(ring + i - a // 512), r("QCT", 128 * (i // 4), 128 * (i // 4) + 128, 1, pp), r("REP", 512 * (i % 2), 512 * (i % 2) + 512, 1, pp), True, True)
+            src = ind(XW, r("EU", a // 16, b // 16))
+            if e == "S":
+                act(r("XG", a, b), src, bias=-127.5)
+            else:
+                ts(r("XG", a, b), src, -127.5, A.add)
+            tt(r("H", a, b), r("XG", a, b), bank(ring, 0, b - a), A.min)
+            if b % 2048 == 0:
+                h = b // 2048 - 1
                 for k in range(16):
-                    mm(PQ[h][:, 128 + k:512:16], T.SD[:, 2048 * h + k:2048 * h + 2048:16], T.W3[:, 8:32], False, False,
-                       "SD%d SD%d W31 W32 W33" % (c - 1, c), "P%d:q" % h)
-            if c >= 2:
-                h = c - 2
-                sg = h == 0 and bool(S_CHUNKS)
+                    mm(bank(2 * h + 1, 15 - k, 256, 16), r("XG", 2048 * h + k, 2048 * h + 2048, 16), r("W3", 8, 24), False, k == 15)
                 for k in range(16):
-                    mm(PQ[h][:, k:128:16], T.HD[:, 2048 * h + k:2048 * h + 2048:16], T.W3[:, 0:8], False, k == 15 and not sg,
-                       "HD%d HD%d W30" % (2 * h, 2 * h + 1), "P%d:q" % h)
-                for k in range(16 if sg else 0):
-                    mm(PQ[0][:, k:128:16], T.GD[:, k:2048:16], T.W3[:, 32:40], False, k == 15, "GD0 GD1 W34", "P0:q")
-        lanes_s()
-        act(T.QT[:], XW.indirect(T.CU[:]), XK + " CU", "QT")
-        act(T.KC[:], T.KF[:].indirect(T.C10[:]), "KF C10", "KC", bias=-2048.0)
-        act(T.QH[:, 0:256], T.QT[:], "QT", "QH0", bias=-159.625, scale=-0.25)
-        act(T.QH[:, 256:512], T.QT[:], "QT", "QH1", scale=0.5)
-        mm(T.P6[:], I1, T.QH[:], True, False, "IV0 QH0 QH1", "P6:a")
-        mm(T.P7[:, 0:256], I1, T.ND[:], True, False, "IV0 ND", "P7:r")
-
-        def choice(h):
-            sl = slice(128 * h, 128 * h + 128)
-            s2 = slice(256 + 128 * h, 384 + 128 * h)
-            k, H = "P%d:q" % h, str(h)
-            return [
-                lambda: ts(T.P8[:, sl], PQ[h][:, 0:128], 1.5 * 2.0 ** 31, A.add, k, "P8" + H, -1.5 * 2.0 ** 31, A.add),
-                lambda: tt(T.NC[:, sl], T.P8[:, sl], PQ[h][:, 0:128], A.is_gt, k + " P8" + H, "NC" + H),
-                lambda: tt(T.P2[:, s2], T.P8[:, sl], PQ[h][:, 384:512], A.add, k + " P8" + H, "P2:y" + H),
-                lambda: tt(T.TA[:, sl], T.NC[:, sl], PQ[h][:, 128:256], A.mult, k + " NC" + H, "TA" + H),
-                lambda: tt(T.P2[:, sl], T.TA[:, sl], PQ[h][:, 256:384], A.max, k + " TA" + H, "P2:t" + H),
-                lambda: tt(T.KEY[:, sl], T.P8[:, sl], T.P2[:, sl], A.add, "P8%s P2:t%s" % (H, H), "KEY" + H),
-                lambda: scan(T.SC1[:, sl], T.RSB[:, 0:128], T.KEY[:, sl], A.max, A.min, "RSB KEY" + H, "SC1" + H),
-                lambda: tt(T.EQ[:, sl], T.SC1[:, sl].indirect(T.LAST[:]), T.KEY[:, sl], A.is_equal, "LAST SC1%s KEY%s" % (H, H), "EQ" + H),
-                lambda: tt(T.RP[:, sl], T.EQ[:, sl], T.P2[:, s2], A.mult, "EQ%s P2:y%s" % (H, H), "RP" + H),
-                lambda: scan(T.SC2[:, sl], T.RS0[:], T.RP[:, sl], A.mult, A.max, "RS0 RP" + H, "SC2" + H)]
-        c0, c1 = choice(0), choice(1)
-        ow = own_rivals()
-        weave(c0[:6], ow[:1])
-        weave(c1, c0[6:] + ow[1:])
-        own = append(t, T.OC, T.OLD, T.VO, "OLD", "OC", "VO")
-        cp(T.YI[:], T.SC2[:, 15::16], "SC20 SC21", "YI")
-        ts(T.HL[:], T.SC1[:, 15::16], 2.0 ** 26, A.is_lt, "SC10 SC11", "HL")
-        ts(T.SE[:], T.YI[:], 4095, A.bitwise_and, "YI", "SE")
-        ts(T.PP[:], T.YI[:], 12, A.arith_shift_right, "YI", "PP", 15, A.bitwise_and)
-        ts(T.SM[:, 0:16], T.SE[:], -2048.0, A.add, "SE", "SM0")
-        act(T.HM[:], T.HL[:].indirect(c16), "HL LIN", "HM")
-        tt(T.PM[:], T.PP[:].indirect(c16), T.SI[:], A.is_equal, "PP LIN SI", "PM")
-        tt(T.DG[:, 0:256], T.SM[:, 0:16].indirect(c16), T.MS[:], A.mult, "SM0 LIN MS", "DG0")
-        act(T.PM2[:, 0::2], T.PM[:, 1::2], "PM", "PM2a")
-        act(T.PM2[:, 1::2], T.PM[:, 0::2], "PM", "PM2b")
+                    mm(bank(2 * h, 15 - k, 256, 16), r("H", 2048 * h + k, 2048 * h + 2048, 16), r("W3", 0, 16), False, k == 15)
         for h in range(2):
-            mm(T.P3[:, 128 * h:128 * h + 128], T.PM[:, 128 * h:128 * h + 128], I1, True, True, "PM IV0", "P3:p")
-        for j in range(2):
-            mm(T.P4[:, 128 + 8 * j:136 + 8 * j], T.DG[:, 128 * j:128 * j + 128], T.S8H[:], True, True, "DG0 S8H", "P4:e")
+            mm(qy(h), hf(r("QC"), h), BOU, True, False)
+            mm(qy(h), hf(G, h), WB2, False, False)
+            mm(qy(h), hf(r("EF"), h), PRV, False, False)
+            for k in range(16):
+                mm(sub(qy(h), 15 - k, 128, 16), r("XG", 2048 * h + k, 2048 * h + 2048, 16), r("W3", 24, 32), False, False)
+        append(t, r("OC"), r("OLD"), r("VO"))
         for h in range(2):
-            mm(T.P2[:, 128 * h:128 + 128 * h], T.PM2[:, 128 * h:128 * h + 128], I1, True, True, "PM2a PM2b IV0", "P2:t0 P2:t1")
-        tt(T.T5[:, 0:16], T.SM[:, 0:16], T.CL[:], A.subtract, "SM0 CL", "T50")
-        tt(MD, T.P3[:, 0:256], T.DX[:], A.mult, "P3:p DX", "MD")
-        tt(T.T5[:, 16:32], T.T5[:, 0:16], T.HL[:], A.mult, "T50 HL", "T51")
-        ts(T.EI[:, 0:16], T.P4[:, 128:144], 2048.0, A.add, "P4:e", "EI0")
-        tt(T.SM[:, 16:32], T.T5[:, 16:32], T.CL[:], A.add, "T51 CL", "SM1")
-        ts(T.EI[:, 16:32], T.EI[:, 0:16], 1023, A.bitwise_and, "EI0", "EI1")
-        cp(T.EW[:], T.EI[:, 0:16], "EI0", "EW")
-        cp(T.E10[:], T.EI[:, 16:32], "EI1", "E10")
-        mm(T.P7[:, 0:256], BO1, MD, False, False, "BO MD", "P7:r")
-        mm(T.P1[:, 0:256], BO1, MD, True, False, "BO MD", "P1:q")
-        act(T.KE[:], T.KV[:].indirect(T.E10[:]), "KV E10", "KE")
-        act(T.PE_[:], T.SM[:, 16:32].indirect(c16), "SM1 LIN", "PE")
-        act(T.YT[:], XW.indirect(T.EW[:]), XK + " EW", "YT")
-        tt(M2, T.P2[:, 0:256], T.KC[:], A.mult, "P2:t0 P2:t1 KC", "M2")
-        tt(M1, T.P3[:, 0:256], T.KC[:], A.mult, "P3:p KC", "M1")
-        tt(M4, T.P2[:, 0:256], T.KE[:], A.mult, "P2:t0 P2:t1 KE", "M4")
-        tt(T.DG[:, 256:512], T.SM[:, 16:32].indirect(c16), T.MS[:], A.mult, "SM1 LIN MS", "DG1")
+            qa = lambda s: bank(2 * h, 128 * s, 128 * s + 128)
+            qb = lambda s: bank(2 * h + 1, 128 * s, 128 * s + 128)
+            x = lambda name: hf(r(name), h)
+            act(x("R0"), qa(0), ACT.Relu)
+            tt(x("N"), x("R0"), qb(0), A.max)
+            tt(x("NC"), x("N"), qa(1), A.is_gt)
+            tt(qa(2), x("NC"), qb(1), A.mult)
+            mm(qy(h), r("IF"), x("N"), False, True)
+            tt(qa(3), x("N"), qa(2), A.add)
+            scan(x("SC1"), r("RSB"), qa(3), A.max, A.min)
+            tt(x("NE"), x("SC1"), qa(3), A.not_equal)
+            tt(x("HY"), qy(h), x("NE"), A.subtract)
+            scan(x("SC2"), x("NE"), x("HY"), A.mult, A.max)
+        mm(bank(4), I1, r("CIN"), True, False)
+        mm(bank(7), r("ON"), r("CZ"), True, False)
+        mm(bank(7, 0, 512, 2), IQ, r("QC"), False, False)
+        mm(bank(7, 1, 512, 2), IH, r("QC"), False, False)
+        bt = lambda i: r("BT", 16 * i, 16 * i + 16)
+        ts(r("YI"), r("SC2", 15, 256, 16), 2.0 ** 25, A.mult)
+        ts(lt(QM), r("SC1", 15, 256, 16), 5000.0, A.is_ge)
+        ts(bt(0), r("YI"), 2, A.arith_shift_right, 1024, A.bitwise_and)
+        ts(bt(1), r("YI"), 1023, A.bitwise_and)
+        ts(bt(2), r("YI"), 13, A.arith_shift_right, 7, A.bitwise_and)
+        ts(bt(3), r("YI"), 4095, A.bitwise_and)
+        tt(lt(QKE), bt(0), bt(1), A.add)
+        tt(lt(QKC), bt(0), r("C10"), A.add)
+        tt(lt(QD), bt(0), r("CL", 16, 32), A.not_equal)
+        act(lt(QA), bt(2))
+        act(lt(QA2), bt(2), ACT.Square)
+        act(lt(QE), bt(3), bias=-2048.0)
+        tt(r("T5", 0, 16), r("CL", 0, 16), bt(3), A.subtract)
+        tt(r("T5", 16, 32), r("T5", 0, 16), lt(QM), A.mult)
+        tt(lt(QP), r("T5", 16, 32), lt(QE), A.add)
         for h in range(2):
-            sl, s2 = slice(128 * h, 128 * h + 128), slice(256 + 128 * h, 384 + 128 * h)
-            mm(T.P6[:, sl], T.HM[:, sl], INB, False, False, "HM IV3", "P6:a")
-            mm(T.P6[:, s2], T.HM[:, sl], IB, False, False, "HM IV2", "P6:a")
-        mm(T.P7[:, 0:256], BO1, M4, False, True, "BO M4", "P7:r")
-        mm(T.P1[:, 0:256], BO1, M4, False, True, "BO M4", "P1:q")
-        for j in range(2):
-            mm(T.P4[:, 144 + 8 * j:152 + 8 * j], T.DG[:, 256 + 128 * j:384 + 128 * j], T.S8H[:], True, True, "DG1 S8H", "P4:x")
+            mm(bank(5, 128 * h, 128 * h + 128), hf(r("LT"), h), I1, True, True)
         for h in range(2):
-            sl = slice(128 * h, 128 * h + 128)
-            mm(T.P0[:, sl], T.PE_[:, sl], T.IF[:], True, True, "PE IF", "P0:q")
-        mm(T.P6[:, 0:256], I1, T.YT[:], False, False, "IV0 YT", "P6:a")
-        mm(T.P6[:, 256:512], IH, T.YT[:], False, True, "IV1 YT", "P6:a")
+            mm(bank(4, 256 * h, 256 * h + 256), hf(r("LT"), h), r("IDUP"), False, h == 1)
+        act(G, bank(5, 0, 256))
+        op("V", lambda q: q.transpose(ap(r("WT")), ap(bank(4))), [r("WT")], [bank(4)], 1)
+        wq = lambda a, b: ind(r("WT"), r("SELQ", a, b))
+        cp(r("UW", 0, 32), wq(QKE, QKE + 2))
+        mm(bank(6, 0, 256), WM, G, True, True)
+        act(r("MSK"), bank(6, 0, 256), ACT.Relu, bias=RHO, scale=-1.0)
+        act(r("UW", 32, 64), wq(QE, QE + 2))
+        act(r("DW", 16, 32), wq(QD, QD + 1), bias=BB1, scale=0.5)
+        act(r("NG", 32, 48), wq(QP, QP + 1), bias=XBH, scale=-0.5)
+        tt(ME, ind(r("KA"), r("UW", 0, 16)), r("MSK"), A.mult)
+        tt(MC, ind(r("KI"), r("UW", 16, 32)), r("MSK"), A.mult)
         dst = T.cores[(rank + 1 + t % (n - 1)) % n]
         src = T.cores[(rank - 1 - t % (n - 1)) % n]
-        sv = slice(256 * t, 256 * t + 256)
-        mm(T.P5[:, 0:256], I1, T.BNB[:, o:o + 256], True, False, "BNB IV0", "P5:v")
-        if not last:
-            mm(T.P5[:, 0:256], BON, MD, False, False, "MD BO5", "P5:v")
-        mm(T.P5[:, 0:256], BO1, M2, False, True, "BO M2", "P5:v")
-        act(T.SV[:, sv], T.P5[:, 0:256], "P5:v", sk + "b", bias=2048.0 if last else 2048.0 + XO)
-        remote(T.LV[:, sv], T.SV[:, sv], "arv%d" % t, dst, src, sk + "b", sk + "y", lk + "v")
-        scan(T.SW[:], T.RSB[:], T.P7[:, 0:256], A.max, A.min, "RSB P7:r", "SW")
-        tt(M3, T.P3[:, 0:256], T.KE[:], A.mult, "P3:p KE", "M3")
-        distances(T.AB2, T.P1[:, 0:256], lambda m: T.SW[:, 16 * m + 15:16 * m + 16], "P1:q SW", "AB2")
-        act(T.C2[:], T.SW[:, 15::16], "SW", "C2n", scale=-1.0 / BIG)
-        act(T.WX[:, 0:16], T.P4[:, 144:160], "P4:x", "WX0")
-        act(T.WX[:, 16:32], T.P4[:, 144:160], "P4:x", "WX1", scale=-1.0 / BIG, bias=-2048.0 / BIG)
-        if not last:
-            wbatch()
-        distances(T.ABX, T.P0[:, 0:256], lambda m: T.WX[:, m:m + 1], "P0:q WX0", "ABX")
-        act(T.AA[:], T.P6[:, 0:256], "P6:a", "AA", f=ACT.Abs, bias=1184.0)
-        act(T.RR[:], T.P6[:, 256:512], "P6:a", "RR", bias=1.5 * 2.0 ** 23, scale=0.9995)
-        act(T.R2[:], T.RR[:], "RR", "R2", bias=-1.5 * 2.0 ** 23)
-        s2 = rivals(T.SC3, T.AB2, T.U2[:], T.TRB, T.C2[:], T.SND[:, sa], "AB2", "C2n", sk + "a")
-        xr = rivals(T.SCX, T.ABX, T.UX[:, 0:16], T.TRX, T.WX[:, 16:32], T.UX[:, 16:32], "ABX", "WX1", "UX") + [
-            lambda: ts(T.OX[:], T.UX[:, 16:32], -BIG, A.mult, "UX", "OX")]
-        weave(own[:2])
-        weave(s2, own[2:])
-        remote(T.LND[:, sa], T.SND[:, sa], "arr%d" % t, dst, src, sk + "a " + sk + "y", sk + "x", lk)
-        weave(xr)
-        tt(T.VA[:], T.AA[:], T.R2[:], A.min, "AA R2", "VA")
+        sa, sv = (16 * t, 16 * t + 16), (256 * t, 256 * t + 256)
+        for i in range(16):
+            mm(bank(5, 256, 272), ZH(1, i), sub(ME, i, 256, 16), i == 0, i == 15)
+        tt(r("NG", 16, 32), r("DW", 16, 32), bank(5, 256, 272), A.subtract)
+        masked(t, bank(4, 256, 512), BOO, r("SV", *sv))
+        remote(r("LV", *sv), r("SV", *sv), "arv%d" % t, dst, src)
+        rivals(1, 0, bank(6, 256, 384, 1, (0, 16, 1)), [(G, BODN), (ME, BOO)], r("NG", 16, 32), BB, r("SND", *sa))
+        remote(r("LND", *sa), r("SND", *sa), "arr%d" % t, dst, src)
+        rivals(2, 2, bank(4, 0, 128, 1, (0, 16, 1)), [(G, BOP)], r("NG", 32, 48), XB, r("OX"))
+        act(r("YT"), ind(XW, r("UW", 32, 48)))
+        mm(bank(7, 0, 512, 2), I1, r("YT"), False, False)
+        mm(bank(7, 1, 512, 2), IH, r("YT"), False, True)
+        act(r("ZR"), bank(7))
+        act(r("VA"), ind(r("ZR"), r("UW", 48, 64)), ACT.Abs)
+        for b in range(4):
+            cp(ind(XW, r("OX", 4 * b, 4 * b + 4)), r("VA", 64 * b, 64 * b + 64))
         for h in range(2):
-            mm(T.P3[0:8, 16:17], T.HL[:, 8 * h:8 * h + 8], T.ON[:, 0:1], h == 0, h == 1, "HL ON", "P3:p")
+            mm(bank(5, 272, 273), hf(r("LT"), h), r("ON", 0, 1), h == 0, h == 1)
+        act(r("YM", t, t + 1), bank(5, 272, 273))
         if not last:
-            act(T.VC[:], T.VA[:], "VA", "VC", bias=255.0, scale=-1.0)
-            for h in range(2):
-                mm(T.P7[:, 256:264], T.ON[:], T.HL[:, 8 * h:8 * h + 8], h == 0, h == 1, "HL ON", "P7:n")
-        act(T.YM[0:8, t:t + 1], T.P3[0:8, 16:17], "P3:p", "YM", bias=256.0, scale=-128.0)
-        xa = [(lambda b=b: cp(T.XT[:, 0:XO].indirect(T.OX[:, 4 * b:4 * b + 4]), T.VA[:, 64 * b:64 * b + 64], "VA OX", "X")) for b in range(4)]
-        xc = [(lambda b=b: cp(T.XT[:, XO:2 * XO].indirect(T.OX[:, 4 * b:4 * b + 4]), T.VC[:, 64 * b:64 * b + 64], "VC OX", "Xc")) for b in range(4)]
-        if not last:
-            wbatch_s()
-            lanes_pe(t + 1)
-            lanes_s0()
-            lw = lanes_w()
-            weave(xa, xc[:3])
-            weave(xc[3:] + [lw[4]], [lw[0]])
-            shapes_of_lanes()
-            fill = lw[1:4] + lw[5:] + [lambda: ts(T.PA[:, 0:8], T.P7[:, 256:264], 128.0, A.mult, "P7:n", "PA0"),
-                                       lambda: ts(T.PA[:, 8:16], T.PA[:, 0:8], 1, A.bitwise_and, "PA0", "PA1"),
-                                       lambda: cp(T.PF[:], T.PA[:, 8:16], "PA1", "PF")]
+            act(r("PA", 0, 1), bank(5, 272, 273))
+            ts(r("PA", 1, 2), r("PA", 0, 1), 1, A.bitwise_and)
+            act(r("PF", 0, 1), r("PA", 1, 2))
+            act(r("WA"), WAC, scale=r("PF", 0, 1))
+            act(r("DW", 0, 16), wq(QD, QD + 1), bias=BBH, scale=-1.0)
+            lanes(t + 1, r("DW", 0, 16))
         else:
-            fill = []
-            weave(xa)
             for b in range(8):
-                act(T.SD[:, 512 * b:512 * b + 512], T.XT[:, 512 * b:512 * b + 512], "X", "YS%d SD%d" % (b, b // 2), acc=T.YS[:, b:b + 1])
-            dma("S", T.ys[:], T.YS[:], " ".join("YS%d" % b for b in range(8)), "")
-            dma("S", T.ym[:], T.YM[0:8, 0:ST], "YM", "")
-            for j, (a, b) in enumerate(((1.0, 2048.0), (0.5, 0.0), (-1.0, 1.0))):
-                bank = (T.P5, T.P5, T.P7)[j]
-                cs = slice(256 * (j % 2), 256 * (j % 2) + 256)
-                k = ("P5:v", "P5:o", "P7:r")[j]
-                mm(bank[:, cs], BO1, (M1, M3, MD)[j], True, True, "BO M1 M3 MD", k)
-                act(T.YO[:, 256 * j:256 * j + 256], bank[:, cs], k, "YO%d" % j, bias=b, scale=a)
-                act(T.YR[:, 256 * j:256 * j + 256], T.YO[:, 256 * j:256 * j + 256].indirect(T.REV[:]), "REV YO%d" % j, "YR%d" % j)
-                dma("S", (T.yc, T.yv, T.yd)[j][:], T.YR[0::16, 256 * j:256 * j + 256], "YR%d" % j, "")
-        ts(T.RC[:], T.LND[:, sa], -BIG, A.mult, lk, "RC")
-        rec = append(t, T.RC, T.OL2, T.LV[:, sv], "OL2", "RC", lk + "v")
-        weave(rec, fill[0::2], fill[1::2])
-    dma("Y", T.yb[:], T.B[:, 0:2048], "B", "")
-    _emit(g, T, [ops[i] for i in _order(ops, SHIFT)])
+                act(r("XG", 512 * b, 512 * b + 512), r("XT", 512 * b, 512 * b + 512), acc=r("YS", b, b + 1))
+            dma("S", T.ys[:], r("YS"), [], [r("YS")], 0)
+            dma("S", T.ym[:], r("YM", 0, ST, 1, (QM, 128, 16)), [], [r("YM")], 0)
+            for j, (w, x, a, b) in enumerate(((BOE, MC, 1.0, 2048.0), (BOE, ME, 1.0, 0.0), (BOD, G, 2.0, 0.0))):
+                ps = bank((6, 6, 5)[j], (256, 0, 0)[j], (512, 256, 256)[j])
+                mm(ps, w, x, True, True)
+                act(r("YO", 256 * j, 256 * j + 256), ps, bias=b, scale=a)
+                act(r("YR", 256 * j, 256 * j + 256), ind(r("YO", 256 * j, 256 * j + 256), r("REV")))
+                dma("S", (T.yc, T.yv, T.yd)[j][:], r("YR", 256 * j, 256 * j + 256, 1, row0), [], [r("YR", 256 * j, 256 * j + 256)], 0)
+        append(t, r("LND", *sa), r("OL2"), r("LV", *sv))
+    dma("Y", T.yb[:], r("B", 0, 2048), [], [r("B", 0, 2048)], MB)
+    deps = _graph(ops)
+    _emit(g, T, ops, deps, _order(ops, deps, after))

@@ -4,22 +4,23 @@ ST = 6
 F32, BF, F16, I32, U16 = "float32", "bfloat16", "float16", "int32", "uint16"
 BIG = 16384.0
 SEG = (0, 256, 448, 576, 640)
-QD, QA, QKE, QKC, QE, QM, QP, QA2, Q1 = 0, 1, 2, 3, 4, 5, 6, 7, 15
-CHUNKS = ((0, 1024, "S"), (1024, 2048, "S"), (2048, 3072, "S"), (3072, 3584, "S"), (3584, 4096, "S"))
+QD, QA, QKE, QKC, QE, QM, QP, QA2, QP2, Q1 = 0, 1, 2, 3, 4, 5, 6, 7, 8, 15
+CHUNKS = ((0, 512, "V"), (512, 1024, "S"), (1024, 2048, "S"), (2048, 3072, "S"), (3072, 3584, "S"), (3584, 4096, "S"))
+HOP, NEAR, TCY, BIAS = 100.0, 0.5, 0.5, 100.0
 
 SB = {
-    "XT": (4160, BF), "B": (2112, F32), "BI": (2048, I32), "KI": (2048, I32), "KA": (2048, I32), "LN": (768, I32),
+    "XT": (4160, BF), "B": (2112, F32), "BI": (2048, I32), "KI": (2048, I32), "KA": (2048, I32), "KV": (4096, F32), "LN": (768, I32),
     "PI": (8, I32), "COL": (24, F32), "JF": (256, F32), "CG": (128, F32), "SI": (128, F32), "SR": (272, F32), "EQ": (16, F32),
-    "REP": (1024, BF), "IDUP": (256, BF), "CI0": (512, F32), "CIN": (512, F16), "SJ": (640, BF), "SM": (640, BF), "MK": (640, BF),
-    "REPT": (640, BF), "RH": (128, BF), "BO": (128 * 15, BF), "IV": (128 * 5, BF), "IF": (128, F32), "ZH": (144 * 4, BF), "W3": (32, BF),
+    "REP": (1024, BF), "IDUP": (256, BF), "SJ": (640, BF), "SM": (640, BF), "MK": (640, BF),
+    "REPT": (640, BF), "RH": (128, BF), "BO": (128 * 14, BF), "IV": (128 * 4, BF), "W3": (32, BF),
     "S8": (8, BF), "BM": (272, F32), "BNB": (272, BF), "RSB": (128, F32), "CZ": (512, BF), "ON": (128, BF), "ZE": (128, BF),
     "REV": (16, U16), "ENDS": (2, U16), "SELQ": (8, U16),
     "EU": (256, U16), "EF": (256, F16), "QC": (256, BF), "QCT": (256, F16), "XG": (4096, BF), "H": (4096, F16),
-    "R0": (256, I32), "N": (256, F32), "NC": (256, F32), "SC1": (256, F32), "NE": (256, F32), "HY": (256, F32), "SC2": (256, F32),
-    "YI": (16, I32), "BT": (64, I32), "T5": (32, F32), "LT": (256, F16), "CL": (32, I32), "C10": (16, I32),
+    "R0": (256, I32), "N": (256, F32), "NU": (256, F32), "NC": (256, F32), "SC1": (256, F32), "NE": (256, F32), "HY": (256, F32), "SC2": (256, F32),
+    "YI": (16, I32), "BT": (64, I32), "T5": (32, F32), "LT": (256, F16), "DT": (256, F16), "CL": (32, I32), "C10": (16, I32),
     "G": (256, F16), "WT": (512, F32), "UW": (64, U16), "MSK": (256, BF), "MM": (512, F16), "WA": (128, BF), "PA": (8, I32), "PF": (8, F32),
     "CU": (16, U16), "CRU": (16, U16), "OC": (16, U16), "OX": (16, U16),
-    "TW": (384, F16), "AB": (640 * 3, BF), "SC": (640 * 3, BF), "DW": (48, F32), "NG": (48, F32), "WN": (48, F32),
+    "TW": (384, F16), "AB": (640 * 3, BF), "SC": (640 * 3, BF), "DW": (16, F32), "NG": (48, F32), "WN": (48, F32),
     "VO": (256, F32), "OLD": (256, F32), "OL2": (256, F32), "YT": (256, BF), "ZR": (512, I32), "VA": (256, BF),
     "SND": (16 * ST, U16), "LND": (16 * ST, U16), "SV": (256 * ST, F32), "LV": (256 * ST, F32),
     "YS": (8, F32), "YM": (8, F32), "YO": (768, F32), "YR": (768, F32),
@@ -43,6 +44,10 @@ def sub(x, a, b, s=1):
     return (x[0], x[1] + a * x[3], x[1] + (b - 1) * x[3] + 1, x[3] * s, x[4])
 
 
+def top(x, n):
+    return x[:4] + ((0, n, 1),)
+
+
 def size(x):
     return 16 * size(x[2]) if x[0] == "*" else len(range(x[1], x[2], x[3]))
 
@@ -54,13 +59,14 @@ def _meet(x, y):
 
 
 def _banks(x):
-    return [(x[0], k) for k in range(x[1] // 512, (x[2] - 1) // 512 + 1)] if x[0] not in SB and x[0][0] == "P" else []
+    return [(x[0], k) for k in range(x[1] // 512, (x[2] - 1) // 512 + 1)] if x[0] in SCRATCH and x[0] not in SB else []
 
 
-def _graph(ops):
+def _graph(ops, either):
     seen, last, deps = {}, {}, []
     for i, (e, fn, rd, wr, kind, cost) in enumerate(ops):
         d = set()
+        e = i if i in either else e
         for x, w in [(x, False) for x in rd] + [(x, True) for x in wr]:
             d.update(j for j, y, v in seen.get(x[0], []) if (w or v) and _meet(x, y))
         for k in set(b for x in rd + wr for b in _banks(x)):
@@ -78,7 +84,7 @@ def _graph(ops):
     return deps
 
 
-def _order(ops, deps, after):
+def _order(ops, deps, after, either):
     n = len(ops)
     users = [[] for _ in ops]
     for i in range(n):
@@ -96,12 +102,15 @@ def _order(ops, deps, after):
     ready = {i: 0.0 for i in range(n) if not left[i]}
     free, order, done = {}, [], {}
     while ready:
+        for i in ready:
+            if i in either and max(ready[i], free.get(either[i][0], 0.0)) + either[i][5] + (BIAS if either[i][0] == "V" else -BIAS) < max(ready[i], free.get(ops[i][0], 0.0)) + ops[i][5]:
+                ops[i], either[i] = either[i], ops[i]
         start = {i: max(t, free.get(ops[i][0], 0.0)) for i, t in ready.items()}
         i = min(start, key=lambda j: (start[j], -tail[j]))
         near = [j for j in start if ops[j][0] == ops[i][0] and start[j] <= start[i] + NEAR * ops[i][5]]
         i = max(near, key=lambda j: (tail[j], -j))
         end = start[i] + ops[i][5]
-        free[ops[i][0]] = end if ops[i][4] == "c" else start[i] + (ops[i][5] if ops[i][4][0] == "send" else 60)
+        free[ops[i][0]] = end if ops[i][4] == "c" or ops[i][4][0] == "send" else start[i] + 60
         order.append(i)
         del ready[i]
         for u, at in [(u, end + hop(i, u)) for u in users[i]] + [(u, start[i]) for u in then.get(i, [])]:
@@ -110,9 +119,6 @@ def _order(ops, deps, after):
             if not left[u]:
                 ready[u] = done[u]
     return order
-
-
-HOP, NEAR = 80.0, 0.5
 
 
 def _emit(g, T, ops, deps, order):
@@ -170,7 +176,7 @@ def rank_program(g, core, T, topo):
     if rank is None:
         return
     n = len(T.cores)
-    ops, after = [], []
+    ops, after, either = [], [], {}
     A = ALU
 
     def ap(x):
@@ -216,9 +222,17 @@ def rank_program(g, core, T, topo):
     def act(out, a, f=ACT.Identity, bias=0.0, scale=1.0, acc=None):
         op("S", lambda q: q.activation(ap(out), ap(a), f, bias=ap(bias), scale=ap(scale), accum_out=ap(acc)), [out] + ([acc] if acc else []), [a, bias, scale], 1)
 
+    def lin(out, a, bias=0.0, scale=1.0):
+        ts(out, a, scale, A.mult, bias, A.add)
+        v = ops.pop()
+        act(out, a, bias=bias, scale=scale)
+        either[len(ops) - 1] = v
+
+    def hold(first):
+        after.append((len(ops), first))
+
     def mm(out, l, rh, st, sp):
-        c = max(min(64, size(l)), size(rh)) * (4 if SB[l[0]][1] == F32 else 1)
-        op("T", lambda q: q.matmul(ap(out), ap(l), ap(rh), st, sp), [out], [l, rh], 0.5 * c)
+        op("T", lambda q: q.matmul(ap(out), ap(l), ap(rh), st, sp), [out], [l, rh], TCY * max(min(64, size(l)), size(rh)))
 
     def dma(e, out, a, wr, rd, nbytes):
         op(e, lambda q: q.dma_start(ap(out), ap(a)), wr, rd, 2000 + nbytes / 190.0, "d")
@@ -230,15 +244,15 @@ def rank_program(g, core, T, topo):
             op("G", lambda q: q.iota(ap(out), pat, base, cm, allow_small_or_imprecise_dtypes=True), [out], [], 130 + 1.66 * size(out))
 
     col = lambda i: r("COL", i, i + 1)
-    PR, PG, PP, P63, ZC, RVC, EVN, ODD, RHO, XB, BB, BB1, BBH, SQ, CA, CK, E1, E2, EN, MI, PX, XBH = [col(i) for i in range(22)]
+    PR, PG, PP, P63, RVC, EVN, ODD, RHO, XB, BB, BB1, SQ, CA, CK, E1, E2, EN, MI, PX, XC, CP = [col(i) for i in range(21)]
     eq = lambda i: r("EQ", i, i + 1)
     bo = lambda i, k=1: r("BO", 128 * i, 128 * (i + k))
-    BO1, BOH, BOU, BOE, BOO, BOD, BODN, BOP, BO8, WM, WB1, WB2, WAC, WGA, WG2 = [bo(i) for i in range(15)]
+    BO1, BOH, BOU, BOE, BOO, BOD, BOP, BO8, WM, WB1, WB2, WAC, WGA, WG2 = [bo(i) for i in range(14)]
     s8 = lambda x: sub(x, 0, 128, 16)
     I1, IQ, IH, PRV = [r("IV", 128 * i, 128 * i + 128) for i in range(4)]
-    ZH = lambda i, k: r("ZH", 144 * i + 15 - k, 144 * i + 143 - k)
     lt = lambda q: r("LT", q, 256, 16)
-    XW, BW, G, MC, ME = r("XT"), r("B"), r("G"), r("MM", 0, 256), r("MM", 256, 512)
+    dt = lambda q: r("DT", q, 256, 16)
+    XW, BW, G, ME, MC = r("XT"), r("B"), r("G"), r("MM", 0, 256), r("MM", 256, 512)
     hf = lambda x, h: sub(x, 128 * h, 128 * h + 128)
     row0 = (0, 128, 16)
     MB = 1 << 20
@@ -263,7 +277,6 @@ def rank_program(g, core, T, topo):
         iota(r("SM", SEG[mi], SEG[mi + 1]), [[4, 4], [0, 64 - 16 * mi]], mi)
     iota(r("IDUP"), [[16, 8], [0, 2], [1, 16]])
     iota(r("RH"), [[0, 8], [-2, 8], [0, 2]])
-    iota(r("CI0"), [[32, 16], [0, 2], [2, 16]])
     pi = lambda i: r("PI", i, i + 1)
     ts(pi(1), pi(0), 15, A.bitwise_and)
     ts(pi(2), pi(0), 4, A.arith_shift_right)
@@ -275,39 +288,34 @@ def rank_program(g, core, T, topo):
     act(r("COL", 0, 2), r("PI", 1, 3))
     act(PP, pi(0))
     act(P63, pi(3))
-    act(ZC, PG, bias=15.0, scale=16.0)
-    act(RVC, PR, bias=255.0, scale=-1.0)
+    act(RVC, pi(1), bias=255.0, scale=-1.0)
     act(ODD, pi(4))
-    act(EVN, ODD, bias=1.0, scale=-1.0)
-    act(XB, PR, bias=4096.0 + 48)
-    act(XBH, PR, bias=2048.0 + 24, scale=0.5)
-    act(BB, PR, bias=2048.0 + 48)
-    act(BBH, PR, bias=1024.0 + 24, scale=0.5)
-    act(BB1, PR, bias=1024.0 + 23.5, scale=0.5)
+    act(EVN, pi(4), bias=1.0, scale=-1.0)
+    act(XB, pi(1), bias=4096.0 + 48)
+    act(BB, pi(1), bias=2048.0 + 48)
+    act(XC, pi(1), bias=2048.0 + 48)
+    act(BB1, pi(1), bias=2048.0 + 49)
     ts(r("EQ"), r("JF", 0, 16), PR, A.is_equal)
     ts(r("REV"), r("JF", 0, 16), -16.0, A.mult, RVC, A.add)
-    ts(r("ZH", 432, 576), r("JF", 0, 144), ZC, A.is_equal)
-    ts(r("ZH", 0, 144), r("ZH", 432, 576), EVN, A.mult)
-    ts(r("ZH", 144, 288), r("ZH", 432, 576), ODD, A.mult)
-    ts(r("ZH", 288, 432), r("ZH", 432, 576), eq(QD), A.mult, -0.5, A.mult)
     ts(BO1, r("CG"), PG, A.is_equal)
     ts(I1, r("JF", 0, 128), PP, A.is_equal)
     ts(CK, eq(0), -2048.0, A.mult)
-    ts(MC, ind(r("LN", 0, 256), r("REV")), CK, A.add)
-    cp(ME, ind(r("LN", 256, 512), r("REV")))
     ts(G, ind(r("LN", 512, 768), r("REV")), eq(Q1), A.add)
-    for x, c, w in ((BOH, -0.5, None), (BOU, -2.0 ** -13, None), (BOE, EVN, None), (BOO, ODD, None), (BOD, eq(QD), 0.5), (BODN, eq(QD), -0.5),
-                    (BOP, eq(QP), None), (BO8, eq(QD), 0.125), (WB1, eq(Q1), 8192.0), (WB2, eq(Q1), 2.0 ** -14), (WAC, eq(QM), -1.0 / 16)):
+    ts(r("OLD"), ind(r("LN", 256, 512), r("REV")), 2.0, A.mult, eq(0), A.add)
+    tt(ME, r("OLD"), G, A.subtract)
+    ts(MC, ind(r("LN", 0, 256), r("REV")), CK, A.add)
+    ts(CP, eq(QE), eq(QP), A.add, eq(QP2), A.subtract)
+    for x, c, w in ((BOH, -0.5, None), (BOU, -2.0 ** -13, None), (BOE, EVN, None), (BOO, ODD, None), (BOD, eq(QD), None),
+                    (BOP, CP, None), (BO8, eq(QD), 0.125), (WB1, eq(Q1), 8192.0), (WB2, eq(Q1), 2.0 ** -14), (WAC, eq(QM), -1.0 / 16)):
         ts(x, BO1, c, A.mult, w, w and A.mult)
     ts(CA, eq(Q1), -17.0 / 32, A.mult, eq(QD), A.add)
     ts(WGA, BO1, CA, A.mult)
     ts(WG2, BO1, CA, A.mult)
-    ts(r("S8"), s8(BOD), 2048.0, A.mult)
+    act(r("S8"), s8(BOD), scale=1024.0)
     for i, w in enumerate((-1.0, -1.0, 0.5, 2.0 ** -13)):
         act(r("W3", 8 * i, 8 * i + 8), s8(BO1), scale=w)
     act(IQ, I1, scale=-0.25)
     act(IH, I1, scale=0.5)
-    act(r("IF"), I1, scale=2.0 ** -12)
     ts(PX, pi(1), -2.0, A.mult, PP, A.add)
     act(PX, PX, bias=15.0)
     ts(PRV, r("JF", 0, 128), PX, A.is_equal, 2.0 ** -25, A.mult)
@@ -319,6 +327,11 @@ def rank_program(g, core, T, topo):
     ms(r("WA"), 0.0)
     act(r("LT"), r("JF"), scale=0.0)
     act(lt(Q1), r("ON", 0, 16))
+    act(r("DT"), r("JF"), scale=0.0)
+    act(dt(QE), r("ON", 0, 16), scale=2048.0)
+    for h in range(2):
+        ts(sub(dt(QM), 8 * h, 8 * h + 8), r("ON", 0, 8), PP, A.mult, 2.0, A.mult)
+    ts(sub(dt(QM), 8, 16), sub(dt(QM), 8, 16), 256.0, A.add)
     ms(r("CZ", 0, 512, 2), -31.5 / 128)
     ms(r("CZ", 1, 512, 2), 63.5 / 128)
     ts(r("RSB"), r("SI"), 0.0, A.is_equal, 2.0 ** 20, A.mult)
@@ -326,11 +339,11 @@ def rank_program(g, core, T, topo):
     ts(r("BM"), r("SR"), PR, A.is_equal, BIG, A.mult)
     ts(r("MK"), r("SJ"), PR, A.is_le, 2.0 ** 30, A.mult)
     for mi in range(3):
-        ms(r("MK", SEG[mi] + 63 - 16 * mi, SEG[mi + 1], 64 - 16 * mi), 8.0 * (3 - mi))
+        ms(r("MK", SEG[mi] + 63 - 16 * mi, SEG[mi + 1], 64 - 16 * mi), 16.0 * (3 - mi))
     ts(r("REPT"), r("SM"), PP, A.is_equal, -1.0, A.mult)
     act(MI, pi(5))
-    act(E1, MI, bias=288.0, scale=-32.0)
-    act(E2, MI, bias=64.0, scale=-16.0)
+    act(E1, pi(5), bias=288.0, scale=-32.0)
+    act(E2, pi(5), bias=64.0, scale=-16.0)
     ts(EN, pi(6), 1.0, A.add, E2, A.mult)
     act(EN, EN, bias=-1.0)
     ts(r("ENDS", 0, 1), E1, MI, A.mult, EN, A.add)
@@ -343,35 +356,36 @@ def rank_program(g, core, T, topo):
     tt(RHO, PR, ODD, A.subtract)
     act(RHO, RHO, ACT.Square, scale=0.5)
     act(RHO, RHO, bias=1.0, scale=-1.0)
-    ts(E2, eq(QE), eq(QP), A.add, 2048.0, A.mult)
-    ts(r("CIN"), r("CI0"), eq(QM), A.mult, E2, A.add)
-    ts(r("KA"), r("KI"), 1023, A.bitwise_and)
-    act(r("KI"), r("KI"), bias=-2048.0)
     act(r("B", 0, 2048), r("BI"))
+    for u in range(2):
+        ts(r("KA", 1024 * u, 1024 * u + 1024), r("KI", 1024 * u, 1024 * u + 1024) if u == 0 else r("KI", 1024, 2048), 1023, A.bitwise_and)
+        act(r("KV", 1024 * u, 1024 * u + 1024), r("KA", 1024 * u, 1024 * u + 1024), bias=1.0 - u, scale=2.0)
+        ts(r("KV", 2048 + 1024 * u, 3072 + 1024 * u), r("KA", 1024 * u, 1024 * u + 1024), 2.0, A.mult, float(u), A.add)
+        act(r("KI", 1024 * u, 1024 * u + 1024), r("KI", 1024 * u, 1024 * u + 1024), bias=-2048.0)
 
-    def rivals(k, pk, tw, terms, neg, base, out):
-        p16 = (0, 16, 1)
-        mm(sub(tw, 0, 128), r("ZE", 0, 16), r("ZE"), True, False)
-        for j, (src, w) in enumerate(terms):
-            for i in range(16):
-                mm(sub(tw, i, 128, 16), sub(src, i, 256, 16), s8(w), False, j == len(terms) - 1 and i == 15)
-        own = r("TW", 128 * k, 128 * k + 128, 1, p16)
-        act(own, tw)
-        for bk in range(2):
-            lo, hi = 512 * bk, min(640, 512 * bk + 512)
-            parts = [(0, 0, 256)] + [(SEG[mi] + b * (64 - 16 * mi), 64 * b + 16 * mi, 64 - 16 * mi) for mi in (1, 2, 3) for b in range(4)]
-            parts = [x for x in parts if lo <= x[0] < hi]
-            for j, (src, w) in enumerate(terms):
-                if j == 0:
-                    mm(bank(pk, lo, hi), r("ZE"), r("CZ", 0, hi - lo), True, False)
-                for a, c, ln in parts:
-                    mm(bank(pk, a, a + ln), w, sub(src, c, c + ln), False, False)
-            mm(bank(pk, lo, hi), own, r("REPT", lo, hi, 1, p16), False, True)
+    def columns(tw, src, w, out):
+        for i in range(16):
+            mm(sub(tw, i, 128, 16), sub(src, i, size(src), 16), s8(w), True, True)
+        act(out, tw)
+
+    def rivals(k, pk, src, w, neg, base, out, early):
+        own = top(r("TW", 128 * k, 128 * k + 128), 16)
+        parts = [(0, 0, 256)] + [(SEG[mi] + b * (64 - 16 * mi), 64 * b + 16 * mi, 64 - 16 * mi) for mi in (1, 2, 3) for b in range(4)]
+        for lo, hi in ((0, 512), (512, 640)):
+            if early:
+                mm(bank(pk, lo, hi), r("ZE"), r("CZ", 0, hi - lo), True, False)
+            else:
+                mm(bank(pk, lo, hi), own, top(r("REPT", lo, hi), 16), True, False)
+            mine = [x for x in parts if lo <= x[0] < hi]
+            for a, c, ln in mine:
+                mm(bank(pk, a, a + ln), w, sub(src, c, c + ln), False, not early and a == mine[-1][0])
+            if early:
+                mm(bank(pk, lo, hi), own, top(r("REPT", lo, hi), 16), False, True)
         ab, sc, wn = r("AB", 640 * k, 640 * k + 640), r("SC", 640 * k, 640 * k + 640), r("WN", 16 * k, 16 * k + 16)
         act(ab, bank(pk, 0, 640), ACT.Abs, scale=BIG)
         scan(sc, ab, r("MK"), A.min, A.max)
         tt(wn, ind(sc, r("ENDS", 0, 1)), neg, A.min)
-        ts(out, wn, -2.0, A.mult, base, A.add)
+        ts(out, wn, -1.0, A.mult, base, A.add)
 
     def append(t, oc, old, val):
         o = (-5 * t) % 16
@@ -385,27 +399,25 @@ def rank_program(g, core, T, topo):
         mm(ps, w, MC, False, True)
         act(out, ps, bias=2048.0)
 
-    def lanes(t, dw):
-        for i in range(16):
-            mm(bank(6, 256, 288), ZH(0, i), r("MM", i, 512, 16), i == 0, False)
-        for i in range(16):
-            mm(bank(6, 272, 288), ZH(2, i), sub(G, i, 256, 16), False, i == 15)
+    def lanes(t):
+        tw = top(r("TW", 0, 128), 32)
+        columns(top(bank(4, 0, 128), 32), r("MM"), BOE, tw)
+        mm(bank(4, 128, 160), tw, top(sub(I1, 0, 32), 32), True, True)
         for h in range(2):
-            mm(bank(6, 288 + 8 * h, 296 + 8 * h), hf(MC, h), s8(BOE), True, True)
-            mm(bank(6, 304 + 8 * h, 312 + 8 * h), hf(G, h), r("S8"), True, True)
-        act(r("CU"), bank(6, 256, 272), bias=2048.0)
-        act(r("CRU"), bank(6, 272, 288), bias=1.0, scale=2.0)
-        act(r("CL", 0, 16), bank(6, 288, 304), bias=2048.0)
-        act(r("CL", 16, 32), bank(6, 304, 320))
-        tt(r("NG", 0, 16), dw, bank(6, 272, 288), A.subtract)
+            mm(bank(4, 160 + 8 * h, 168 + 8 * h), hf(MC, h), s8(BOE), True, True)
+            mm(bank(4, 176 + 8 * h, 184 + 8 * h), hf(G, h), r("S8"), True, True)
+        act(r("CU"), bank(4, 144, 160), bias=2048.0)
+        act(r("CRU"), bank(4, 128, 144))
+        act(r("CL"), bank(4, 160, 192))
+        tt(r("NG", 0, 16), r("DW"), bank(4, 128, 144), A.subtract)
+        act(dt(QKE), r("CL", 16, 32), scale=2.0)
         ts(r("C10"), r("CL", 0, 16), 1023, A.bitwise_and)
-        act(r("QC"), ind(XW, r("CU")), bias=-127.5)
+        act(dt(QKC), r("C10"))
+        lin(r("QC"), ind(XW, r("CU")), bias=-127.5)
         for h in range(2):
-            mm(bank(4, 128 * h, 128 * h + 128), hf(r("QC"), h), I1, True, False)
-            mm(bank(4, 128 * h, 128 * h + 128), hf(G, h), BO8, False, True)
-        act(r("QCT"), bank(4, 0, 256), bias=-1.0 / 16)
-        masked(t, bank(5, 0, 256), BOE, r("VO"))
-        rivals(0, 0, bank(6, 384, 512, 1, (0, 16, 1)), [(G, BOD), (ME, BOE)], r("NG", 0, 16), BB, r("OC"))
+            mm(bank(6, 256 + 128 * h, 384 + 128 * h), hf(r("QC"), h), I1, True, False)
+            mm(bank(6, 256 + 128 * h, 384 + 128 * h), hf(G, h), BO8, False, True)
+        lin(r("QCT"), bank(6, 256, 512), bias=-1.0 / 16)
 
     def remote(out, in_, sem, dst, src):
         rid, pid, _ = topo.addr(dst)
@@ -414,10 +426,10 @@ def rank_program(g, core, T, topo):
            ("send", len(topo.engines(core, dst))))
         op("A", None, [out], [tok], 1800 + size(out) * 8, ("arrive", sem, len(topo.engines(src, core))))
 
-    for i in range(16):
-        mm(bank(7, 0, 16), ZH(2, i), sub(G, i, 256, 16), i == 0, i == 15)
-    act(r("DW", 0, 16), bank(7, 0, 16), bias=BBH, scale=2.0)
-    lanes(0, r("DW", 0, 16))
+    columns(top(bank(7, 0, 128), 16), G, BOD, top(r("TW", 128, 256), 16))
+    mm(bank(7, 128, 144), top(r("TW", 128, 256), 16), top(sub(I1, 0, 16), 16), True, True)
+    act(r("DW"), bank(7, 128, 144), bias=BB1, scale=-2.0)
+    lanes(0)
 
     for t in range(ST):
         last = t == ST - 1
@@ -425,18 +437,18 @@ def rank_program(g, core, T, topo):
         cp(r("EU"), ind(bw, r("CRU")))
         act(r("EF"), ind(bw, r("CRU")), bias=-2048.0)
         for h in range(2):
-            mm(bank(2 * h, 0, 256), hf(G, h), bo(13, 2), True, False)
+            mm(bank(2 * h, 0, 256), hf(G, h), bo(12, 2), True, False)
             for s in range(2):
                 mm(bank(2 * h, 128 * s, 128 * s + 128), hf(r("QC"), h), BO1, False, False)
             mm(bank(2 * h, 128, 256), r("ON"), r("WA"), False, False)
-            mm(bank(2 * h + 1, 0, 256), hf(r("QC"), h), bo(0, 2), True, False)
-            mm(bank(2 * h + 1, 128, 256), hf(G, h), WB1, False, False)
-        qy = lambda h: bank(7 - 2 * h, 0, 128)
-        for c, (a, b, e) in enumerate(CHUNKS):
-            ring = 4 + 2 * (c % 2)
+            mm(bank(2 * h + 1, 0, 384), hf(r("QC"), h), bo(0, 3), True, False)
+            mm(bank(2 * h + 1, 128, 384), hf(G, h), bo(9, 2), False, False)
+            mm(bank(2 * h + 1, 256, 384), hf(r("EF"), h), PRV, False, False)
+        for a, b, e in CHUNKS:
+            ring = 4 + a // 512 % 4
             for i in range(a // 512, b // 512):
                 pp = (64 * (i % 4 // 2), 64 * (i % 4 // 2) + 64, 1)
-                mm(bank(ring + i - a // 512), r("QCT", 128 * (i // 4), 128 * (i // 4) + 128, 1, pp), r("REP", 512 * (i % 2), 512 * (i % 2) + 512, 1, pp), True, True)
+                mm(bank(4 + i % 4), r("QCT", 128 * (i // 4), 128 * (i // 4) + 128, 1, pp), r("REP", 512 * (i % 2), 512 * (i % 2) + 512, 1, pp), True, True)
             src = ind(XW, r("EU", a // 16, b // 16))
             if e == "S":
                 act(r("XG", a, b), src, bias=-127.5)
@@ -446,16 +458,11 @@ def rank_program(g, core, T, topo):
             if b % 2048 == 0:
                 h = b // 2048 - 1
                 for k in range(16):
-                    mm(bank(2 * h + 1, 15 - k, 256, 16), r("XG", 2048 * h + k, 2048 * h + 2048, 16), r("W3", 8, 24), False, k == 15)
+                    mm(bank(2 * h + 1, 15 - k, 384, 16), r("XG", 2048 * h + k, 2048 * h + 2048, 16), r("W3", 8, 32), False, k == 15)
                 for k in range(16):
                     mm(bank(2 * h, 15 - k, 256, 16), r("H", 2048 * h + k, 2048 * h + 2048, 16), r("W3", 0, 16), False, k == 15)
-        for h in range(2):
-            mm(qy(h), hf(r("QC"), h), BOU, True, False)
-            mm(qy(h), hf(G, h), WB2, False, False)
-            mm(qy(h), hf(r("EF"), h), PRV, False, False)
-            for k in range(16):
-                mm(sub(qy(h), 15 - k, 128, 16), r("XG", 2048 * h + k, 2048 * h + 2048, 16), r("W3", 24, 32), False, False)
-        append(t, r("OC"), r("OLD"), r("VO"))
+        masked(t, bank(6, 0, 256), BOE, r("VO"))
+        rivals(0, 4, ME, BOE, r("NG", 0, 16), BB, r("OC"), False)
         for h in range(2):
             qa = lambda s: bank(2 * h, 128 * s, 128 * s + 128)
             qb = lambda s: bank(2 * h + 1, 128 * s, 128 * s + 128)
@@ -464,13 +471,16 @@ def rank_program(g, core, T, topo):
             tt(x("N"), x("R0"), qb(0), A.max)
             tt(x("NC"), x("N"), qa(1), A.is_gt)
             tt(qa(2), x("NC"), qb(1), A.mult)
-            mm(qy(h), r("IF"), x("N"), False, True)
+            act(x("NU"), x("N"), scale=2.0 ** -12)
             tt(qa(3), x("N"), qa(2), A.add)
             scan(x("SC1"), r("RSB"), qa(3), A.max, A.min)
             tt(x("NE"), x("SC1"), qa(3), A.not_equal)
-            tt(x("HY"), qy(h), x("NE"), A.subtract)
+            tt(qb(3), x("NU"), qb(2), A.add)
+            tt(x("HY"), qb(3), x("NE"), A.subtract)
             scan(x("SC2"), x("NE"), x("HY"), A.mult, A.max)
-        mm(bank(4), I1, r("CIN"), True, False)
+        both = bank(4, 256, 768)
+        for h in range(2):
+            mm(sub(both, 256 * h, 256 * h + 256), hf(r("DT"), h), r("IDUP"), True, False)
         mm(bank(7), r("ON"), r("CZ"), True, False)
         mm(bank(7, 0, 512, 2), IQ, r("QC"), False, False)
         mm(bank(7, 1, 512, 2), IH, r("QC"), False, False)
@@ -482,69 +492,72 @@ def rank_program(g, core, T, topo):
         ts(bt(2), r("YI"), 13, A.arith_shift_right, 7, A.bitwise_and)
         ts(bt(3), r("YI"), 4095, A.bitwise_and)
         tt(lt(QKE), bt(0), bt(1), A.add)
-        tt(lt(QKC), bt(0), r("C10"), A.add)
         tt(lt(QD), bt(0), r("CL", 16, 32), A.not_equal)
+        act(lt(QKC), bt(0))
         act(lt(QA), bt(2))
         act(lt(QA2), bt(2), ACT.Square)
-        act(lt(QE), bt(3), bias=-2048.0)
-        tt(r("T5", 0, 16), r("CL", 0, 16), bt(3), A.subtract)
-        tt(r("T5", 16, 32), r("T5", 0, 16), lt(QM), A.mult)
-        tt(lt(QP), r("T5", 16, 32), lt(QE), A.add)
+        ts(lt(QE), bt(3), -2048.0, A.add)
+        tt(lt(QP), r("CL", 0, 16), lt(QM), A.mult)
+        tt(lt(QP2), lt(QE), lt(QM), A.mult)
         for h in range(2):
-            mm(bank(5, 128 * h, 128 * h + 128), hf(r("LT"), h), I1, True, True)
+            mm(bank(6, 128 * h, 128 * h + 128), hf(r("LT"), h), I1, True, True)
         for h in range(2):
-            mm(bank(4, 256 * h, 256 * h + 256), hf(r("LT"), h), r("IDUP"), False, h == 1)
-        act(G, bank(5, 0, 256))
-        op("V", lambda q: q.transpose(ap(r("WT")), ap(bank(4))), [r("WT")], [bank(4)], 1)
+            mm(sub(both, 256 * h, 256 * h + 256), hf(r("LT"), h), r("IDUP"), False, True)
+        act(G, bank(6, 0, 256))
+        op("V", lambda q, both=both: q.transpose(ap(r("WT")), ap(both)), [r("WT")], [both], 1)
         wq = lambda a, b: ind(r("WT"), r("SELQ", a, b))
         cp(r("UW", 0, 32), wq(QKE, QKE + 2))
-        mm(bank(6, 0, 256), WM, G, True, True)
-        act(r("MSK"), bank(6, 0, 256), ACT.Relu, bias=RHO, scale=-1.0)
+        mm(bank(6, 256, 512), WM, G, True, True)
+        act(r("MSK"), bank(6, 256, 512), ACT.Relu, bias=RHO, scale=-1.0)
         act(r("UW", 32, 64), wq(QE, QE + 2))
-        act(r("DW", 16, 32), wq(QD, QD + 1), bias=BB1, scale=0.5)
-        act(r("NG", 32, 48), wq(QP, QP + 1), bias=XBH, scale=-0.5)
-        tt(ME, ind(r("KA"), r("UW", 0, 16)), r("MSK"), A.mult)
+        tt(ME, ind(r("KV"), r("UW", 0, 16)), r("MSK"), A.mult)
         tt(MC, ind(r("KI"), r("UW", 16, 32)), r("MSK"), A.mult)
+        hold(len(ops) - 1)
+        append(t, r("OC"), r("OLD"), r("VO"))
         dst = T.cores[(rank + 1 + t % (n - 1)) % n]
         src = T.cores[(rank - 1 - t % (n - 1)) % n]
         sa, sv = (16 * t, 16 * t + 16), (256 * t, 256 * t + 256)
-        for i in range(16):
-            mm(bank(5, 256, 272), ZH(1, i), sub(ME, i, 256, 16), i == 0, i == 15)
-        tt(r("NG", 16, 32), r("DW", 16, 32), bank(5, 256, 272), A.subtract)
-        masked(t, bank(4, 256, 512), BOO, r("SV", *sv))
+        columns(top(bank(6, 0, 128), 16), ME, BOO, top(r("TW", 128, 256), 16))
+        mm(bank(6, 128, 144), top(r("TW", 128, 256), 16), top(sub(I1, 0, 16), 16), True, True)
+        act(r("NG", 16, 32), bank(6, 128, 144), bias=BB, scale=-1.0)
+        masked(t, bank(5, 256, 512), BOO, r("SV", *sv))
         remote(r("LV", *sv), r("SV", *sv), "arv%d" % t, dst, src)
-        rivals(1, 0, bank(6, 256, 384, 1, (0, 16, 1)), [(G, BODN), (ME, BOO)], r("NG", 16, 32), BB, r("SND", *sa))
+        rivals(1, 0, ME, BOO, r("NG", 16, 32), BB, r("SND", *sa), True)
         remote(r("LND", *sa), r("SND", *sa), "arr%d" % t, dst, src)
-        rivals(2, 2, bank(4, 0, 128, 1, (0, 16, 1)), [(G, BOP)], r("NG", 32, 48), XB, r("OX"))
+        columns(top(bank(3, 128, 256), 16), G, BOP, top(r("TW", 256, 384), 16))
+        mm(bank(3, 256, 272), top(r("TW", 256, 384), 16), top(sub(I1, 0, 16), 16), True, True)
+        act(r("NG", 32, 48), bank(3, 256, 272), bias=XC, scale=-1.0)
+        rivals(2, 2, G, BOP, r("NG", 32, 48), XB, r("OX"), False)
         act(r("YT"), ind(XW, r("UW", 32, 48)))
         mm(bank(7, 0, 512, 2), I1, r("YT"), False, False)
         mm(bank(7, 1, 512, 2), IH, r("YT"), False, True)
-        act(r("ZR"), bank(7))
+        lin(r("ZR"), bank(7))
         act(r("VA"), ind(r("ZR"), r("UW", 48, 64)), ACT.Abs)
         for b in range(4):
             cp(ind(XW, r("OX", 4 * b, 4 * b + 4)), r("VA", 64 * b, 64 * b + 64))
         for h in range(2):
-            mm(bank(5, 272, 273), hf(r("LT"), h), r("ON", 0, 1), h == 0, h == 1)
-        act(r("YM", t, t + 1), bank(5, 272, 273))
+            mm(bank(7, 0, 1), hf(r("LT"), h), r("ON", 0, 1), h == 0, h == 1)
+        act(r("YM", t, t + 1), bank(7, 0, 1))
         if not last:
-            act(r("PA", 0, 1), bank(5, 272, 273))
+            act(r("PA", 0, 1), bank(7, 0, 1))
             ts(r("PA", 1, 2), r("PA", 0, 1), 1, A.bitwise_and)
             act(r("PF", 0, 1), r("PA", 1, 2))
             act(r("WA"), WAC, scale=r("PF", 0, 1))
-            act(r("DW", 0, 16), wq(QD, QD + 1), bias=BBH, scale=-1.0)
-            lanes(t + 1, r("DW", 0, 16))
+            act(r("DW"), wq(QD, QD + 1), bias=BB1, scale=-2.0)
+            lanes(t + 1)
         else:
             for b in range(8):
                 act(r("XG", 512 * b, 512 * b + 512), r("XT", 512 * b, 512 * b + 512), acc=r("YS", b, b + 1))
             dma("S", T.ys[:], r("YS"), [], [r("YS")], 0)
             dma("S", T.ym[:], r("YM", 0, ST, 1, (QM, 128, 16)), [], [r("YM")], 0)
-            for j, (w, x, a, b) in enumerate(((BOE, MC, 1.0, 2048.0), (BOE, ME, 1.0, 0.0), (BOD, G, 2.0, 0.0))):
-                ps = bank((6, 6, 5)[j], (256, 0, 0)[j], (512, 256, 256)[j])
-                mm(ps, w, x, True, True)
+            for j, (terms, a, b) in enumerate((([(BOE, MC)], 1.0, 2048.0), ([(BOE, ME), (BOD, G)], 0.5, -0.5), ([(BOD, G)], 1.0, 0.0))):
+                ps = bank((4, 6, 5)[j], 0, 256)
+                for i, (w, x) in enumerate(terms):
+                    mm(ps, w, x, i == 0, i == len(terms) - 1)
                 act(r("YO", 256 * j, 256 * j + 256), ps, bias=b, scale=a)
                 act(r("YR", 256 * j, 256 * j + 256), ind(r("YO", 256 * j, 256 * j + 256), r("REV")))
                 dma("S", (T.yc, T.yv, T.yd)[j][:], r("YR", 256 * j, 256 * j + 256, 1, row0), [], [r("YR", 256 * j, 256 * j + 256)], 0)
         append(t, r("LND", *sa), r("OL2"), r("LV", *sv))
     dma("Y", T.yb[:], r("B", 0, 2048), [], [r("B", 0, 2048)], MB)
-    deps = _graph(ops)
-    _emit(g, T, ops, deps, _order(ops, deps, after))
+    deps = _graph(ops, either)
+    _emit(g, T, ops, deps, _order(ops, deps, after, either))

@@ -5,8 +5,9 @@ F32, BF, F16, I32, U16 = "float32", "bfloat16", "float16", "int32", "uint16"
 BIG = 16384.0
 SEG = (0, 256, 448, 576, 640)
 QD, QA, QKE, QKC, QE, QM, QP, QA2, QP2, Q1 = 0, 1, 2, 3, 4, 5, 6, 7, 8, 15
-CHUNKS = ((0, 512, "V"), (512, 1024, "S"), (1024, 2048, "S"), (2048, 3072, "S"), (3072, 3584, "S"), (3584, 4096, "S"))
-HOP, NEAR, TCY, BIAS = 100.0, 0.5, 0.5, 100.0
+CHUNKS = ((0, 1024, "V"), (1024, 2048, "S"), (2048, 3072, "S"), (3072, 3584, "S"), (3584, 4096, "S"))
+PIECES = ((0, 0, 128), (1, 0, 128))
+HOP, NEAR, TCY, BIAS, FLY, RAW = 170.0, 0.5, 0.42, 100.0, 1000.0, False
 
 SB = {
     "XT": (4160, BF), "B": (2112, F32), "BI": (2048, I32), "KI": (2048, I32), "KA": (2048, I32), "KV": (4096, F32), "LN": (768, I32),
@@ -16,20 +17,20 @@ SB = {
     "S8": (8, BF), "BM": (272, F32), "BNB": (272, BF), "RSB": (128, F32), "CZ": (512, BF), "ON": (128, BF), "ZE": (128, BF),
     "REV": (16, U16), "ENDS": (2, U16), "SELQ": (8, U16),
     "EU": (256, U16), "EF": (256, F16), "QC": (256, BF), "QCT": (256, F16), "XG": (4096, BF), "H": (4096, F16),
-    "R0": (256, I32), "N": (256, F32), "NU": (256, F32), "NC": (256, F32), "SC1": (256, F32), "NE": (256, F32), "HY": (256, F32), "SC2": (256, F32),
+    "R0": (256, F32), "N": (256, I32), "NU": (256, F32), "NC": (256, F32), "SC1": (256, F32), "NE": (256, F32), "HY": (256, F32), "SC2": (256, F32),
     "YI": (16, I32), "BT": (64, I32), "T5": (32, F32), "LT": (256, F16), "DT": (256, F16), "CL": (32, I32), "C10": (16, I32),
-    "G": (256, F16), "WT": (512, F32), "UW": (64, U16), "MSK": (256, BF), "MM": (512, F16), "WA": (128, BF), "PA": (8, I32), "PF": (8, F32),
+    "G": (256, F16), "WT": (512, F32), "UW": (64, U16), "MSK": (256, BF), "MM": (512 * (ST + 1), F16), "WA": (128, BF), "PA": (8, I32), "PF": (8, F32),
     "CU": (16, U16), "CRU": (16, U16), "OC": (16, U16), "OX": (16, U16),
     "TW": (384, F16), "AB": (640 * 3, BF), "SC": (640 * 3, BF), "DW": (16, F32), "NG": (48, F32), "WN": (48, F32),
     "VO": (256, F32), "OLD": (256, F32), "OL2": (256, F32), "YT": (256, BF), "ZR": (512, I32), "VA": (256, BF),
-    "SND": (16 * ST, U16), "LND": (16 * ST, U16), "SV": (256 * ST, F32), "LV": (256 * ST, F32),
+    "SR2": (16 * ST, U16), "LR2": (16 * ST, U16), "SND": (16 * ST, U16), "LND": (16 * ST, U16), "VR": (256, F32), "LV": (256 * ST, F16),
     "YS": (8, F32), "YM": (8, F32), "YO": (768, F32), "YR": (768, F32),
 }
 SCRATCH = {k: ("sbuf", [128, n], dt) for k, (n, dt) in SB.items()}
 for _b in range(4):
     SCRATCH["P%d" % _b] = ("psum", [128, 1024], F32)
 NDMA = 24
-SEMAPHORES = ["qV", "qS", "qT", "qG", "sent"] + ["arr%d" % t for t in range(ST)] + ["arv%d" % t for t in range(ST)] + ["d%d" % i for i in range(NDMA)]
+SEMAPHORES = ["qV", "qS", "qT", "qG", "sent"] + ["arr%d" % t for t in range(ST)] + ["arv%d" % t for t in range(ST)] + ["arw%d" % t for t in range(ST)] + ["d%d" % i for i in range(NDMA)]
 
 
 def r(name, a=0, b=None, s=1, p=(0, 128, 1)):
@@ -91,14 +92,14 @@ def _order(ops, deps, after, either):
         for j in deps[i]:
             users[j].append(i)
     hop = lambda j, i: 0 if ops[j][0] == ops[i][0] == "T" else HOP
-    tail = [0.0] * n
-    for i in reversed(range(n)):
-        tail[i] = ops[i][5] + max([tail[u] + hop(i, u) for u in users[i]] + [0])
     left = [len(d) for d in deps]
     then = {}
     for i, j in after:
         left[i] += 1
         then.setdefault(j, []).append(i)
+    tail = [0.0] * n
+    for i in reversed(range(n)):
+        tail[i] = ops[i][5] + max([tail[u] + hop(i, u) for u in users[i]] + [tail[u] for u in then.get(i, []) if ops[i][4] == "c"] + [0])
     ready = {i: 0.0 for i in range(n) if not left[i]}
     free, order, done = {}, [], {}
     while ready:
@@ -194,8 +195,11 @@ def rank_program(g, core, T, topo):
         rd = [y for x in ins for y in (x[1:] if x[0] == "*" else [x])] + [x[2] for x in out if x[0] == "*"]
         wr = [x[1] if x[0] == "*" else x for x in out]
         if kind == "c" and e in "VS":
-            per = 3.8 if out[0][0] == "*" else 1.56 if any(x[0] == "*" for x in ins) else per
-            per = 50 + 0.83 * max(size(out[0]) * per, 64 if e == "V" else 0)
+            listed = 3.8 if out[0][0] == "*" else 1.56 if any(x[0] == "*" for x in ins) else 0
+            if e == "S" or listed:
+                per = (65 if e == "S" else 50) + 0.83 * size(out[0]) * (listed or 1)
+            else:
+                per = 30 + 0.83 * max(size(out[0]) * per, 64)
         ops.append((e, fn, rd, wr, kind, per))
 
     def half(*xs):
@@ -244,7 +248,7 @@ def rank_program(g, core, T, topo):
             op("G", lambda q: q.iota(ap(out), pat, base, cm, allow_small_or_imprecise_dtypes=True), [out], [], 130 + 1.66 * size(out))
 
     col = lambda i: r("COL", i, i + 1)
-    PR, PG, PP, P63, RVC, EVN, ODD, RHO, XB, BB, BB1, SQ, CA, CK, E1, E2, EN, MI, PX, XC, CP = [col(i) for i in range(21)]
+    PR, PG, PP, P63, RVC, EVN, ODD, RHO, SQ, CA, CK, E1, E2, EN, MI, PX, CP, BIGC = [col(i) for i in range(18)]
     eq = lambda i: r("EQ", i, i + 1)
     bo = lambda i, k=1: r("BO", 128 * i, 128 * (i + k))
     BO1, BOH, BOU, BOE, BOO, BOD, BOP, BO8, WM, WB1, WB2, WAC, WGA, WG2 = [bo(i) for i in range(14)]
@@ -252,14 +256,14 @@ def rank_program(g, core, T, topo):
     I1, IQ, IH, PRV = [r("IV", 128 * i, 128 * i + 128) for i in range(4)]
     lt = lambda q: r("LT", q, 256, 16)
     dt = lambda q: r("DT", q, 256, 16)
-    XW, BW, G, ME, MC = r("XT"), r("B"), r("G"), r("MM", 0, 256), r("MM", 256, 512)
+    XW, BW, G, ME, MC = r("XT", 64), r("B", 64), r("G"), r("MM", 0, 256), r("MM", 256, 512)
     hf = lambda x, h: sub(x, 128 * h, 128 * h + 128)
     row0 = (0, 128, 16)
     MB = 1 << 20
 
     ms(r("LN"), 0)
     loads = [(r("LN", 256 * i, 256 * i + 256, 1, row0), x[:], r("LN", 256 * i, 256 * i + 256), 0) for i, x in ((1, T.lv), (2, T.ld), (0, T.lc))]
-    loads += [(r("BI"), T.bnd[:], r("BI"), MB), (r("XT", 0, 4096), T.x[:], r("XT", 0, 4096), 2 * MB), (r("KI", 0, 1024), T.kt[:], r("KI", 0, 1024), 2.5 * MB)]
+    loads += [(r("BI"), T.bnd[:], r("BI"), MB), (XW, T.x[:], XW, 2 * MB), (r("KI", 0, 1024), T.kt[:], r("KI", 0, 1024), 2.5 * MB)]
     loads += [(r("KI", 1024, 2048, 1, (u, 128, 2)), T.kt[1 - u::2, :], r("KI", 1024 + 512 * u, 1536 + 512 * u), 3 * MB) for u in range(2)]
     for i, (out, a, wr, nbytes) in enumerate(loads):
         dma("Y", out, a, [wr], [], nbytes)
@@ -291,10 +295,6 @@ def rank_program(g, core, T, topo):
     act(RVC, pi(1), bias=255.0, scale=-1.0)
     act(ODD, pi(4))
     act(EVN, pi(4), bias=1.0, scale=-1.0)
-    act(XB, pi(1), bias=4096.0 + 48)
-    act(BB, pi(1), bias=2048.0 + 48)
-    act(XC, pi(1), bias=2048.0 + 48)
-    act(BB1, pi(1), bias=2048.0 + 49)
     ts(r("EQ"), r("JF", 0, 16), PR, A.is_equal)
     ts(r("REV"), r("JF", 0, 16), -16.0, A.mult, RVC, A.add)
     ts(BO1, r("CG"), PG, A.is_equal)
@@ -320,8 +320,9 @@ def rank_program(g, core, T, topo):
     act(PX, PX, bias=15.0)
     ts(PRV, r("JF", 0, 128), PX, A.is_equal, 2.0 ** -25, A.mult)
     ts(r("REP"), r("REP"), P63, A.is_equal)
-    ms(r("XT", 4096, 4160), 0.0)
-    ms(r("B", 2048, 2112), 0.0)
+    ms(r("XT", 0, 64), 0.0)
+    ms(r("B", 0, 64), 0.0)
+    ms(BIGC, BIG)
     ms(r("ON"), 1.0)
     ms(r("ZE"), 0.0)
     ms(r("WA"), 0.0)
@@ -338,8 +339,9 @@ def rank_program(g, core, T, topo):
     ts(r("BNB"), r("SR"), PR, A.not_equal, -BIG, A.mult)
     ts(r("BM"), r("SR"), PR, A.is_equal, BIG, A.mult)
     ts(r("MK"), r("SJ"), PR, A.is_le, 2.0 ** 30, A.mult)
-    for mi in range(3):
-        ms(r("MK", SEG[mi] + 63 - 16 * mi, SEG[mi + 1], 64 - 16 * mi), 16.0 * (3 - mi))
+    for mi in range(4):
+        ends = r("MK", SEG[mi] + 63 - 16 * mi, SEG[mi + 1], 64 - 16 * mi)
+        ts(ends, ends, PR, A.add, 16.0 * mi, A.add)
     ts(r("REPT"), r("SM"), PP, A.is_equal, -1.0, A.mult)
     act(MI, pi(5))
     act(E1, pi(5), bias=288.0, scale=-32.0)
@@ -356,7 +358,7 @@ def rank_program(g, core, T, topo):
     tt(RHO, PR, ODD, A.subtract)
     act(RHO, RHO, ACT.Square, scale=0.5)
     act(RHO, RHO, bias=1.0, scale=-1.0)
-    act(r("B", 0, 2048), r("BI"))
+    lin(BW, r("BI"))
     for u in range(2):
         ts(r("KA", 1024 * u, 1024 * u + 1024), r("KI", 1024 * u, 1024 * u + 1024) if u == 0 else r("KI", 1024, 2048), 1023, A.bitwise_and)
         act(r("KV", 1024 * u, 1024 * u + 1024), r("KA", 1024 * u, 1024 * u + 1024), bias=1.0 - u, scale=2.0)
@@ -366,9 +368,9 @@ def rank_program(g, core, T, topo):
     def columns(tw, src, w, out):
         for i in range(16):
             mm(sub(tw, i, 128, 16), sub(src, i, size(src), 16), s8(w), True, True)
-        act(out, tw)
+        lin(out, tw)
 
-    def rivals(k, pk, src, w, neg, base, out, early):
+    def rivals(k, pk, src, w, place, out, early):
         own = top(r("TW", 128 * k, 128 * k + 128), 16)
         parts = [(0, 0, 256)] + [(SEG[mi] + b * (64 - 16 * mi), 64 * b + 16 * mi, 64 - 16 * mi) for mi in (1, 2, 3) for b in range(4)]
         for lo, hi in ((0, 512), (512, 640)):
@@ -381,27 +383,27 @@ def rank_program(g, core, T, topo):
                 mm(bank(pk, a, a + ln), w, sub(src, c, c + ln), False, not early and a == mine[-1][0])
             if early:
                 mm(bank(pk, lo, hi), own, top(r("REPT", lo, hi), 16), False, True)
-        ab, sc, wn = r("AB", 640 * k, 640 * k + 640), r("SC", 640 * k, 640 * k + 640), r("WN", 16 * k, 16 * k + 16)
+        ab, sc = r("AB", 640 * k, 640 * k + 640), r("SC", 640 * k, 640 * k + 640)
         act(ab, bank(pk, 0, 640), ACT.Abs, scale=BIG)
         scan(sc, ab, r("MK"), A.min, A.max)
-        tt(wn, ind(sc, r("ENDS", 0, 1)), neg, A.min)
-        ts(out, wn, -1.0, A.mult, base, A.add)
+        tt(out, ind(sc, r("ENDS", 0, 1)), place, A.min)
 
-    def append(t, oc, old, val):
+    def append(t, oc, old, val, raw=None):
         o = (-5 * t) % 16
-        tt(old, ind(BW, oc), r("BM", o, o + 256), A.subtract)
+        tt(old, ind(r("B"), raw or oc), r("BM", o, o + 256), A.subtract)
         for b in range(4):
-            tt(ind(BW, sub(oc, 4 * b, 4 * b + 4)), sub(old, 64 * b, 64 * b + 64), sub(val, 64 * b, 64 * b + 64), A.max)
+            tt(ind(r("B"), sub(oc, 4 * b, 4 * b + 4)), sub(old, 64 * b, 64 * b + 64), sub(val, 64 * b, 64 * b + 64), A.max)
 
-    def masked(t, ps, w, out):
+    def masked(t, ps, w, src, out):
         o = (-5 * t) % 16
         mm(ps, I1, r("BNB", o, o + 256), True, False)
-        mm(ps, w, MC, False, True)
-        act(out, ps, bias=2048.0)
+        mm(ps, w, src, False, True)
+        lin(out, ps, bias=2048.0)
 
     def lanes(t):
         tw = top(r("TW", 0, 128), 32)
-        columns(top(bank(4, 0, 128), 32), r("MM"), BOE, tw)
+        MC = r("MM", 512 * t + 256, 512 * t + 512)
+        columns(top(bank(4, 0, 128), 32), r("MM", 512 * t, 512 * t + 512), BOE, tw)
         mm(bank(4, 128, 160), tw, top(sub(I1, 0, 32), 32), True, True)
         for h in range(2):
             mm(bank(4, 160 + 8 * h, 168 + 8 * h), hf(MC, h), s8(BOE), True, True)
@@ -409,7 +411,7 @@ def rank_program(g, core, T, topo):
         act(r("CU"), bank(4, 144, 160), bias=2048.0)
         act(r("CRU"), bank(4, 128, 144))
         act(r("CL"), bank(4, 160, 192))
-        tt(r("NG", 0, 16), r("DW"), bank(4, 128, 144), A.subtract)
+        tt(r("NG", 0, 16), r("DW"), bank(4, 128, 144), A.add)
         act(dt(QKE), r("CL", 16, 32), scale=2.0)
         ts(r("C10"), r("CL", 0, 16), 1023, A.bitwise_and)
         act(dt(QKC), r("C10"))
@@ -422,13 +424,13 @@ def rank_program(g, core, T, topo):
     def remote(out, in_, sem, dst, src):
         rid, pid, _ = topo.addr(dst)
         tok = ("tok" + sem, 0, 1, 1, (0, 1, 1))
-        op("G", lambda q: q.remote_dma(ap(out), ap(in_), T.sem[sem], T.sem.sent, pid, rid, topo.mask(core, dst)), [tok, ("sends", 0, 1, 1, (0, 1, 1))], [in_], 300,
+        op("G", lambda q: q.remote_dma(ap(out), ap(in_), T.sem[sem], T.sem.sent, pid, rid, topo.mask(core, dst)), [tok], [in_], 300,
            ("send", len(topo.engines(core, dst))))
-        op("A", None, [out], [tok], 1800 + size(out) * 8, ("arrive", sem, len(topo.engines(src, core))))
+        op("A", None, [out], [tok], FLY + size(out) * 4, ("arrive", sem, len(topo.engines(src, core))))
 
     columns(top(bank(7, 0, 128), 16), G, BOD, top(r("TW", 128, 256), 16))
     mm(bank(7, 128, 144), top(r("TW", 128, 256), 16), top(sub(I1, 0, 16), 16), True, True)
-    act(r("DW"), bank(7, 128, 144), bias=BB1, scale=-2.0)
+    act(r("DW"), bank(7, 128, 144), bias=63.0, scale=2.0)
     lanes(0)
 
     for t in range(ST):
@@ -441,9 +443,9 @@ def rank_program(g, core, T, topo):
             for s in range(2):
                 mm(bank(2 * h, 128 * s, 128 * s + 128), hf(r("QC"), h), BO1, False, False)
             mm(bank(2 * h, 128, 256), r("ON"), r("WA"), False, False)
-            mm(bank(2 * h + 1, 0, 384), hf(r("QC"), h), bo(0, 3), True, False)
-            mm(bank(2 * h + 1, 128, 384), hf(G, h), bo(9, 2), False, False)
-            mm(bank(2 * h + 1, 256, 384), hf(r("EF"), h), PRV, False, False)
+            mm(bank(2 * h + 1, 0, 256), hf(r("QC"), h), bo(1, 2), True, False)
+            mm(bank(2 * h + 1, 0, 256), hf(G, h), bo(9, 2), False, False)
+            mm(bank(2 * h + 1, 128, 256), hf(r("EF"), h), PRV, False, False)
         for a, b, e in CHUNKS:
             ring = 4 + a // 512 % 4
             for i in range(a // 512, b // 512):
@@ -458,25 +460,26 @@ def rank_program(g, core, T, topo):
             if b % 2048 == 0:
                 h = b // 2048 - 1
                 for k in range(16):
-                    mm(bank(2 * h + 1, 15 - k, 384, 16), r("XG", 2048 * h + k, 2048 * h + 2048, 16), r("W3", 8, 32), False, k == 15)
+                    mm(bank(2 * h + 1, 15 - k, 256, 16), r("XG", 2048 * h + k, 2048 * h + 2048, 16), r("W3", 16, 32), False, k == 15)
                 for k in range(16):
                     mm(bank(2 * h, 15 - k, 256, 16), r("H", 2048 * h + k, 2048 * h + 2048, 16), r("W3", 0, 16), False, k == 15)
-        masked(t, bank(6, 0, 256), BOE, r("VO"))
-        rivals(0, 4, ME, BOE, r("NG", 0, 16), BB, r("OC"), False)
-        for h in range(2):
-            qa = lambda s: bank(2 * h, 128 * s, 128 * s + 128)
-            qb = lambda s: bank(2 * h + 1, 128 * s, 128 * s + 128)
-            x = lambda name: hf(r(name), h)
-            act(x("R0"), qa(0), ACT.Relu)
-            tt(x("N"), x("R0"), qb(0), A.max)
+        masked(t, bank(6, 0, 256), BOE, MC, r("VO"))
+        rivals(0, 4, ME, BOE, r("NG", 0, 16), r("OC"), False)
+        for h, a, b in PIECES:
+            qa = lambda s: bank(2 * h, 128 * s + a, 128 * s + b)
+            qb = lambda s: bank(2 * h + 1, 128 * s + a, 128 * s + b)
+            x = lambda name: r(name, 128 * h + a, 128 * h + b)
+            if a == 0:
+                act(hf(r("R0"), h), bank(2 * h + 1, 0, 128), ACT.Relu, bias=BIGC, scale=-2.0)
+            tt(x("N"), x("R0"), qa(0), A.max)
             tt(x("NC"), x("N"), qa(1), A.is_gt)
-            tt(qa(2), x("NC"), qb(1), A.mult)
+            tt(qa(2), x("NC"), qb(0), A.mult)
             act(x("NU"), x("N"), scale=2.0 ** -12)
             tt(qa(3), x("N"), qa(2), A.add)
-            scan(x("SC1"), r("RSB"), qa(3), A.max, A.min)
+            scan(x("SC1"), r("RSB", a, b), qa(3), A.max, A.min)
             tt(x("NE"), x("SC1"), qa(3), A.not_equal)
-            tt(qb(3), x("NU"), qb(2), A.add)
-            tt(x("HY"), qb(3), x("NE"), A.subtract)
+            tt(qb(2), x("NU"), qb(1), A.add)
+            tt(x("HY"), qb(2), x("NE"), A.subtract)
             scan(x("SC2"), x("NE"), x("HY"), A.mult, A.max)
         both = bank(4, 256, 768)
         for h in range(2):
@@ -510,6 +513,7 @@ def rank_program(g, core, T, topo):
         mm(bank(6, 256, 512), WM, G, True, True)
         act(r("MSK"), bank(6, 256, 512), ACT.Relu, bias=RHO, scale=-1.0)
         act(r("UW", 32, 64), wq(QE, QE + 2))
+        ME, MC = r("MM", 512 * t + 512, 512 * t + 768), r("MM", 512 * t + 768, 512 * t + 1024)
         tt(ME, ind(r("KV"), r("UW", 0, 16)), r("MSK"), A.mult)
         tt(MC, ind(r("KI"), r("UW", 16, 32)), r("MSK"), A.mult)
         hold(len(ops) - 1)
@@ -519,22 +523,25 @@ def rank_program(g, core, T, topo):
         sa, sv = (16 * t, 16 * t + 16), (256 * t, 256 * t + 256)
         columns(top(bank(6, 0, 128), 16), ME, BOO, top(r("TW", 128, 256), 16))
         mm(bank(6, 128, 144), top(r("TW", 128, 256), 16), top(sub(I1, 0, 16), 16), True, True)
-        act(r("NG", 16, 32), bank(6, 128, 144), bias=BB, scale=-1.0)
-        masked(t, bank(5, 256, 512), BOO, r("SV", *sv))
-        remote(r("LV", *sv), r("SV", *sv), "arv%d" % t, dst, src)
-        rivals(1, 0, ME, BOO, r("NG", 16, 32), BB, r("SND", *sa), True)
+        lin(r("NG", 16, 32), bank(6, 128, 144), bias=64.0)
+        if RAW:
+            lin(r("SR2", *sa), bank(6, 128, 144), bias=64.0)
+            remote(r("LR2", *sa), r("SR2", *sa), "arw%d" % t, dst, src)
+        remote(r("LV", *sv), MC, "arv%d" % t, dst, src)
+        rivals(1, 0, ME, BOO, r("NG", 16, 32), r("SND", *sa), True)
         remote(r("LND", *sa), r("SND", *sa), "arr%d" % t, dst, src)
-        columns(top(bank(3, 128, 256), 16), G, BOP, top(r("TW", 256, 384), 16))
-        mm(bank(3, 256, 272), top(r("TW", 256, 384), 16), top(sub(I1, 0, 16), 16), True, True)
-        act(r("NG", 32, 48), bank(3, 256, 272), bias=XC, scale=-1.0)
-        rivals(2, 2, G, BOP, r("NG", 32, 48), XB, r("OX"), False)
+        columns(top(bank(4, 0, 128), 16), G, BOP, top(r("TW", 256, 384), 16))
+        mm(bank(4, 128, 144), top(r("TW", 256, 384), 16), top(sub(I1, 0, 16), 16), True, True)
+        lin(r("NG", 32, 48), bank(4, 128, 144), bias=2048.0 + 64)
+        rivals(2, 2, G, BOP, r("NG", 32, 48), r("OX"), True)
         act(r("YT"), ind(XW, r("UW", 32, 48)))
         mm(bank(7, 0, 512, 2), I1, r("YT"), False, False)
         mm(bank(7, 1, 512, 2), IH, r("YT"), False, True)
         lin(r("ZR"), bank(7))
         act(r("VA"), ind(r("ZR"), r("UW", 48, 64)), ACT.Abs)
         for b in range(4):
-            cp(ind(XW, r("OX", 4 * b, 4 * b + 4)), r("VA", 64 * b, 64 * b + 64))
+            cp(ind(r("XT"), r("OX", 4 * b, 4 * b + 4)), r("VA", 64 * b, 64 * b + 64))
+        shapes_done = len(ops) - 1
         for h in range(2):
             mm(bank(7, 0, 1), hf(r("LT"), h), r("ON", 0, 1), h == 0, h == 1)
         act(r("YM", t, t + 1), bank(7, 0, 1))
@@ -543,11 +550,11 @@ def rank_program(g, core, T, topo):
             ts(r("PA", 1, 2), r("PA", 0, 1), 1, A.bitwise_and)
             act(r("PF", 0, 1), r("PA", 1, 2))
             act(r("WA"), WAC, scale=r("PF", 0, 1))
-            act(r("DW"), wq(QD, QD + 1), bias=BB1, scale=-2.0)
+            act(r("DW"), wq(QD, QD + 1), bias=63.0, scale=2.0)
             lanes(t + 1)
         else:
             for b in range(8):
-                act(r("XG", 512 * b, 512 * b + 512), r("XT", 512 * b, 512 * b + 512), acc=r("YS", b, b + 1))
+                act(r("XG", 512 * b, 512 * b + 512), sub(XW, 512 * b, 512 * b + 512), acc=r("YS", b, b + 1))
             dma("S", T.ys[:], r("YS"), [], [r("YS")], 0)
             dma("S", T.ym[:], r("YM", 0, ST, 1, (QM, 128, 16)), [], [r("YM")], 0)
             for j, (terms, a, b) in enumerate((([(BOE, MC)], 1.0, 2048.0), ([(BOE, ME), (BOD, G)], 0.5, -0.5), ([(BOD, G)], 1.0, 0.0))):
@@ -557,7 +564,9 @@ def rank_program(g, core, T, topo):
                 act(r("YO", 256 * j, 256 * j + 256), ps, bias=b, scale=a)
                 act(r("YR", 256 * j, 256 * j + 256), ind(r("YO", 256 * j, 256 * j + 256), r("REV")))
                 dma("S", (T.yc, T.yv, T.yd)[j][:], r("YR", 256 * j, 256 * j + 256, 1, row0), [], [r("YR", 256 * j, 256 * j + 256)], 0)
-        append(t, r("LND", *sa), r("OL2"), r("LV", *sv))
-    dma("Y", T.yb[:], r("B", 0, 2048), [], [r("B", 0, 2048)], MB)
+        masked(t, bank(5, 256, 512), BOO, r("LV", *sv), r("VR"))
+        after.append((len(ops) + RAW, shapes_done))
+        append(t, r("LND", *sa), r("OL2"), r("VR"), r("LR2", *sa) if RAW else None)
+    dma("Y", T.yb[:], BW, [], [BW], MB)
     deps = _graph(ops, either)
     _emit(g, T, ops, deps, _order(ops, deps, after, either))

@@ -7,30 +7,34 @@ SEG = (0, 256, 448, 576, 640)
 QD, QA, QKE, QKC, QE, QM, QP, QA2, QP2, Q1 = 0, 1, 2, 3, 4, 5, 6, 7, 8, 15
 CHUNKS = ((0, 1024, "V"), (1024, 2048, "S"), (2048, 3072, "S"), (3072, 3584, "S"), (3584, 4096, "S"))
 PIECES = ((0, 0, 128), (1, 0, 128))
-HOP, NEAR, TCY, BIAS, FLY, RAW = 170.0, 0.5, 0.42, 100.0, 1000.0, False
+OWNS, RAW, EUS, KT, UWV, YT_, ONS = True, True, False, 2, False, False, ["QC", "QCT", "VO", "VR"]
+HOP, NEAR, TCY, BIAS, FLY, DBW = 200.0, 0.5, 0.42, 100.0, 700.0, 320.0
+ORDER = ("rows scan0 off0 WT UW o0 ME MC o1 tw2 o2 SV scan2 ZR off2 scan1 o3 off1 x0 RC x1 OL2 x2 r0 x3 r1 NG0 PA r2 C10 r3 EU",
+         "G MSK UW2 twX YT NGX abs2 SR2 NG2 abs1 VA twN VR",
+         "g in mask parts2 colsX own2 backX cols2 parts1 fold back2 own1 z colsN")
 
 SB = {
-    "XT": (4160, BF), "B": (2112, F32), "BI": (2048, I32), "KI": (2048, I32), "KA": (2048, I32), "KV": (4096, F32), "LN": (768, I32),
-    "PI": (8, I32), "COL": (24, F32), "JF": (256, F32), "CG": (128, F32), "SI": (128, F32), "SR": (272, F32), "EQ": (16, F32),
+    "XT": (4160, BF), "B": (2112, F32), "BI": (2048, I32), "KI": (1024, I32), "KA": (1024, I32), "KF": (2048, F32), "SW": (128, F32), "KV": (4096, F32), "LN": (768, I32),
+    "PI": (16, I32), "COL": (28, F32), "JF": (256, F32), "CG": (128, F32), "SI": (128, F32), "SR": (272, F32), "EQ": (16, F32),
     "REP": (1024, BF), "IDUP": (256, BF), "SJ": (640, BF), "SM": (640, BF), "MK": (640, BF),
-    "REPT": (640, BF), "RH": (128, BF), "BO": (128 * 14, BF), "IV": (128 * 4, BF), "W3": (32, BF),
-    "S8": (8, BF), "BM": (272, F32), "BNB": (272, BF), "RSB": (128, F32), "CZ": (512, BF), "ON": (128, BF), "ZE": (128, BF),
+    "REPT": (640, BF), "RH": (128, BF), "BO": (128 * 14, BF), "IV": (128 * 4, BF), "E4": (128 * 4, BF), "W3": (32, BF),
+    "S8": (8, BF), "BM": (272, F32), "BNB": (272, BF), "BMN": (272, BF), "OG": (256, F16), "IF": (128, F32), "RSB": (128, F32), "CZ": (512, BF), "ON": (128, BF), "ZE": (128, BF),
     "REV": (16, U16), "ENDS": (2, U16), "SELQ": (8, U16),
     "EU": (256, U16), "EF": (256, F16), "QC": (256, BF), "QCT": (256, F16), "XG": (4096, BF), "H": (4096, F16),
     "R0": (256, F32), "N": (256, I32), "NU": (256, F32), "NC": (256, F32), "SC1": (256, F32), "NE": (256, F32), "HY": (256, F32), "SC2": (256, F32),
     "YI": (16, I32), "BT": (64, I32), "T5": (32, F32), "LT": (256, F16), "DT": (256, F16), "CL": (32, I32), "C10": (16, I32),
     "G": (256, F16), "WT": (512, F32), "UW": (64, U16), "MSK": (256, BF), "MM": (512 * (ST + 1), F16), "WA": (128, BF), "PA": (8, I32), "PF": (8, F32),
-    "CU": (16, U16), "CRU": (16, U16), "OC": (16, U16), "OX": (16, U16),
-    "TW": (384, F16), "AB": (640 * 3, BF), "SC": (640 * 3, BF), "DW": (16, F32), "NG": (48, F32), "WN": (48, F32),
+    "CU": (16, U16), "CRU": (16, U16), "OC": (16, U16), "OCR": (16, U16), "OX": (16, U16),
+    "TW": (512, F16), "AB": (640 * 3, BF), "SC": (640 * 3, BF), "DW": (16, F32), "NG": (48, F32), "WN": (48, F32),
     "VO": (256, F32), "OLD": (256, F32), "OL2": (256, F32), "YT": (256, BF), "ZR": (512, I32), "VA": (256, BF),
-    "SR2": (16 * ST, U16), "LR2": (16 * ST, U16), "SND": (16 * ST, U16), "LND": (16 * ST, U16), "VR": (256, F32), "LV": (256 * ST, F16),
+    "RC": (16, U16), "SV": (80 * ST, F16), "SND": (16 * ST, U16), "LND": (16 * ST, U16), "VR": (256, F32), "LV": (80 * ST, F16),
     "YS": (8, F32), "YM": (8, F32), "YO": (768, F32), "YR": (768, F32),
 }
 SCRATCH = {k: ("sbuf", [128, n], dt) for k, (n, dt) in SB.items()}
 for _b in range(4):
     SCRATCH["P%d" % _b] = ("psum", [128, 1024], F32)
 NDMA = 24
-SEMAPHORES = ["qV", "qS", "qT", "qG", "sent"] + ["arr%d" % t for t in range(ST)] + ["arv%d" % t for t in range(ST)] + ["arw%d" % t for t in range(ST)] + ["d%d" % i for i in range(NDMA)]
+SEMAPHORES = ["qV", "qS", "qT", "qG", "sent"] + ["arr%d" % t for t in range(ST)] + ["arv%d" % t for t in range(ST)] + ["d%d" % i for i in range(NDMA)]
 
 
 def r(name, a=0, b=None, s=1, p=(0, 128, 1)):
@@ -97,8 +101,13 @@ def _order(ops, deps, after, either):
     for i, j in after:
         left[i] += 1
         then.setdefault(j, []).append(i)
-    tail = [0.0] * n
-    for i in reversed(range(n)):
+    tail, todo, topo = [0.0] * n, list(left), [i for i in range(n) if not left[i]]
+    for i in topo:
+        for u in users[i] + then.get(i, []):
+            todo[u] -= 1
+            if not todo[u]:
+                topo.append(u)
+    for i in reversed(topo):
         tail[i] = ops[i][5] + max([tail[u] + hop(i, u) for u in users[i]] + [tail[u] for u in then.get(i, []) if ops[i][4] == "c"] + [0])
     ready = {i: 0.0 for i in range(n) if not left[i]}
     free, order, done = {}, [], {}
@@ -177,7 +186,7 @@ def rank_program(g, core, T, topo):
     if rank is None:
         return
     n = len(T.cores)
-    ops, after, either = [], [], {}
+    ops, after, either, names = [], [], {}, {}
     A = ALU
 
     def ap(x):
@@ -232,14 +241,29 @@ def rank_program(g, core, T, topo):
         act(out, a, bias=bias, scale=scale)
         either[len(ops) - 1] = v
 
-    def hold(first):
-        after.append((len(ops), first))
+    def tag(name, k=1):
+        names[name] = (len(ops) - k, len(ops) - 1)
+
+    def settle():
+        for line in ORDER:
+            turn = [names[x] for x in line.split() if x in names]
+            after.extend((b[0], a[1]) for a, b in zip(turn, turn[1:]))
+        names.clear()
+
+    def named(name, out, a, bias=0.0):
+        if name in ORDER[0].split():
+            ts(out, a, bias, A.add)
+        elif name in ORDER[1].split() + ONS:
+            act(out, a, bias=bias)
+        else:
+            lin(out, a, bias=bias)
+        tag(name)
 
     def mm(out, l, rh, st, sp):
-        op("T", lambda q: q.matmul(ap(out), ap(l), ap(rh), st, sp), [out], [l, rh], TCY * max(min(64, size(l)), size(rh)))
+        op("T", lambda q: q.matmul(ap(out), ap(l), ap(rh), st, sp), [out], [l, rh], TCY * max(min(64, size(l)), size(rh)) * (4 if SB[l[0]][1] == F32 else 1))
 
     def dma(e, out, a, wr, rd, nbytes):
-        op(e, lambda q: q.dma_start(ap(out), ap(a)), wr, rd, 2000 + nbytes / 190.0, "d")
+        op(e, lambda q: q.dma_start(ap(out), ap(a)), wr, rd, 1100 + nbytes / DBW, "d")
 
     def iota(out, pat, base=0, cm=0):
         if SB[out[0]][1] == I32:
@@ -248,7 +272,7 @@ def rank_program(g, core, T, topo):
             op("G", lambda q: q.iota(ap(out), pat, base, cm, allow_small_or_imprecise_dtypes=True), [out], [], 130 + 1.66 * size(out))
 
     col = lambda i: r("COL", i, i + 1)
-    PR, PG, PP, P63, RVC, EVN, ODD, RHO, SQ, CA, CK, E1, E2, EN, MI, PX, CP, BIGC = [col(i) for i in range(18)]
+    PR, PG, PP, P63, RVC, EVN, ODD, RHO, SQ, CA, CK, E1, E2, EN, MI, PX, CP, BIGC, SWP, P4, P5 = [col(i) for i in range(21)]
     eq = lambda i: r("EQ", i, i + 1)
     bo = lambda i, k=1: r("BO", 128 * i, 128 * (i + k))
     BO1, BOH, BOU, BOE, BOO, BOD, BOP, BO8, WM, WB1, WB2, WAC, WGA, WG2 = [bo(i) for i in range(14)]
@@ -263,8 +287,8 @@ def rank_program(g, core, T, topo):
 
     ms(r("LN"), 0)
     loads = [(r("LN", 256 * i, 256 * i + 256, 1, row0), x[:], r("LN", 256 * i, 256 * i + 256), 0) for i, x in ((1, T.lv), (2, T.ld), (0, T.lc))]
-    loads += [(r("BI"), T.bnd[:], r("BI"), MB), (XW, T.x[:], XW, 2 * MB), (r("KI", 0, 1024), T.kt[:], r("KI", 0, 1024), 2.5 * MB)]
-    loads += [(r("KI", 1024, 2048, 1, (u, 128, 2)), T.kt[1 - u::2, :], r("KI", 1024 + 512 * u, 1536 + 512 * u), 3 * MB) for u in range(2)]
+    loads = [(r("BI", 0, 512), T.bnd[:, 0:512], r("BI", 0, 512), MB / 4)] + loads
+    loads += [(r("BI", 512), T.bnd[:, 512:2048], r("BI", 512), 0.8 * MB), (XW, T.x[:], XW, 1.8 * MB), (r("KI"), T.kt[:], r("KI"), 2.3 * MB)]
     for i, (out, a, wr, nbytes) in enumerate(loads):
         dma("Y", out, a, [wr], [], nbytes)
         if i:
@@ -316,10 +340,19 @@ def rank_program(g, core, T, topo):
         act(r("W3", 8 * i, 8 * i + 8), s8(BO1), scale=w)
     act(IQ, I1, scale=-0.25)
     act(IH, I1, scale=0.5)
+    if YT_:
+        act(r("IF"), I1)
     ts(PX, pi(1), -2.0, A.mult, PP, A.add)
     act(PX, PX, bias=15.0)
     ts(PRV, r("JF", 0, 128), PX, A.is_equal, 2.0 ** -25, A.mult)
     ts(r("REP"), r("REP"), P63, A.is_equal)
+    ts(pi(8), pi(0), 2, A.arith_shift_right, 7, A.bitwise_and)
+    act(P4, pi(8))
+    ts(pi(9), pi(0), 5, A.arith_shift_right)
+    act(P5, pi(9))
+    ts(r("COL", 24, 28), r("JF", 0, 4), P5, A.is_equal, 0.25, A.mult)
+    for i in range(4):
+        ts(r("E4", 128 * i, 128 * i + 128), r("CG"), P4, A.is_equal, col(24 + i), A.mult)
     ms(r("XT", 0, 64), 0.0)
     ms(r("B", 0, 64), 0.0)
     ms(BIGC, BIG)
@@ -338,6 +371,7 @@ def rank_program(g, core, T, topo):
     ts(r("RSB"), r("SI"), 0.0, A.is_equal, 2.0 ** 20, A.mult)
     ts(r("BNB"), r("SR"), PR, A.not_equal, -BIG, A.mult)
     ts(r("BM"), r("SR"), PR, A.is_equal, BIG, A.mult)
+    ts(r("BMN"), r("SR"), PR, A.is_equal, -BIG, A.mult)
     ts(r("MK"), r("SJ"), PR, A.is_le, 2.0 ** 30, A.mult)
     for mi in range(4):
         ends = r("MK", SEG[mi] + 63 - 16 * mi, SEG[mi + 1], 64 - 16 * mi)
@@ -358,52 +392,71 @@ def rank_program(g, core, T, topo):
     tt(RHO, PR, ODD, A.subtract)
     act(RHO, RHO, ACT.Square, scale=0.5)
     act(RHO, RHO, bias=1.0, scale=-1.0)
-    lin(BW, r("BI"))
-    for u in range(2):
-        ts(r("KA", 1024 * u, 1024 * u + 1024), r("KI", 1024 * u, 1024 * u + 1024) if u == 0 else r("KI", 1024, 2048), 1023, A.bitwise_and)
-        act(r("KV", 1024 * u, 1024 * u + 1024), r("KA", 1024 * u, 1024 * u + 1024), bias=1.0 - u, scale=2.0)
-        ts(r("KV", 2048 + 1024 * u, 3072 + 1024 * u), r("KA", 1024 * u, 1024 * u + 1024), 2.0, A.mult, float(u), A.add)
-        act(r("KI", 1024 * u, 1024 * u + 1024), r("KI", 1024 * u, 1024 * u + 1024), bias=-2048.0)
+    act(r("B", 64, 576), r("BI", 0, 512))
+    act(r("B", 576), r("BI", 512))
+    for a in (0, 512):
+        ts(r("KA", a, a + 512), r("KI", a, a + 512), 1023, A.bitwise_and)
+    for name, a, b, src, bias, scale in (("KV", 0, 3072, "KA", 1.0, 2.0), ("KV", 2048, 1024, "KA", 0.0, 2.0), ("KF", 0, 1024, "KI", -2048.0, 1.0)):
+        for c in (0, 512):
+            act(r(name, a + c, a + c + 512), r(src, c, c + 512), bias=bias, scale=scale)
+        for u in range(2):
+            dma("Y", r(name, b, b + 1024, 1, (u, 128, 2)), r(name, a, a + 1024, 1, (1 - u, 128, 2)), [r(name, b + 512 * u, b + 512 * u + 512)], [r(name, a, a + 1024)], MB / 2)
 
-    def columns(tw, src, w, out):
+    def columns(tw, src, w, out, name, row=lambda i: i):
         for i in range(16):
-            mm(sub(tw, i, 128, 16), sub(src, i, size(src), 16), s8(w), True, True)
-        lin(out, tw)
+            mm(sub(tw, row(i), 128, 16), sub(src, i, size(src), 16), s8(w), True, True)
+        tag("cols" + name, 16)
+        named("tw" + name, out, tw)
 
     def rivals(k, pk, src, w, place, out, early):
         own = top(r("TW", 128 * k, 128 * k + 128), 16)
         parts = [(0, 0, 256)] + [(SEG[mi] + b * (64 - 16 * mi), 64 * b + 16 * mi, 64 - 16 * mi) for mi in (1, 2, 3) for b in range(4)]
-        for lo, hi in ((0, 512), (512, 640)):
+        two = ((0, 512), (512, 640))
+        for lo, hi in two:
             if early:
                 mm(bank(pk, lo, hi), r("ZE"), r("CZ", 0, hi - lo), True, False)
             else:
                 mm(bank(pk, lo, hi), own, top(r("REPT", lo, hi), 16), True, False)
-            mine = [x for x in parts if lo <= x[0] < hi]
-            for a, c, ln in mine:
-                mm(bank(pk, a, a + ln), w, sub(src, c, c + ln), False, not early and a == mine[-1][0])
-            if early:
+        for a, c, ln in parts:
+            mm(bank(pk, a, a + ln), w, sub(src, c, c + ln), False, not early and a + ln in (512, 640))
+        tag("parts%d" % k, len(parts))
+        if early:
+            for lo, hi in two:
                 mm(bank(pk, lo, hi), own, top(r("REPT", lo, hi), 16), False, True)
+            tag("own%d" % k, 2)
         ab, sc = r("AB", 640 * k, 640 * k + 640), r("SC", 640 * k, 640 * k + 640)
         act(ab, bank(pk, 0, 640), ACT.Abs, scale=BIG)
+        tag("abs%d" % k)
         scan(sc, ab, r("MK"), A.min, A.max)
+        tag("scan%d" % k)
         tt(out, ind(sc, r("ENDS", 0, 1)), place, A.min)
+        tag("off%d" % k)
 
-    def append(t, oc, old, val, raw=None):
+    def olds(t, oc, old, ps):
         o = (-5 * t) % 16
-        tt(old, ind(r("B"), raw or oc), r("BM", o, o + 256), A.subtract)
+        if ps:
+            act(r("OG"), ind(r("B"), oc), bias=-2048.0)
+            mm(ps, I1, r("BMN", o, o + 256), True, False)
+            mm(ps, I1, r("OG"), False, True)
+            act(old, ps, bias=2048.0)
+        else:
+            tt(old, ind(r("B"), oc), r("BM", o, o + 256), A.subtract)
+
+    def append(oc, old, val, name):
         for b in range(4):
             tt(ind(r("B"), sub(oc, 4 * b, 4 * b + 4)), sub(old, 64 * b, 64 * b + 64), sub(val, 64 * b, 64 * b + 64), A.max)
+            tag(name + str(b))
 
     def masked(t, ps, w, src, out):
         o = (-5 * t) % 16
         mm(ps, I1, r("BNB", o, o + 256), True, False)
         mm(ps, w, src, False, True)
-        lin(out, ps, bias=2048.0)
+        named(out[0], out, ps, 2048.0)
 
     def lanes(t):
         tw = top(r("TW", 0, 128), 32)
         MC = r("MM", 512 * t + 256, 512 * t + 512)
-        columns(top(bank(4, 0, 128), 32), r("MM", 512 * t, 512 * t + 512), BOE, tw)
+        columns(top(bank(4, 0, 128), 32), r("MM", 512 * t, 512 * t + 512), BOE, tw, "N")
         mm(bank(4, 128, 160), tw, top(sub(I1, 0, 32), 32), True, True)
         for h in range(2):
             mm(bank(4, 160 + 8 * h, 168 + 8 * h), hf(MC, h), s8(BOE), True, True)
@@ -412,23 +465,27 @@ def rank_program(g, core, T, topo):
         act(r("CRU"), bank(4, 128, 144))
         act(r("CL"), bank(4, 160, 192))
         tt(r("NG", 0, 16), r("DW"), bank(4, 128, 144), A.add)
+        tag("NG0")
+        if OWNS:
+            act(r("OCR"), r("NG", 0, 16))
         act(dt(QKE), r("CL", 16, 32), scale=2.0)
         ts(r("C10"), r("CL", 0, 16), 1023, A.bitwise_and)
+        tag("C10")
         act(dt(QKC), r("C10"))
-        lin(r("QC"), ind(XW, r("CU")), bias=-127.5)
+        named("QC", r("QC"), ind(XW, r("CU")), -127.5)
         for h in range(2):
             mm(bank(6, 256 + 128 * h, 384 + 128 * h), hf(r("QC"), h), I1, True, False)
             mm(bank(6, 256 + 128 * h, 384 + 128 * h), hf(G, h), BO8, False, True)
-        lin(r("QCT"), bank(6, 256, 512), bias=-1.0 / 16)
+        named("QCT" if t else "", r("QCT"), bank(6, 256, 512), -1.0 / 16)
 
     def remote(out, in_, sem, dst, src):
         rid, pid, _ = topo.addr(dst)
         tok = ("tok" + sem, 0, 1, 1, (0, 1, 1))
         op("G", lambda q: q.remote_dma(ap(out), ap(in_), T.sem[sem], T.sem.sent, pid, rid, topo.mask(core, dst)), [tok], [in_], 300,
            ("send", len(topo.engines(core, dst))))
-        op("A", None, [out], [tok], FLY + size(out) * 4, ("arrive", sem, len(topo.engines(src, core))))
+        op("A", None, [out], [tok], FLY + size(out) * 6, ("arrive", sem, len(topo.engines(src, core))))
 
-    columns(top(bank(7, 0, 128), 16), G, BOD, top(r("TW", 128, 256), 16))
+    columns(top(bank(7, 0, 128), 16), G, BOD, top(r("TW", 128, 256), 16), "")
     mm(bank(7, 128, 144), top(r("TW", 128, 256), 16), top(sub(I1, 0, 16), 16), True, True)
     act(r("DW"), bank(7, 128, 144), bias=63.0, scale=2.0)
     lanes(0)
@@ -436,19 +493,30 @@ def rank_program(g, core, T, topo):
     for t in range(ST):
         last = t == ST - 1
         bw = r("BI") if t == 0 else BW
-        cp(r("EU"), ind(bw, r("CRU")))
-        act(r("EF"), ind(bw, r("CRU")), bias=-2048.0)
+        if EUS:
+            act(r("EU"), ind(bw, r("CRU")))
+            tag("EU")
+            ts(r("EF"), r("EU"), -2048.0, A.add)
+        else:
+            cp(r("EU"), ind(bw, r("CRU")))
+            tag("EU")
+            act(r("EF"), ind(bw, r("CRU")), bias=-2048.0)
+        tag("EF")
         for h in range(2):
             mm(bank(2 * h, 0, 256), hf(G, h), bo(12, 2), True, False)
             for s in range(2):
                 mm(bank(2 * h, 128 * s, 128 * s + 128), hf(r("QC"), h), BO1, False, False)
             mm(bank(2 * h, 128, 256), r("ON"), r("WA"), False, False)
-            mm(bank(2 * h + 1, 0, 256), hf(r("QC"), h), bo(1, 2), True, False)
-            mm(bank(2 * h + 1, 0, 256), hf(G, h), bo(9, 2), False, False)
-            mm(bank(2 * h + 1, 128, 256), hf(r("EF"), h), PRV, False, False)
+            if YT_:
+                mm(bank(2 * h + 1, 0, 128), hf(r("QC"), h), BOH, True, False)
+                mm(bank(2 * h + 1, 0, 128), hf(G, h), WB1, False, False)
+            else:
+                mm(bank(2 * h + 1, 0, 256), hf(r("QC"), h), bo(1, 2), True, False)
+                mm(bank(2 * h + 1, 0, 256), hf(G, h), bo(9, 2), False, False)
+                mm(bank(2 * h + 1, 128, 256), hf(r("EF"), h), PRV, False, False)
         for a, b, e in CHUNKS:
             ring = 4 + a // 512 % 4
-            for i in range(a // 512, b // 512):
+            for i in range((a + 511) // 512, (b + 511) // 512):
                 pp = (64 * (i % 4 // 2), 64 * (i % 4 // 2) + 64, 1)
                 mm(bank(4 + i % 4), r("QCT", 128 * (i // 4), 128 * (i // 4) + 128, 1, pp), r("REP", 512 * (i % 2), 512 * (i % 2) + 512, 1, pp), True, True)
             src = ind(XW, r("EU", a // 16, b // 16))
@@ -456,14 +524,24 @@ def rank_program(g, core, T, topo):
                 act(r("XG", a, b), src, bias=-127.5)
             else:
                 ts(r("XG", a, b), src, -127.5, A.add)
-            tt(r("H", a, b), r("XG", a, b), bank(ring, 0, b - a), A.min)
+            tag("g%d" % a)
+            tt(r("H", a, b), r("XG", a, b), bank(ring, a % 512, a % 512 + b - a), A.min)
             if b % 2048 == 0:
                 h = b // 2048 - 1
                 for k in range(16):
-                    mm(bank(2 * h + 1, 15 - k, 256, 16), r("XG", 2048 * h + k, 2048 * h + 2048, 16), r("W3", 16, 32), False, k == 15)
+                    mm(bank(2 * h + 1, 15 - k, 128 if YT_ else 256, 16), r("XG", 2048 * h + k, 2048 * h + 2048, 16), r("W3", 16, 24 if YT_ else 32), False, k == 15)
+                if YT_:
+                    mm(bank(2 * h + 1, 128, 256), hf(r("QC"), h), BOU, True, False)
+                    mm(bank(2 * h + 1, 128, 256), hf(G, h), WB2, False, False)
+                    mm(bank(2 * h + 1, 128, 256), hf(r("EF"), h), PRV, False, False)
+                    for k in range(16):
+                        mm(bank(2 * h + 1, 143 - k, 256, 16), r("XG", 2048 * h + k, 2048 * h + 2048, 16), r("W3", 24, 32), False, False)
                 for k in range(16):
                     mm(bank(2 * h, 15 - k, 256, 16), r("H", 2048 * h + k, 2048 * h + 2048, 16), r("W3", 0, 16), False, k == 15)
+        settle()
         masked(t, bank(6, 0, 256), BOE, MC, r("VO"))
+        if OWNS:
+            olds(t, r("OCR"), r("OLD"), bank(6, 256, 512))
         rivals(0, 4, ME, BOE, r("NG", 0, 16), r("OC"), False)
         for h, a, b in PIECES:
             qa = lambda s: bank(2 * h, 128 * s + a, 128 * s + b)
@@ -478,8 +556,11 @@ def rank_program(g, core, T, topo):
             tt(qa(3), x("N"), qa(2), A.add)
             scan(x("SC1"), r("RSB", a, b), qa(3), A.max, A.min)
             tt(x("NE"), x("SC1"), qa(3), A.not_equal)
-            tt(qb(2), x("NU"), qb(1), A.add)
-            tt(x("HY"), qb(2), x("NE"), A.subtract)
+            if YT_:
+                mm(qb(1), r("IF"), x("NU"), False, True)
+            else:
+                tt(qb(2), x("NU"), qb(1), A.add)
+            tt(x("HY"), qb(1 if YT_ else 2), x("NE"), A.subtract)
             scan(x("SC2"), x("NE"), x("HY"), A.mult, A.max)
         both = bank(4, 256, 768)
         for h in range(2):
@@ -490,83 +571,118 @@ def rank_program(g, core, T, topo):
         bt = lambda i: r("BT", 16 * i, 16 * i + 16)
         ts(r("YI"), r("SC2", 15, 256, 16), 2.0 ** 25, A.mult)
         ts(lt(QM), r("SC1", 15, 256, 16), 5000.0, A.is_ge)
-        ts(bt(0), r("YI"), 2, A.arith_shift_right, 1024, A.bitwise_and)
-        ts(bt(1), r("YI"), 1023, A.bitwise_and)
+        tt(lt(QP), r("CL", 0, 16), lt(QM), A.mult)
+        first = len(ops)
         ts(bt(2), r("YI"), 13, A.arith_shift_right, 7, A.bitwise_and)
         ts(bt(3), r("YI"), 4095, A.bitwise_and)
-        tt(lt(QKE), bt(0), bt(1), A.add)
+        ts(bt(0), r("YI"), 2, A.arith_shift_right, 1024, A.bitwise_and)
+        ts(bt(1), r("YI"), 1023, A.bitwise_and)
+        ts(lt(QE), bt(3), -2048.0, A.add)
         tt(lt(QD), bt(0), r("CL", 16, 32), A.not_equal)
-        act(lt(QKC), bt(0))
+        tt(lt(QKE), bt(0), bt(1), A.add)
+        tt(lt(QP2), lt(QE), lt(QM), A.mult)
+        tag("rows")
+        after.extend((i + 1, i) for i in range(first, len(ops) - 1))
         act(lt(QA), bt(2))
         act(lt(QA2), bt(2), ACT.Square)
-        ts(lt(QE), bt(3), -2048.0, A.add)
-        tt(lt(QP), r("CL", 0, 16), lt(QM), A.mult)
-        tt(lt(QP2), lt(QE), lt(QM), A.mult)
+        act(lt(QKC), bt(0))
         for h in range(2):
             mm(bank(6, 128 * h, 128 * h + 128), hf(r("LT"), h), I1, True, True)
+        tag("g", 2)
         for h in range(2):
             mm(sub(both, 256 * h, 256 * h + 256), hf(r("LT"), h), r("IDUP"), False, True)
+        tag("in", 2)
         act(G, bank(6, 0, 256))
+        tag("G")
         op("V", lambda q, both=both: q.transpose(ap(r("WT")), ap(both)), [r("WT")], [both], 1)
+        tag("WT")
         wq = lambda a, b: ind(r("WT"), r("SELQ", a, b))
-        cp(r("UW", 0, 32), wq(QKE, QKE + 2))
+        cp(r("UW", 0, 64 if UWV else 32), wq(QKE, QKE + (4 if UWV else 2)))
+        tag("UW")
         mm(bank(6, 256, 512), WM, G, True, True)
+        tag("mask")
         act(r("MSK"), bank(6, 256, 512), ACT.Relu, bias=RHO, scale=-1.0)
-        act(r("UW", 32, 64), wq(QE, QE + 2))
+        tag("MSK")
+        if not UWV:
+            act(r("UW", 32, 64), wq(QE, QE + 2))
+            tag("UW2")
         ME, MC = r("MM", 512 * t + 512, 512 * t + 768), r("MM", 512 * t + 768, 512 * t + 1024)
         tt(ME, ind(r("KV"), r("UW", 0, 16)), r("MSK"), A.mult)
-        tt(MC, ind(r("KI"), r("UW", 16, 32)), r("MSK"), A.mult)
-        hold(len(ops) - 1)
-        append(t, r("OC"), r("OLD"), r("VO"))
+        tag("ME")
+        tt(MC, ind(r("KF"), r("UW", 16, 32)), r("MSK"), A.mult)
+        tag("MC")
+        if not OWNS:
+            olds(t, r("OC"), r("OLD"), None)
+            tag("OLD")
+        append(r("OC"), r("OLD"), r("VO"), "o")
         dst = T.cores[(rank + 1 + t % (n - 1)) % n]
         src = T.cores[(rank - 1 - t % (n - 1)) % n]
-        sa, sv = (16 * t, 16 * t + 16), (256 * t, 256 * t + 256)
-        columns(top(bank(6, 0, 128), 16), ME, BOO, top(r("TW", 128, 256), 16))
-        mm(bank(6, 128, 144), top(r("TW", 128, 256), 16), top(sub(I1, 0, 16), 16), True, True)
-        lin(r("NG", 16, 32), bank(6, 128, 144), bias=64.0)
-        if RAW:
-            lin(r("SR2", *sa), bank(6, 128, 144), bias=64.0)
-            remote(r("LR2", *sa), r("SR2", *sa), "arw%d" % t, dst, src)
-        remote(r("LV", *sv), MC, "arv%d" % t, dst, src)
+        sa = (16 * t, 16 * t + 16)
+        i16 = top(sub(I1, 0, 16), 16)
+        columns(top(bank(6, 0, 128), 16), ME, BOO, top(r("TW", 128, 256), 16), "2")
+        mm(bank(6, 128, 144), top(r("TW", 128, 256), 16), i16, True, True)
+        tag("back2")
+        named("NG2", r("NG", 16, 32), bank(6, 128, 144), 64.0)
+        sv, quarter = 80 * t, lambda x, i: x[:4] + ((32 * i, 32 * i + 32, 1),)
+        for i in range(4):
+            mm(quarter(bank(5, 256, 320), i), sub(BOO, 0, 128, 4), sub(MC, 64 * i, 64 * i + 64), True, True)
+        tag("fold", 4)
+        named("SV", r("SV", sv, sv + 64), bank(5, 256, 320))
+        named("SR2", r("SV", sv + 64, sv + 80), bank(6, 128, 144))
+        remote(r("LV", sv, sv + 80), r("SV", sv, sv + 80), "arv%d" % t, dst, src)
         rivals(1, 0, ME, BOO, r("NG", 16, 32), r("SND", *sa), True)
         remote(r("LND", *sa), r("SND", *sa), "arr%d" % t, dst, src)
-        columns(top(bank(4, 0, 128), 16), G, BOP, top(r("TW", 256, 384), 16))
-        mm(bank(4, 128, 144), top(r("TW", 256, 384), 16), top(sub(I1, 0, 16), 16), True, True)
-        lin(r("NG", 32, 48), bank(4, 128, 144), bias=2048.0 + 64)
+        columns(top(bank(4, 0, 128), 16), G, BOP, top(r("TW", 256, 384), 16), "X")
+        mm(bank(4, 128, 144), top(r("TW", 256, 384), 16), i16, True, True)
+        tag("backX")
+        named("NGX", r("NG", 32, 48), bank(4, 128, 144), 2048.0 + 64)
         rivals(2, 2, G, BOP, r("NG", 32, 48), r("OX"), True)
         act(r("YT"), ind(XW, r("UW", 32, 48)))
+        tag("YT")
         mm(bank(7, 0, 512, 2), I1, r("YT"), False, False)
         mm(bank(7, 1, 512, 2), IH, r("YT"), False, True)
-        lin(r("ZR"), bank(7))
+        tag("z", 2)
+        named("ZR", r("ZR"), bank(7))
         act(r("VA"), ind(r("ZR"), r("UW", 48, 64)), ACT.Abs)
+        tag("VA")
         for b in range(4):
             cp(ind(r("XT"), r("OX", 4 * b, 4 * b + 4)), r("VA", 64 * b, 64 * b + 64))
-        shapes_done = len(ops) - 1
+            tag("x%d" % b)
         for h in range(2):
             mm(bank(7, 0, 1), hf(r("LT"), h), r("ON", 0, 1), h == 0, h == 1)
         act(r("YM", t, t + 1), bank(7, 0, 1))
         if not last:
             act(r("PA", 0, 1), bank(7, 0, 1))
             ts(r("PA", 1, 2), r("PA", 0, 1), 1, A.bitwise_and)
+            tag("PA")
             act(r("PF", 0, 1), r("PA", 1, 2))
             act(r("WA"), WAC, scale=r("PF", 0, 1))
             act(r("DW"), wq(QD, QD + 1), bias=63.0, scale=2.0)
             lanes(t + 1)
         else:
+            for i in range(64):
+                mm(bank(3, 0, 64), I1, sub(XW, i, 4096, 64), i == 0, i == 63)
             for b in range(8):
-                act(r("XG", 512 * b, 512 * b + 512), sub(XW, 512 * b, 512 * b + 512), acc=r("YS", b, b + 1))
+                act(r("NU", 8 * b, 8 * b + 8), bank(3, 8 * b, 8 * b + 8), acc=r("YS", b, b + 1))
             dma("S", T.ys[:], r("YS"), [], [r("YS")], 0)
-            dma("S", T.ym[:], r("YM", 0, ST, 1, (QM, 128, 16)), [], [r("YM")], 0)
+            dma("Y", T.ym[:], r("YM", 0, ST, 1, (QM, 128, 16)), [], [r("YM")], 0)
             for j, (terms, a, b) in enumerate((([(BOE, MC)], 1.0, 2048.0), ([(BOE, ME), (BOD, G)], 0.5, -0.5), ([(BOD, G)], 1.0, 0.0))):
                 ps = bank((4, 6, 5)[j], 0, 256)
                 for i, (w, x) in enumerate(terms):
                     mm(ps, w, x, i == 0, i == len(terms) - 1)
                 act(r("YO", 256 * j, 256 * j + 256), ps, bias=b, scale=a)
                 act(r("YR", 256 * j, 256 * j + 256), ind(r("YO", 256 * j, 256 * j + 256), r("REV")))
-                dma("S", (T.yc, T.yv, T.yd)[j][:], r("YR", 256 * j, 256 * j + 256, 1, row0), [], [r("YR", 256 * j, 256 * j + 256)], 0)
-        masked(t, bank(5, 256, 512), BOO, r("LV", *sv), r("VR"))
-        after.append((len(ops) + RAW, shapes_done))
-        append(t, r("LND", *sa), r("OL2"), r("VR"), r("LR2", *sa) if RAW else None)
+                dma("Y", (T.yc, T.yv, T.yd)[j][:], r("YR", 256 * j, 256 * j + 256, 1, row0), [], [r("YR", 256 * j, 256 * j + 256)], 0)
+        o = (-5 * t) % 16
+        mm(bank(1, 0, 256), I1, r("BNB", o, o + 256), True, False)
+        for i in range(4):
+            mm(bank(1, 64 * i, 64 * i + 64), r("E4", 128 * i, 128 * i + 128), r("LV", sv, sv + 64), False, i == 3)
+        named("VR", r("VR"), bank(1, 0, 256), 2048.0)
+        named("RC", r("RC"), r("LV", sv + 64, sv + 80), 64.0)
+        olds(t, r("RC"), r("OL2"), None)
+        tag("OL2")
+        append(r("LND", *sa), r("OL2"), r("VR"), "r")
+    settle()
     dma("Y", T.yb[:], BW, [], [BW], MB)
     deps = _graph(ops, either)
     _emit(g, T, ops, deps, _order(ops, deps, after, either))

from concourse.mybir import AluOpType as ALU, ActivationFunctionType as ACT

ST = 6
F32, BF, F16, I32, U16 = "float32", "bfloat16", "float16", "int32", "uint16"
BIG = 16384.0
SEG = (0, 256, 448, 576, 640)
QD, QA, QKE, QKC, QE, QM, QP, QA2, QP2, Q1 = 0, 1, 2, 3, 4, 5, 6, 7, 8, 15
CHUNKS = ((0, 1024, "V"), (1024, 2048, "S"), (2048, 3072, "S"), (3072, 3584, "S"), (3584, 4096, "S"))
PIECES = ((0, 0, 128), (1, 0, 128))
OWNS, RAW, EUS, KT, UWV, YT_, ONS = True, True, False, 2, False, False, ["QC", "QCT", "VO", "VR"]
HOP, NEAR, TCY, BIAS, FLY, DBW = 200.0, 0.5, 0.42, 100.0, 700.0, 320.0
ORDER = ("rows scan0 off0 WT UW o0 ME MC o1 tw2 o2 SV scan2 ZR off2 scan1 o3 off1 x0 RC x1 OL2 x2 r0 x3 r1 NG0 PA r2 C10 r3 EU",
         "G MSK UW2 twX YT NGX abs2 SR2 NG2 abs1 VA twN VR",
         "g in mask parts2 colsX own2 backX cols2 parts1 fold back2 own1 z colsN")

SB = {
    "XT": (4160, BF), "B": (2112, F32), "BI": (2048, I32), "KI": (1024, I32), "KA": (1024, I32), "KF": (2048, F32), "SW": (128, F32), "KV": (4096, F32), "LN": (768, I32),
    "PI": (16, I32), "COL": (28, F32), "JF": (256, F32), "CG": (128, F32), "SI": (128, F32), "SR": (272, F32), "EQ": (16, F32),
    "REP": (1024, BF), "IDUP": (256, BF), "SJ": (640, BF), "SM": (640, BF), "MK": (640, BF),
    "REPT": (640, BF), "RH": (128, BF), "BO": (128 * 14, BF), "IV": (128 * 4, BF), "E4": (128 * 4, BF), "W3": (32, BF),
    "S8": (8, BF), "BM": (272, F32), "BNB": (272, BF), "BMN": (272, BF), "OG": (256, F16), "IF": (128, F32), "RSB": (128, F32), "CZ": (512, BF), "ON": (128, BF), "ZE": (128, BF),
    "REV": (16, U16), "ENDS": (2, U16), "SELQ": (8, U16),
    "EU": (256, U16), "EF": (256, F16), "QC": (256, BF), "QCT": (256, F16), "XG": (4096, BF), "H": (4096, F16),
    "R0": (256, F32), "N": (256, I32), "NU": (256, F32), "NC": (256, F32), "SC1": (256, F32), "NE": (256, F32), "HY": (256, F32), "SC2": (256, F32),
    "YI": (16, I32), "BT": (64, I32), "T5": (32, F32), "LT": (256, F16), "DT": (256, F16), "CL": (32, I32), "C10": (16, I32),
    "G": (256, F16), "WT": (512, F32), "UW": (64, U16), "MSK": (256, BF), "MM": (512 * (ST + 1), F16), "WA": (128, BF), "PA": (8, I32), "PF": (8, F32),
    "CU": (16, U16), "CRU": (16, U16), "OC": (16, U16), "OCR": (16, U16), "OX": (16, U16),
    "TW": (512, F16), "AB": (640 * 3, BF), "SC": (640 * 3, BF), "DW": (16, F32), "NG": (48, F32), "WN": (48, F32),
    "VO": (256, F32), "OLD": (256, F32), "OL2": (256, F32), "YT": (256, BF), "ZR": (512, I32), "VA": (256, BF),
    "RC": (16, U16), "SV": (80 * ST, F16), "SND": (16 * ST, U16), "LND": (16 * ST, U16), "VR": (256, F32), "LV": (80 * ST, F16),
    "YS": (8, F32), "YM": (8, F32), "YO": (768, F32), "YR": (768, F32),
}
SCRATCH = {k: ("sbuf", [128, n], dt) for k, (n, dt) in SB.items()}
for _b in range(4):
    SCRATCH["P%d" % _b] = ("psum", [128, 1024], F32)
NDMA = 24
SEMAPHORES = ["qV", "qS", "qT", "qG", "sent"] + ["arr%d" % t for t in range(ST)] + ["arv%d" % t for t in range(ST)] + ["d%d" % i for i in range(NDMA)]


def r(name, a=0, b=None, s=1, p=(0, 128, 1)):
    return (name, a, SB[name][0] if b is None else b, s, p)


def bank(k, a=0, b=512, s=1, p=(0, 128, 1)):
    return ("P%d" % (k // 2), 512 * (k % 2) + a, 512 * (k % 2) + b, s, p)


def sub(x, a, b, s=1):
    return (x[0], x[1] + a * x[3], x[1] + (b - 1) * x[3] + 1, x[3] * s, x[4])


def top(x, n):
    return x[:4] + ((0, n, 1),)


def size(x):
    return 16 * size(x[2]) if x[0] == "*" else len(range(x[1], x[2], x[3]))


def _meet(x, y):
    if x[2] <= y[1] or y[2] <= x[1] or x[4][1] <= y[4][0] or y[4][1] <= x[4][0]:
        return False
    return not (x[3] == y[3] > 1 and (x[1] - y[1]) % x[3])


def _banks(x):
    return [(x[0], k) for k in range(x[1] // 512, (x[2] - 1) // 512 + 1)] if x[0] in SCRATCH and x[0] not in SB else []


def _graph(ops, either):
    seen, last, deps = {}, {}, []
    for i, (e, fn, rd, wr, kind, cost) in enumerate(ops):
        d = set()
        e = i if i in either else e
        for x, w in [(x, False) for x in rd] + [(x, True) for x in wr]:
            d.update(j for j, y, v in seen.get(x[0], []) if (w or v) and _meet(x, y))
        for k in set(b for x in rd + wr for b in _banks(x)):
            old = last.get(k, (e, [], []))
            if old[0] != e:
                old = (e, [], old[1])
            d.update(old[2] + (old[1][-1:] if e == "T" else []))
            last[k] = (e, old[1] + [i], old[2])
        for x in wr:
            seen[x[0]] = [z for z in seen.get(x[0], []) if not (x[3] == 1 and x[4] == (0, 128, 1) and x[1] <= z[1][1] and z[1][2] <= x[2]) and z[1] != x]
        for x, w in [(x, False) for x in rd] + [(x, True) for x in wr]:
            seen.setdefault(x[0], []).append((i, x, w))
        d.discard(i)
        deps.append(sorted(d))
    return deps


def _order(ops, deps, after, either):
    n = len(ops)
    users = [[] for _ in ops]
    for i in range(n):
        for j in deps[i]:
            users[j].append(i)
    hop = lambda j, i: 0 if ops[j][0] == ops[i][0] == "T" else HOP
    left = [len(d) for d in deps]
    then = {}
    for i, j in after:
        left[i] += 1
        then.setdefault(j, []).append(i)
    tail, todo, topo = [0.0] * n, list(left), [i for i in range(n) if not left[i]]
    for i in topo:
        for u in users[i] + then.get(i, []):
            todo[u] -= 1
            if not todo[u]:
                topo.append(u)
    for i in reversed(topo):
        tail[i] = ops[i][5] + max([tail[u] + hop(i, u) for u in users[i]] + [tail[u] for u in then.get(i, []) if ops[i][4] == "c"] + [0])
    ready = {i: 0.0 for i in range(n) if not left[i]}
    free, order, done = {}, [], {}
    while ready:
        for i in ready:
            if i in either and max(ready[i], free.get(either[i][0], 0.0)) + either[i][5] + (BIAS if either[i][0] == "V" else -BIAS) < max(ready[i], free.get(ops[i][0], 0.0)) + ops[i][5]:
                ops[i], either[i] = either[i], ops[i]
        start = {i: max(t, free.get(ops[i][0], 0.0)) for i, t in ready.items()}
        i = min(start, key=lambda j: (start[j], -tail[j]))
        near = [j for j in start if ops[j][0] == ops[i][0] and start[j] <= start[i] + NEAR * ops[i][5]]
        i = max(near, key=lambda j: (tail[j], -j))
        end = start[i] + ops[i][5]
        free[ops[i][0]] = end if ops[i][4] == "c" or ops[i][4][0] == "send" else start[i] + 60
        order.append(i)
        del ready[i]
        for u, at in [(u, end + hop(i, u)) for u in users[i]] + [(u, start[i]) for u in then.get(i, [])]:
            left[u] -= 1
            done[u] = max(done.get(u, 0.0), at)
            if not left[u]:
                ready[u] = done[u]
    return order


def _emit(g, T, ops, deps, order):
    q = {"V": g.vector, "S": g.scalar, "T": g.tensor, "G": g, "Y": g.sync}
    pos = {j: i for i, j in enumerate(order)}

    def stream(j):
        return ops[j][0] if ops[j][4] == "c" else ("op", j)

    known, clock, waits, need = {}, {}, {}, set()
    for i in order:
        e, kind = ops[i][0], ops[i][4]
        kn = known.setdefault(e, {})
        waits[i] = []
        if kind[0] != "arrive":
            for j in sorted(deps[i], key=lambda j: -pos[j]):
                if kn.get(stream(j), -1) < pos[j] and ops[j][4][0] != "send" and not (e == "T" == ops[j][0]):
                    waits[i].append(j)
                    need.add(j)
                    kn[stream(j)] = pos[j]
                    for s, v in clock[j].items():
                        if kn.get(s, -1) < v:
                            kn[s] = v
        clock[i] = dict(kn) if kind[0] != "arrive" else {}
    mark, cnt, nd, total = {}, {}, [0], {}
    for i in order:
        e, fn, kind = ops[i][0], ops[i][1], ops[i][4]
        for j in waits[i]:
            q[e].wait_ge(T.sem[mark[j][0]], mark[j][1])
        if kind == "c":
            ins = fn(q[e])
            if i in need:
                cnt[e] = cnt.get(e, 0) + 1
                ins.then_inc(T.sem["q" + e], 1)
                mark[i] = ("q" + e, cnt[e])
                total["q" + e] = cnt[e]
        elif kind == "d":
            s = "d%d" % nd[0]
            nd[0] += 1
            fn(q[e]).then_inc(T.sem[s], 16)
            mark[i] = (s, 16)
            total[s] = 16
        elif kind[0] == "send":
            fn(q[e])
            total["sent"] = total.get("sent", 0) + kind[1]
        else:
            mark[i] = (kind[1], kind[2])
            total[kind[1]] = kind[2]
    for s in sorted(total):
        g.wait_ge(T.sem[s], total[s])


def rank_program(g, core, T, topo):
    rank = T.rank_of(core)
    if rank is None:
        return
    n = len(T.cores)
    ops, after, either, names = [], [], {}, {}
    A = ALU

    def ap(x):
        if not isinstance(x, tuple):
            return x
        if x[0] == "*":
            return ap(x[1]).indirect(ap(x[2]))
        return T[x[0]][x[4][0]:x[4][1]:x[4][2], x[1]:x[2]:x[3]]

    def ind(win, off):
        return ("*", win, off)

    def op(e, fn, out, ins, per, kind="c"):
        ins = [x for x in ins if isinstance(x, tuple)]
        rd = [y for x in ins for y in (x[1:] if x[0] == "*" else [x])] + [x[2] for x in out if x[0] == "*"]
        wr = [x[1] if x[0] == "*" else x for x in out]
        if kind == "c" and e in "VS":
            listed = 3.8 if out[0][0] == "*" else 1.56 if any(x[0] == "*" for x in ins) else 0
            if e == "S" or listed:
                per = (65 if e == "S" else 50) + 0.83 * size(out[0]) * (listed or 1)
            else:
                per = 30 + 0.83 * max(size(out[0]) * per, 64)
        ops.append((e, fn, rd, wr, kind, per))

    def half(*xs):
        return 0.5 if all(x[0] in SB and SB[x[0]][1] in (BF, F16, U16) for x in xs) else 1

    def tt(out, a, b, o):
        op("V", lambda q: q.tensor_tensor(ap(out), ap(a), ap(b), o), [out], [a, b], 1 if _banks(a) + _banks(b) else 2)

    def ts(out, a, s1, o0, s2=None, o1=None):
        if o1 is None:
            op("V", lambda q: q.tensor_scalar(ap(out), ap(a), ap(s1), None, o0), [out], [a, s1], half(out, a))
        else:
            op("V", lambda q: q.tensor_scalar(ap(out), ap(a), ap(s1), ap(s2), o0, o1), [out], [a, s1, s2], half(out, a))

    def cp(out, a):
        op("V", lambda q: q.tensor_copy(ap(out), ap(a)), [out], [a], half(out, a))

    def scan(out, d0, d1, o0, o1):
        op("V", lambda q: q.tensor_tensor_scan(ap(out), ap(d0), ap(d1), 0.0, o0, o1), [out], [d0, d1], half(out, d0, d1))

    def ms(out, c):
        op("V", lambda q: q.memset(ap(out), c), [out], [], half(out))

    def act(out, a, f=ACT.Identity, bias=0.0, scale=1.0, acc=None):
        op("S", lambda q: q.activation(ap(out), ap(a), f, bias=ap(bias), scale=ap(scale), accum_out=ap(acc)), [out] + ([acc] if acc else []), [a, bias, scale], 1)

    def lin(out, a, bias=0.0, scale=1.0):
        ts(out, a, scale, A.mult, bias, A.add)
        v = ops.pop()
        act(out, a, bias=bias, scale=scale)
        either[len(ops) - 1] = v

    def tag(name, k=1):
        names[name] = (len(ops) - k, len(ops) - 1)

    def settle():
        for line in ORDER:
            turn = [names[x] for x in line.split() if x in names]
            after.extend((b[0], a[1]) for a, b in zip(turn, turn[1:]))
        names.clear()

    def named(name, out, a, bias=0.0):
        if name in ORDER[0].split():
            ts(out, a, bias, A.add)
        elif name in ORDER[1].split() + ONS:
            act(out, a, bias=bias)
        else:
            lin(out, a, bias=bias)
        tag(name)

    def mm(out, l, rh, st, sp):
        op("T", lambda q: q.matmul(ap(out), ap(l), ap(rh), st, sp), [out], [l, rh], TCY * max(min(64, size(l)), size(rh)) * (4 if SB[l[0]][1] == F32 else 1))

    def dma(e, out, a, wr, rd, nbytes):
        op(e, lambda q: q.dma_start(ap(out), ap(a)), wr, rd, 1100 + nbytes / DBW, "d")

    def iota(out, pat, base=0, cm=0):
        if SB[out[0]][1] == I32:
            op("G", lambda q: q.iota(ap(out), pat, base, cm), [out], [], 130 + 1.66 * size(out))
        else:
            op("G", lambda q: q.iota(ap(out), pat, base, cm, allow_small_or_imprecise_dtypes=True), [out], [], 130 + 1.66 * size(out))

    col = lambda i: r("COL", i, i + 1)
    PR, PG, PP, P63, RVC, EVN, ODD, RHO, SQ, CA, CK, E1, E2, EN, MI, PX, CP, BIGC, SWP, P4, P5 = [col(i) for i in range(21)]
    eq = lambda i: r("EQ", i, i + 1)
    bo = lambda i, k=1: r("BO", 128 * i, 128 * (i + k))
    BO1, BOH, BOU, BOE, BOO, BOD, BOP, BO8, WM, WB1, WB2, WAC, WGA, WG2 = [bo(i) for i in range(14)]
    s8 = lambda x: sub(x, 0, 128, 16)
    I1, IQ, IH, PRV = [r("IV", 128 * i, 128 * i + 128) for i in range(4)]
    lt = lambda q: r("LT", q, 256, 16)
    dt = lambda q: r("DT", q, 256, 16)
    XW, BW, G, ME, MC = r("XT", 64), r("B", 64), r("G"), r("MM", 0, 256), r("MM", 256, 512)
    hf = lambda x, h: sub(x, 128 * h, 128 * h + 128)
    row0 = (0, 128, 16)
    MB = 1 << 20

    ms(r("LN"), 0)
    loads = [(r("LN", 256 * i, 256 * i + 256, 1, row0), x[:], r("LN", 256 * i, 256 * i + 256), 0) for i, x in ((1, T.lv), (2, T.ld), (0, T.lc))]
    loads = [(r("BI", 0, 512), T.bnd[:, 0:512], r("BI", 0, 512), MB / 4)] + loads
    loads += [(r("BI", 512), T.bnd[:, 512:2048], r("BI", 512), 0.8 * MB), (XW, T.x[:], XW, 1.8 * MB), (r("KI"), T.kt[:], r("KI"), 2.3 * MB)]
    for i, (out, a, wr, nbytes) in enumerate(loads):
        dma("Y", out, a, [wr], [], nbytes)
        if i:
            after.append((len(ops) - 1, len(ops) - 2))

    iota(r("PI", 0, 1), [[0, 1]], 0, 1)
    iota(r("JF"), [[1, 256]])
    iota(r("CG"), [[1, 8], [0, 16]])
    iota(r("REP"), [[1, 64], [0, 16]])
    iota(r("SI"), [[0, 8], [1, 16]])
    iota(r("SR"), [[0, 17], [-1, 16]], 15)
    for mi in range(4):
        iota(r("SJ", SEG[mi], SEG[mi + 1]), [[0, 4], [1, 64 - 16 * mi]])
        iota(r("SM", SEG[mi], SEG[mi + 1]), [[4, 4], [0, 64 - 16 * mi]], mi)
    iota(r("IDUP"), [[16, 8], [0, 2], [1, 16]])
    iota(r("RH"), [[0, 8], [-2, 8], [0, 2]])
    pi = lambda i: r("PI", i, i + 1)
    ts(pi(1), pi(0), 15, A.bitwise_and)
    ts(pi(2), pi(0), 4, A.arith_shift_right)
    ts(pi(3), pi(0), 63, A.bitwise_and)
    ts(pi(4), pi(0), 1, A.bitwise_and)
    ts(pi(5), pi(0), 3, A.bitwise_and)
    ts(pi(6), pi(0), 2, A.arith_shift_right, 3, A.bitwise_and)
    ts(pi(7), pi(0), 16, A.bitwise_and)
    act(r("COL", 0, 2), r("PI", 1, 3))
    act(PP, pi(0))
    act(P63, pi(3))
    act(RVC, pi(1), bias=255.0, scale=-1.0)
    act(ODD, pi(4))
    act(EVN, pi(4), bias=1.0, scale=-1.0)
    ts(r("EQ"), r("JF", 0, 16), PR, A.is_equal)
    ts(r("REV"), r("JF", 0, 16), -16.0, A.mult, RVC, A.add)
    ts(BO1, r("CG"), PG, A.is_equal)
    ts(I1, r("JF", 0, 128), PP, A.is_equal)
    ts(CK, eq(0), -2048.0, A.mult)
    ts(G, ind(r("LN", 512, 768), r("REV")), eq(Q1), A.add)
    ts(r("OLD"), ind(r("LN", 256, 512), r("REV")), 2.0, A.mult, eq(0), A.add)
    tt(ME, r("OLD"), G, A.subtract)
    ts(MC, ind(r("LN", 0, 256), r("REV")), CK, A.add)
    ts(CP, eq(QE), eq(QP), A.add, eq(QP2), A.subtract)
    for x, c, w in ((BOH, -0.5, None), (BOU, -2.0 ** -13, None), (BOE, EVN, None), (BOO, ODD, None), (BOD, eq(QD), None),
                    (BOP, CP, None), (BO8, eq(QD), 0.125), (WB1, eq(Q1), 8192.0), (WB2, eq(Q1), 2.0 ** -14), (WAC, eq(QM), -1.0 / 16)):
        ts(x, BO1, c, A.mult, w, w and A.mult)
    ts(CA, eq(Q1), -17.0 / 32, A.mult, eq(QD), A.add)
    ts(WGA, BO1, CA, A.mult)
    ts(WG2, BO1, CA, A.mult)
    act(r("S8"), s8(BOD), scale=1024.0)
    for i, w in enumerate((-1.0, -1.0, 0.5, 2.0 ** -13)):
        act(r("W3", 8 * i, 8 * i + 8), s8(BO1), scale=w)
    act(IQ, I1, scale=-0.25)
    act(IH, I1, scale=0.5)
    if YT_:
        act(r("IF"), I1)
    ts(PX, pi(1), -2.0, A.mult, PP, A.add)
    act(PX, PX, bias=15.0)
    ts(PRV, r("JF", 0, 128), PX, A.is_equal, 2.0 ** -25, A.mult)
    ts(r("REP"), r("REP"), P63, A.is_equal)
    ts(pi(8), pi(0), 2, A.arith_shift_right, 7, A.bitwise_and)
    act(P4, pi(8))
    ts(pi(9), pi(0), 5, A.arith_shift_right)
    act(P5, pi(9))
    ts(r("COL", 24, 28), r("JF", 0, 4), P5, A.is_equal, 0.25, A.mult)
    for i in range(4):
        ts(r("E4", 128 * i, 128 * i + 128), r("CG"), P4, A.is_equal, col(24 + i), A.mult)
    ms(r("XT", 0, 64), 0.0)
    ms(r("B", 0, 64), 0.0)
    ms(BIGC, BIG)
    ms(r("ON"), 1.0)
    ms(r("ZE"), 0.0)
    ms(r("WA"), 0.0)
    act(r("LT"), r("JF"), scale=0.0)
    act(lt(Q1), r("ON", 0, 16))
    act(r("DT"), r("JF"), scale=0.0)
    act(dt(QE), r("ON", 0, 16), scale=2048.0)
    for h in range(2):
        ts(sub(dt(QM), 8 * h, 8 * h + 8), r("ON", 0, 8), PP, A.mult, 2.0, A.mult)
    ts(sub(dt(QM), 8, 16), sub(dt(QM), 8, 16), 256.0, A.add)
    ms(r("CZ", 0, 512, 2), -31.5 / 128)
    ms(r("CZ", 1, 512, 2), 63.5 / 128)
    ts(r("RSB"), r("SI"), 0.0, A.is_equal, 2.0 ** 20, A.mult)
    ts(r("BNB"), r("SR"), PR, A.not_equal, -BIG, A.mult)
    ts(r("BM"), r("SR"), PR, A.is_equal, BIG, A.mult)
    ts(r("BMN"), r("SR"), PR, A.is_equal, -BIG, A.mult)
    ts(r("MK"), r("SJ"), PR, A.is_le, 2.0 ** 30, A.mult)
    for mi in range(4):
        ends = r("MK", SEG[mi] + 63 - 16 * mi, SEG[mi + 1], 64 - 16 * mi)
        ts(ends, ends, PR, A.add, 16.0 * mi, A.add)
    ts(r("REPT"), r("SM"), PP, A.is_equal, -1.0, A.mult)
    act(MI, pi(5))
    act(E1, pi(5), bias=288.0, scale=-32.0)
    act(E2, pi(5), bias=64.0, scale=-16.0)
    ts(EN, pi(6), 1.0, A.add, E2, A.mult)
    act(EN, EN, bias=-1.0)
    ts(r("ENDS", 0, 1), E1, MI, A.mult, EN, A.add)
    ts(SQ, pi(1), 32.0, A.mult)
    tt(SQ, SQ, pi(7), A.add)
    ts(r("SELQ"), r("JF", 0, 8), SQ, A.add)
    ts(r("IDUP"), r("IDUP"), PP, A.is_equal)
    ts(r("RH"), r("RH"), eq(QA), A.mult, eq(QA2), A.add)
    tt(WM, r("RH"), BO1, A.mult)
    tt(RHO, PR, ODD, A.subtract)
    act(RHO, RHO, ACT.Square, scale=0.5)
    act(RHO, RHO, bias=1.0, scale=-1.0)
    act(r("B", 64, 576), r("BI", 0, 512))
    act(r("B", 576), r("BI", 512))
    for a in (0, 512):
        ts(r("KA", a, a + 512), r("KI", a, a + 512), 1023, A.bitwise_and)
    for name, a, b, src, bias, scale in (("KV", 0, 3072, "KA", 1.0, 2.0), ("KV", 2048, 1024, "KA", 0.0, 2.0), ("KF", 0, 1024, "KI", -2048.0, 1.0)):
        for c in (0, 512):
            act(r(name, a + c, a + c + 512), r(src, c, c + 512), bias=bias, scale=scale)
        for u in range(2):
            dma("Y", r(name, b, b + 1024, 1, (u, 128, 2)), r(name, a, a + 1024, 1, (1 - u, 128, 2)), [r(name, b + 512 * u, b + 512 * u + 512)], [r(name, a, a + 1024)], MB / 2)

    def columns(tw, src, w, out, name, row=lambda i: i):
        for i in range(16):
            mm(sub(tw, row(i), 128, 16), sub(src, i, size(src), 16), s8(w), True, True)
        tag("cols" + name, 16)
        named("tw" + name, out, tw)

    def rivals(k, pk, src, w, place, out, early):
        own = top(r("TW", 128 * k, 128 * k + 128), 16)
        parts = [(0, 0, 256)] + [(SEG[mi] + b * (64 - 16 * mi), 64 * b + 16 * mi, 64 - 16 * mi) for mi in (1, 2, 3) for b in range(4)]
        two = ((0, 512), (512, 640))
        for lo, hi in two:
            if early:
                mm(bank(pk, lo, hi), r("ZE"), r("CZ", 0, hi - lo), True, False)
            else:
                mm(bank(pk, lo, hi), own, top(r("REPT", lo, hi), 16), True, False)
        for a, c, ln in parts:
            mm(bank(pk, a, a + ln), w, sub(src, c, c + ln), False, not early and a + ln in (512, 640))
        tag("parts%d" % k, len(parts))
        if early:
            for lo, hi in two:
                mm(bank(pk, lo, hi), own, top(r("REPT", lo, hi), 16), False, True)
            tag("own%d" % k, 2)
        ab, sc = r("AB", 640 * k, 640 * k + 640), r("SC", 640 * k, 640 * k + 640)
        act(ab, bank(pk, 0, 640), ACT.Abs, scale=BIG)
        tag("abs%d" % k)
        scan(sc, ab, r("MK"), A.min, A.max)
        tag("scan%d" % k)
        tt(out, ind(sc, r("ENDS", 0, 1)), place, A.min)
        tag("off%d" % k)

    def olds(t, oc, old, ps):
        o = (-5 * t) % 16
        if ps:
            act(r("OG"), ind(r("B"), oc), bias=-2048.0)
            mm(ps, I1, r("BMN", o, o + 256), True, False)
            mm(ps, I1, r("OG"), False, True)
            act(old, ps, bias=2048.0)
        else:
            tt(old, ind(r("B"), oc), r("BM", o, o + 256), A.subtract)

    def append(oc, old, val, name):
        for b in range(4):
            tt(ind(r("B"), sub(oc, 4 * b, 4 * b + 4)), sub(old, 64 * b, 64 * b + 64), sub(val, 64 * b, 64 * b + 64), A.max)
            tag(name + str(b))

    def masked(t, ps, w, src, out):
        o = (-5 * t) % 16
        mm(ps, I1, r("BNB", o, o + 256), True, False)
        mm(ps, w, src, False, True)
        named(out[0], out, ps, 2048.0)

    def lanes(t):
        tw = top(r("TW", 0, 128), 32)
        MC = r("MM", 512 * t + 256, 512 * t + 512)
        columns(top(bank(4, 0, 128), 32), r("MM", 512 * t, 512 * t + 512), BOE, tw, "N")
        mm(bank(4, 128, 160), tw, top(sub(I1, 0, 32), 32), True, True)
        for h in range(2):
            mm(bank(4, 160 + 8 * h, 168 + 8 * h), hf(MC, h), s8(BOE), True, True)
            mm(bank(4, 176 + 8 * h, 184 + 8 * h), hf(G, h), r("S8"), True, True)
        act(r("CU"), bank(4, 144, 160), bias=2048.0)
        act(r("CRU"), bank(4, 128, 144))
        act(r("CL"), bank(4, 160, 192))
        tt(r("NG", 0, 16), r("DW"), bank(4, 128, 144), A.add)
        tag("NG0")
        if OWNS:
            act(r("OCR"), r("NG", 0, 16))
        act(dt(QKE), r("CL", 16, 32), scale=2.0)
        ts(r("C10"), r("CL", 0, 16), 1023, A.bitwise_and)
        tag("C10")
        act(dt(QKC), r("C10"))
        named("QC", r("QC"), ind(XW, r("CU")), -127.5)
        for h in range(2):
            mm(bank(6, 256 + 128 * h, 384 + 128 * h), hf(r("QC"), h), I1, True, False)
            mm(bank(6, 256 + 128 * h, 384 + 128 * h), hf(G, h), BO8, False, True)
        named("QCT" if t else "", r("QCT"), bank(6, 256, 512), -1.0 / 16)

    def remote(out, in_, sem, dst, src):
        rid, pid, _ = topo.addr(dst)
        tok = ("tok" + sem, 0, 1, 1, (0, 1, 1))
        op("G", lambda q: q.remote_dma(ap(out), ap(in_), T.sem[sem], T.sem.sent, pid, rid, topo.mask(core, dst)), [tok], [in_], 300,
           ("send", len(topo.engines(core, dst))))
        op("A", None, [out], [tok], FLY + size(out) * 6, ("arrive", sem, len(topo.engines(src, core))))

    columns(top(bank(7, 0, 128), 16), G, BOD, top(r("TW", 128, 256), 16), "")
    mm(bank(7, 128, 144), top(r("TW", 128, 256), 16), top(sub(I1, 0, 16), 16), True, True)
    act(r("DW"), bank(7, 128, 144), bias=63.0, scale=2.0)
    lanes(0)

    for t in range(ST):
        last = t == ST - 1
        bw = r("BI") if t == 0 else BW
        if EUS:
            act(r("EU"), ind(bw, r("CRU")))
            tag("EU")
            ts(r("EF"), r("EU"), -2048.0, A.add)
        else:
            cp(r("EU"), ind(bw, r("CRU")))
            tag("EU")
            act(r("EF"), ind(bw, r("CRU")), bias=-2048.0)
        tag("EF")
        for h in range(2):
            mm(bank(2 * h, 0, 256), hf(G, h), bo(12, 2), True, False)
            for s in range(2):
                mm(bank(2 * h, 128 * s, 128 * s + 128), hf(r("QC"), h), BO1, False, False)
            mm(bank(2 * h, 128, 256), r("ON"), r("WA"), False, False)
            if YT_:
                mm(bank(2 * h + 1, 0, 128), hf(r("QC"), h), BOH, True, False)
                mm(bank(2 * h + 1, 0, 128), hf(G, h), WB1, False, False)
            else:
                mm(bank(2 * h + 1, 0, 256), hf(r("QC"), h), bo(1, 2), True, False)
                mm(bank(2 * h + 1, 0, 256), hf(G, h), bo(9, 2), False, False)
                mm(bank(2 * h + 1, 128, 256), hf(r("EF"), h), PRV, False, False)
        for a, b, e in CHUNKS:
            ring = 4 + a // 512 % 4
            for i in range((a + 511) // 512, (b + 511) // 512):
                pp = (64 * (i % 4 // 2), 64 * (i % 4 // 2) + 64, 1)
                mm(bank(4 + i % 4), r("QCT", 128 * (i // 4), 128 * (i // 4) + 128, 1, pp), r("REP", 512 * (i % 2), 512 * (i % 2) + 512, 1, pp), True, True)
            src = ind(XW, r("EU", a // 16, b // 16))
            if e == "S":
                act(r("XG", a, b), src, bias=-127.5)
            else:
                ts(r("XG", a, b), src, -127.5, A.add)
            tag("g%d" % a)
            tt(r("H", a, b), r("XG", a, b), bank(ring, a % 512, a % 512 + b - a), A.min)
            if b % 2048 == 0:
                h = b // 2048 - 1
                for k in range(16):
                    mm(bank(2 * h + 1, 15 - k, 128 if YT_ else 256, 16), r("XG", 2048 * h + k, 2048 * h + 2048, 16), r("W3", 16, 24 if YT_ else 32), False, k == 15)
                if YT_:
                    mm(bank(2 * h + 1, 128, 256), hf(r("QC"), h), BOU, True, False)
                    mm(bank(2 * h + 1, 128, 256), hf(G, h), WB2, False, False)
                    mm(bank(2 * h + 1, 128, 256), hf(r("EF"), h), PRV, False, False)
                    for k in range(16):
                        mm(bank(2 * h + 1, 143 - k, 256, 16), r("XG", 2048 * h + k, 2048 * h + 2048, 16), r("W3", 24, 32), False, False)
                for k in range(16):
                    mm(bank(2 * h, 15 - k, 256, 16), r("H", 2048 * h + k, 2048 * h + 2048, 16), r("W3", 0, 16), False, k == 15)
        settle()
        masked(t, bank(6, 0, 256), BOE, MC, r("VO"))
        if OWNS:
            olds(t, r("OCR"), r("OLD"), bank(6, 256, 512))
        rivals(0, 4, ME, BOE, r("NG", 0, 16), r("OC"), False)
        for h, a, b in PIECES:
            qa = lambda s: bank(2 * h, 128 * s + a, 128 * s + b)
            qb = lambda s: bank(2 * h + 1, 128 * s + a, 128 * s + b)
            x = lambda name: r(name, 128 * h + a, 128 * h + b)
            if a == 0:
                act(hf(r("R0"), h), bank(2 * h + 1, 0, 128), ACT.Relu, bias=BIGC, scale=-2.0)
            tt(x("N"), x("R0"), qa(0), A.max)
            tt(x("NC"), x("N"), qa(1), A.is_gt)
            tt(qa(2), x("NC"), qb(0), A.mult)
            act(x("NU"), x("N"), scale=2.0 ** -12)
            tt(qa(3), x("N"), qa(2), A.add)
            scan(x("SC1"), r("RSB", a, b), qa(3), A.max, A.min)
            tt(x("NE"), x("SC1"), qa(3), A.not_equal)
            if YT_:
                mm(qb(1), r("IF"), x("NU"), False, True)
            else:
                tt(qb(2), x("NU"), qb(1), A.add)
            tt(x("HY"), qb(1 if YT_ else 2), x("NE"), A.subtract)
            scan(x("SC2"), x("NE"), x("HY"), A.mult, A.max)
        both = bank(4, 256, 768)
        for h in range(2):
            mm(sub(both, 256 * h, 256 * h + 256), hf(r("DT"), h), r("IDUP"), True, False)
        mm(bank(7), r("ON"), r("CZ"), True, False)
        mm(bank(7, 0, 512, 2), IQ, r("QC"), False, False)
        mm(bank(7, 1, 512, 2), IH, r("QC"), False, False)
        bt = lambda i: r("BT", 16 * i, 16 * i + 16)
        ts(r("YI"), r("SC2", 15, 256, 16), 2.0 ** 25, A.mult)
        ts(lt(QM), r("SC1", 15, 256, 16), 5000.0, A.is_ge)
        tt(lt(QP), r("CL", 0, 16), lt(QM), A.mult)
        first = len(ops)
        ts(bt(2), r("YI"), 13, A.arith_shift_right, 7, A.bitwise_and)
        ts(bt(3), r("YI"), 4095, A.bitwise_and)
        ts(bt(0), r("YI"), 2, A.arith_shift_right, 1024, A.bitwise_and)
        ts(bt(1), r("YI"), 1023, A.bitwise_and)
        ts(lt(QE), bt(3), -2048.0, A.add)
        tt(lt(QD), bt(0), r("CL", 16, 32), A.not_equal)
        tt(lt(QKE), bt(0), bt(1), A.add)
        tt(lt(QP2), lt(QE), lt(QM), A.mult)
        tag("rows")
        after.extend((i + 1, i) for i in range(first, len(ops) - 1))
        act(lt(QA), bt(2))
        act(lt(QA2), bt(2), ACT.Square)
        act(lt(QKC), bt(0))
        for h in range(2):
            mm(bank(6, 128 * h, 128 * h + 128), hf(r("LT"), h), I1, True, True)
        tag("g", 2)
        for h in range(2):
            mm(sub(both, 256 * h, 256 * h + 256), hf(r("LT"), h), r("IDUP"), False, True)
        tag("in", 2)
        act(G, bank(6, 0, 256))
        tag("G")
        op("V", lambda q, both=both: q.transpose(ap(r("WT")), ap(both)), [r("WT")], [both], 1)
        tag("WT")
        wq = lambda a, b: ind(r("WT"), r("SELQ", a, b))
        cp(r("UW", 0, 64 if UWV else 32), wq(QKE, QKE + (4 if UWV else 2)))
        tag("UW")
        mm(bank(6, 256, 512), WM, G, True, True)
        tag("mask")
        act(r("MSK"), bank(6, 256, 512), ACT.Relu, bias=RHO, scale=-1.0)
        tag("MSK")
        if not UWV:
            act(r("UW", 32, 64), wq(QE, QE + 2))
            tag("UW2")
        ME, MC = r("MM", 512 * t + 512, 512 * t + 768), r("MM", 512 * t + 768, 512 * t + 1024)
        tt(ME, ind(r("KV"), r("UW", 0, 16)), r("MSK"), A.mult)
        tag("ME")
        tt(MC, ind(r("KF"), r("UW", 16, 32)), r("MSK"), A.mult)
        tag("MC")
        if not OWNS:
            olds(t, r("OC"), r("OLD"), None)
            tag("OLD")
        append(r("OC"), r("OLD"), r("VO"), "o")
        dst = T.cores[(rank + 1 + t % (n - 1)) % n]
        src = T.cores[(rank - 1 - t % (n - 1)) % n]
        sa = (16 * t, 16 * t + 16)
        i16 = top(sub(I1, 0, 16), 16)
        columns(top(bank(6, 0, 128), 16), ME, BOO, top(r("TW", 128, 256), 16), "2")
        mm(bank(6, 128, 144), top(r("TW", 128, 256), 16), i16, True, True)
        tag("back2")
        named("NG2", r("NG", 16, 32), bank(6, 128, 144), 64.0)
        sv, quarter = 80 * t, lambda x, i: x[:4] + ((32 * i, 32 * i + 32, 1),)
        for i in range(4):
            mm(quarter(bank(5, 256, 320), i), sub(BOO, 0, 128, 4), sub(MC, 64 * i, 64 * i + 64), True, True)
        tag("fold", 4)
        named("SV", r("SV", sv, sv + 64), bank(5, 256, 320))
        named("SR2", r("SV", sv + 64, sv + 80), bank(6, 128, 144))
        remote(r("LV", sv, sv + 80), r("SV", sv, sv + 80), "arv%d" % t, dst, src)
        rivals(1, 0, ME, BOO, r("NG", 16, 32), r("SND", *sa), True)
        remote(r("LND", *sa), r("SND", *sa), "arr%d" % t, dst, src)
        columns(top(bank(4, 0, 128), 16), G, BOP, top(r("TW", 256, 384), 16), "X")
        mm(bank(4, 128, 144), top(r("TW", 256, 384), 16), i16, True, True)
        tag("backX")
        named("NGX", r("NG", 32, 48), bank(4, 128, 144), 2048.0 + 64)
        rivals(2, 2, G, BOP, r("NG", 32, 48), r("OX"), True)
        act(r("YT"), ind(XW, r("UW", 32, 48)))
        tag("YT")
        mm(bank(7, 0, 512, 2), I1, r("YT"), False, False)
        mm(bank(7, 1, 512, 2), IH, r("YT"), False, True)
        tag("z", 2)
        named("ZR", r("ZR"), bank(7))
        act(r("VA"), ind(r("ZR"), r("UW", 48, 64)), ACT.Abs)
        tag("VA")
        for b in range(4):
            cp(ind(r("XT"), r("OX", 4 * b, 4 * b + 4)), r("VA", 64 * b, 64 * b + 64))
            tag("x%d" % b)
        for h in range(2):
            mm(bank(7, 0, 1), hf(r("LT"), h), r("ON", 0, 1), h == 0, h == 1)
        act(r("YM", t, t + 1), bank(7, 0, 1))
        if not last:
            act(r("PA", 0, 1), bank(7, 0, 1))
            ts(r("PA", 1, 2), r("PA", 0, 1), 1, A.bitwise_and)
            tag("PA")
            act(r("PF", 0, 1), r("PA", 1, 2))
            act(r("WA"), WAC, scale=r("PF", 0, 1))
            act(r("DW"), wq(QD, QD + 1), bias=63.0, scale=2.0)
            lanes(t + 1)
        else:
            for i in range(64):
                mm(bank(3, 0, 64), I1, sub(XW, i, 4096, 64), i == 0, i == 63)
            for b in range(8):
                act(r("NU", 8 * b, 8 * b + 8), bank(3, 8 * b, 8 * b + 8), acc=r("YS", b, b + 1))
            dma("S", T.ys[:], r("YS"), [], [r("YS")], 0)
            dma("Y", T.ym[:], r("YM", 0, ST, 1, (QM, 128, 16)), [], [r("YM")], 0)
            for j, (terms, a, b) in enumerate((([(BOE, MC)], 1.0, 2048.0), ([(BOE, ME), (BOD, G)], 0.5, -0.5), ([(BOD, G)], 1.0, 0.0))):
                ps = bank((4, 6, 5)[j], 0, 256)
                for i, (w, x) in enumerate(terms):
                    mm(ps, w, x, i == 0, i == len(terms) - 1)
                act(r("YO", 256 * j, 256 * j + 256), ps, bias=b, scale=a)
                act(r("YR", 256 * j, 256 * j + 256), ind(r("YO", 256 * j, 256 * j + 256), r("REV")))
                dma("Y", (T.yc, T.yv, T.yd)[j][:], r("YR", 256 * j, 256 * j + 256, 1, row0), [], [r("YR", 256 * j, 256 * j + 256)], 0)
        o = (-5 * t) % 16
        mm(bank(1, 0, 256), I1, r("BNB", o, o + 256), True, False)
        for i in range(4):
            mm(bank(1, 64 * i, 64 * i + 64), r("E4", 128 * i, 128 * i + 128), r("LV", sv, sv + 64), False, i == 3)
        named("VR", r("VR"), bank(1, 0, 256), 2048.0)
        named("RC", r("RC"), r("LV", sv + 64, sv + 80), 64.0)
        olds(t, r("RC"), r("OL2"), None)
        tag("OL2")
        append(r("LND", *sa), r("OL2"), r("VR"), "r")
    settle()
    dma("Y", T.yb[:], BW, [], [BW], MB)
    deps = _graph(ops, either)
    _emit(g, T, ops, deps, _order(ops, deps, after, either))
